import numpy as np
import ml_dtypes


def mxq(x, axis, fmt="e4m3"):
    dtype, down = {"e4m3": (ml_dtypes.float8_e4m3fn, 7), "e5m2": (ml_dtypes.float8_e5m2, 14)}[fmt]
    v = np.moveaxis(np.asarray(x, np.float32).astype(ml_dtypes.bfloat16).astype(np.float64), axis, -1)
    blocks = v.reshape(v.shape[:-1] + (-1, 32))
    amax = np.abs(blocks).max(-1, keepdims=True)
    byte = np.maximum(np.where(amax > 0, np.frexp(amax)[1] - 1 + 127, 0) - down, 1)
    scale = np.exp2(byte - 127.0)
    codes = (blocks / scale).astype(np.float32).astype(dtype).astype(np.float64)
    return np.moveaxis((codes * scale).reshape(v.shape), -1, axis)


WIDE = False


def mx_kscale(k):
    if not WIDE:
        return np.ones(k)
    levels = np.array([18, -18])
    if k % 512:
        return np.exp2(np.random.permutation(np.resize(levels, k // 32))).repeat(32)
    a = np.empty((k // 512, 16))
    for p in range(k // 512):
        a[p, :8] = np.random.permutation(np.resize(levels, 8))
        for g in range(8):
            far = levels[np.abs(levels - a[p, g]) >= 10]
            a[p, g + 8] = far[np.random.randint(len(far))]
    return np.exp2(a.ravel()).repeat(32)


def f64(x):
    return np.asarray(x).astype(np.float64)


def striped(idx):
    return np.tile(np.asarray(idx).reshape(-1, 16).T, (8, 1)).astype(np.uint16)


def unstriped(offs):
    return offs[:16].T.reshape(-1).astype(np.int64)


E2M1 = np.array([0.0, 0.5, 1.0, 1.5, 2.0, 3.0, 4.0, 6.0, -0.0, -0.5, -1.0, -1.5, -2.0, -3.0, -4.0, -6.0])


def pack_weight(w, fmt):
    k, n = w.shape
    w = f64(np.asarray(w, np.float32).astype(ml_dtypes.bfloat16)).reshape(k // 32, 32, n)
    amax = np.abs(w).max(1)
    if fmt == "e4m3":
        byte = np.frexp(amax)[1] - 1 + 127 - 7
    else:
        mant, ex = np.frexp(amax / 6.0)
        byte = np.where(mant > 0.5, ex, ex - 1) + 127
    byte = np.clip(np.where(amax > 0, byte, 1), 1, 254)
    scaled = (w * np.exp2(127.0 - byte)[:, None, :]).reshape(k, n).astype(np.float32)
    by_word = np.ascontiguousarray(scaled.reshape(k // 512, 128, 4, n).transpose(0, 1, 3, 2))
    if fmt == "e4m3":
        words = by_word.astype(ml_dtypes.float8_e4m3fn).view(np.uint8)
    else:
        c = by_word.astype(ml_dtypes.float4_e2m1fn).view(np.uint8) & 0xF
        words = (c[..., 0::2] | (c[..., 1::2] << 4)).reshape(k // 512, 128, 2 * n)
    return np.ascontiguousarray(words), np.ascontiguousarray(byte.astype(np.uint8).reshape(k // 512, 16, n))


def unpack_weight(words, scales, fmt):
    g, _, n = scales.shape
    words = np.ascontiguousarray(words).reshape(g, 128, n, -1)
    if fmt == "e4m3":
        vals = words.view(ml_dtypes.float8_e4m3fn).astype(np.float64)
    else:
        nib = np.empty((g, 128, n, 4), np.uint8)
        nib[..., 0::2] = words & 0xF
        nib[..., 1::2] = words >> 4
        vals = E2M1[nib]
    vals = vals * np.repeat(np.exp2(scales.astype(np.float64) - 127.0), 8, axis=1)[..., None]
    return vals.transpose(0, 1, 3, 2).reshape(g * 512, n)


def planes(y):
    n, m = y.shape
    v = y.astype(np.float32).astype(ml_dtypes.bfloat16).astype(np.float64).reshape(n // 32, 32, m)
    top = np.abs(v).max(1)
    byte = np.clip(np.where(top > 0, np.frexp(top)[1] - 1 + 127 - 7, 1), 1, 254)
    codes = (v * np.exp2(127.0 - byte)[:, None, :]).reshape(n, m).astype(np.float32).astype(ml_dtypes.float8_e4m3fn).view(np.uint8)
    words = codes.reshape(n // 512, 128, 4, m).transpose(0, 1, 3, 2)
    return np.ascontiguousarray(words), np.ascontiguousarray(byte.astype(np.uint8).reshape(n // 512, 16, m))


N, T, D, V = 512, 1024, 512, 1024


def setup_inputs():
    n = np.random.standard_normal
    idx = np.random.permutation(T)[:N]
    s = mx_kscale(D)[:, None]
    z = mx_kscale(V)[:, None]
    w = n((D, V)) / np.sqrt(D)
    wd, wv = pack_weight(w * s, "e4m3"), pack_weight(w.T / z, "e4m3")
    return {
        "xT": (n((D, T)) / s).astype(np.float32),
        "wd_words": wd[0],
        "wd_scales": wd[1],
        "wv_words": wv[0],
        "wv_scales": wv[1],
        "y": n((V, N)).astype(np.float32),
        "cw": (np.random.uniform(0.5, 1.5, (V, 1)) / np.sqrt(V) * z).astype(np.float32),
        "rw": np.tile(np.random.uniform(0.5, 1.5, N), (128, 1)).astype(np.float32),
        "offs": striped(idx),
    }


def reference(xT, wd_words, wd_scales, wv_words, wv_scales, y, cw, rw, offs):
    idx = unstriped(offs)
    a = unpack_weight(wd_words, wd_scales, "e4m3").T @ mxq(f64(xT)[:, idx], 0, "e4m3")
    g = f64(cw) * f64(rw)[:1] * (a - f64(y))
    dx = unpack_weight(wv_words, wv_scales, "e4m3").T @ mxq(g, 0, "e5m2")
    gx = np.zeros((D, T))
    gx[:, idx] = dx
    out_0 = gx
    return (out_0,) + planes(out_0)

@@ -1,0 +1,207 @@
+from contextlib import ExitStack
+
+import concourse.mybir as mybir
+
+N, T, D, V = 512, 1024, 512, 1024
+FLOPS = 2 * 2 * N * D * V
+
+F32 = mybir.dt.float32
+BF16 = mybir.dt.bfloat16
+I32 = mybir.dt.int32
+U32 = mybir.dt.uint32
+U16 = mybir.dt.uint16
+U8 = mybir.dt.uint8
+E4M3 = mybir.dt.float8_e4m3fn_x4
+E5M2 = mybir.dt.float8_e5m2_x4
+MULT = mybir.AluOpType.mult
+SUBTRACT = mybir.AluOpType.subtract
+COPY = mybir.ActivationFunctionType.Copy
+
+P = 128
+LANES = 4
+PASSES = V // (P * LANES)
+QUADS = 4
+CHUNKS = 4
+SPLIT = 384
+
+
+def tile_attend_gml_pl_sq_kernel(
+    tc, xT, wd_words, wd_scales, wv_words, wv_scales, y, cw, rw, offs, out_0, out_1, out_2
+):
+    nc = tc.nc
+    with ExitStack() as ctx:
+        keep = ctx.enter_context(tc.tile_pool(name="keep", bufs=1))
+        psum_a = ctx.enter_context(tc.psum_pool(name="psum_a", bufs=4))
+        psum_dx = ctx.enter_context(tc.psum_pool(name="psum_dx", bufs=1))
+
+        def tile(name, shape, dtype):
+            return keep.tile(shape, dtype, name=name, align_bytes=64)
+
+        offsets = keep.tile([P, N // 16], U16, name="offsets")
+        nc.sync.dma_start(offsets[:], offs)
+
+        wd_sc_raw = tile("wd_sc_raw", [P, V], U8)
+        wv_sc_raw = tile("wv_sc_raw", [P, PASSES * D], U8)
+        nc.vector.memset(wd_sc_raw[:].bitcast(I32), 0)
+        nc.vector.memset(wv_sc_raw[:].bitcast(I32), 0)
+
+        x_rows = xT.rearrange("(p r) t -> p r t", r=LANES)
+        x_planes = [tile(f"x{r}", [P, T], F32) for r in range(LANES)]
+        for r in range(LANES):
+            nc.sync.dma_start(x_planes[r][:], x_rows[:, r, :])
+
+        for q in range(QUADS):
+            nc.scalar.dma_start(
+                wd_sc_raw[32 * q : 32 * q + 4, :].bitcast(I32), wd_scales[0, 4 * q : 4 * q + 4, :].bitcast(I32)
+            )
+        wd_raw = tile("wd_raw", [P, V], I32)
+        nc.sync.dma_start(wd_raw[:], wd_words[0].rearrange("p n t -> p (n t)").bitcast(I32))
+        cw_cols = tile("cw_cols", [P, PASSES, LANES], F32)
+        nc.sync.dma_start(cw_cols[:], cw.rearrange("(o p r) one -> p o (r one)", p=P, r=LANES))
+
+        y_rows = y.rearrange("(o p r) i -> o p (r i)", p=P, r=LANES)
+        y_pairs = [[tile(f"y{o}{u}", [P, 2 * N], F32) for u in range(2)] for o in range(PASSES)]
+        rw_rows = tile("rw_rows", [P, N], F32)
+        wv_raw = [tile(f"wv_raw{o}", [P, D], I32) for o in range(PASSES)]
+        for u in range(2):
+            nc.sync.dma_start(y_pairs[0][u][:], y_rows[0, :, 2 * N * u : 2 * N * (u + 1)])
+        for q in range(QUADS):
+            nc.sync.dma_start(
+                wv_sc_raw[32 * q : 32 * q + 4, :].bitcast(I32).rearrange("f (o w) -> f o w", o=PASSES),
+                wv_scales[:, 4 * q : 4 * q + 4, :].bitcast(I32).rearrange("o f w -> f o w"),
+            )
+        nc.sync.dma_start(rw_rows[:], rw)
+        for u in range(2):
+            nc.sync.dma_start(y_pairs[1][u][:], y_rows[1, :, 2 * N * u : 2 * N * (u + 1)])
+        for o in range(PASSES):
+            nc.sync.dma_start(wv_raw[o][:], wv_words[o].rearrange("p n t -> p (n t)").bitcast(I32))
+
+        windows = [tile(f"window{r}", [P, T], F32) for r in range(LANES)]
+        for r in range(LANES):
+            nc.gpsimd.memset(windows[r][:], 0.0)
+
+        def deal(dst, src):
+            nc.vector.tensor_copy(
+                dst.rearrange("p (r c i) -> p c r i", r=LANES, i=2), src.rearrange("p (c i r) -> p c r i", r=LANES, i=2)
+            )
+
+        def deal_bytes(dst, src):
+            nc.vector.tensor_copy(
+                dst.rearrange("p (o r s) -> p o r s", r=LANES, s=P), src.rearrange("p (o s r) -> p o r s", r=LANES, s=P)
+            )
+
+        wd_sc = tile("wd_sc", [P, V], U8)
+        wv_sc = tile("wv_sc", [P, PASSES * D], U8)
+        deal_bytes(wd_sc[:], wd_sc_raw[:])
+
+        picked = [tile(f"picked{u}", [P, 2, N], BF16) for u in range(2)]
+        x_lanes = tile("x_lanes", [P, N, LANES], BF16)
+        for r in range(LANES):
+            nc.vector.tensor_copy(picked[r // 2][:, r % 2, :], x_planes[r][:].indirect(offsets[:]))
+        nc.scalar.activation(x_lanes[:, :, 0:2], picked[0][:].rearrange("p e i -> p i e"), COPY)
+        nc.vector.tensor_copy(x_lanes[:, :, 2:4], picked[1][:].rearrange("p e i -> p i e"))
+
+        wd_codes = [tile(f"wd_codes{o}", [P, V // PASSES], I32) for o in range(PASSES)]
+        deal(wd_codes[0][:], wd_raw[:, 0:512])
+        x_codes = tile("x_codes", [P, N], U32)
+        x_sc = tile("x_sc", [P, N], U8)
+        nc.vector.quantize_mx(
+            out=x_codes[:].bitcast(E4M3), scales=x_sc[:], in_=x_lanes[:].rearrange("p i r -> p (i r)")
+        )
+        deal(wd_codes[1][:], wd_raw[:, 512:1024])
+        deal_bytes(wv_sc[:], wv_sc_raw[:])
+
+        wv_codes = [tile(f"wv_codes{o}", [P, D], I32) for o in range(PASSES)]
+        g_codes = [tile(f"g_codes{o}", [P, N], U32) for o in range(PASSES)]
+        g_sc = [tile(f"g_sc{o}", [P, N], U8) for o in range(PASSES)]
+        dx_banks = [psum_dx.tile([P, N], F32, name=f"dx_bank{r}") for r in range(LANES)]
+        g_lanes = [tile(f"g_lanes{o}", [P, N, LANES], BF16) for o in range(PASSES)]
+        resid = [tile(f"resid{o}", [P, LANES, N], F32) for o in range(PASSES)]
+
+        def residual(o, r):
+            a_bank = psum_a.tile([P, N], F32, name="a_bank")
+            nc.tensor.matmul_mx(
+                out=a_bank[:],
+                lhsT=wd_codes[o][:, r * P : (r + 1) * P].bitcast(E4M3),
+                lhsT_scale=wd_sc[:, (o * LANES + r) * P : (o * LANES + r + 1) * P],
+                rhs=x_codes[:].bitcast(E4M3),
+                rhs_scale=x_sc[:],
+                start=True,
+                stop=True,
+            )
+            ycw = tile(f"ycw{o}{r}", [P, N], F32)
+            weight = cw_cols[:, o, r : r + 1]
+            nc.scalar.activation(ycw[:], y_pairs[o][r // 2][:, (r % 2) * N : (r % 2 + 1) * N], COPY, scale=weight)
+            nc.vector.scalar_tensor_tensor(resid[o][:, r, :], a_bank[:], weight, ycw[:], MULT, SUBTRACT)
+
+        def weigh(o):
+            nc.vector.tensor_tensor(
+                g_lanes[o][:].rearrange("p (c i) r -> p c r i", i=2),
+                resid[o][:].rearrange("p r (c i) -> p c r i", i=2),
+                rw_rows[:].rearrange("p (c i) -> p c i", i=2).unsqueeze(2).to_broadcast([P, N // 2, LANES, 2]),
+                MULT,
+            )
+
+        def quantise_g(o):
+            nc.vector.quantize_mx(
+                out=g_codes[o][:].bitcast(E5M2), scales=g_sc[o][:], in_=g_lanes[o][:].rearrange("p i r -> p (i r)")
+            )
+
+        def back(o, r):
+            nc.tensor.matmul_mx(
+                out=dx_banks[r][:],
+                lhsT=wv_codes[o][:, r * P : (r + 1) * P].bitcast(E4M3),
+                lhsT_scale=wv_sc[:, o * D + r * P : o * D + (r + 1) * P],
+                rhs=g_codes[o][:].bitcast(E5M2),
+                rhs_scale=g_sc[o][:],
+                start=(o == 0),
+                stop=(o == PASSES - 1),
+            )
+
+        for r in range(LANES):
+            residual(0, r)
+        residual(1, 0)
+        weigh(0)
+        residual(1, 1)
+        quantise_g(0)
+        residual(1, 2)
+        residual(1, 3)
+        deal(wv_codes[0][:], wv_raw[0][:])
+        for r in range(LANES):
+            back(0, r)
+        weigh(1)
+        deal(wv_codes[1][:], wv_raw[1][:])
+        quantise_g(1)
+
+        out_rows = out_0.rearrange("(p r) t -> p r t", r=LANES)
+        out_lanes = tile("out_lanes", [P, T, LANES], BF16)
+
+        for r in range(LANES):
+            back(1, r)
+        dx = [tile(f"dx{r}", [P, N], F32) for r in range(LANES)]
+        for r in range(LANES):
+            nc.scalar.copy(dx[r][:], dx_banks[r][:])
+        for r in range(LANES):
+            nc.vector.tensor_copy(windows[r][:].indirect(offsets[:]), dx[r][:])
+            nc.sync.dma_start(out_rows[:, r, :], windows[r][:])
+            if r < LANES - 1:
+                first = SPLIT if r == 2 else 0
+                nc.scalar.copy(out_lanes[:, first:, r], windows[r][:, first:])
+
+        out_sc = tile("out_sc", [P, T], U8)
+        out_words = out_1[0].rearrange("p n t -> p (n t)").bitcast(I32)
+        for r in (2, 3):
+            nc.vector.tensor_copy(out_lanes[:, :SPLIT, r], windows[r][:, :SPLIT])
+        for a, b in ((SPLIT, 512), (512, 768), (768, T)):
+            nc.scalar.copy(out_lanes[:, a:b, 3], windows[3][:, a:b])
+        width = T // CHUNKS
+        for c in range(CHUNKS):
+            cols = slice(c * width, (c + 1) * width)
+            codes = tile(f"out_codes{c}", [P, width], I32)
+            nc.vector.quantize_mx(
+                out=codes[:].bitcast(E4M3), scales=out_sc[:, cols], in_=out_lanes[:, cols, :].rearrange("p t r -> p (t r)")
+            )
+            nc.sync.dma_start(out_words[:, cols], codes[:])
+        queues = (nc.scalar, nc.sync, nc.scalar, nc.sync)
+        for q in range(QUADS):
+            queues[q].dma_start(out_2[0, 4 * q : 4 * q + 4, :].bitcast(I32), out_sc[32 * q : 32 * q + 4, :].bitcast(I32))

@@ -1,6 +1,7 @@
 from contextlib import ExitStack
 
 import concourse.mybir as mybir
+from concourse.masks import make_identity
 
 N, T, D, V = 512, 1024, 512, 1024
 FLOPS = 2 * 2 * N * D * V
@@ -22,7 +23,10 @@ LANES = 4
 PASSES = V // (P * LANES)
 QUADS = 4
 CHUNKS = 4
-SPLIT = 384
+SPLIT = 448
+GP_SLOTS = 512
+FIRST = 128
+X_SPLIT = 352
 
 
 def tile_attend_gml_pl_sq_kernel(
@@ -31,95 +35,112 @@ def tile_attend_gml_pl_sq_kernel(
     nc = tc.nc
     with ExitStack() as ctx:
         keep = ctx.enter_context(tc.tile_pool(name="keep", bufs=1))
-        psum_a = ctx.enter_context(tc.psum_pool(name="psum_a", bufs=4))
-        psum_dx = ctx.enter_context(tc.psum_pool(name="psum_dx", bufs=1))
+        psum_keep = ctx.enter_context(tc.psum_pool(name="psum_keep", bufs=1))
 
         def tile(name, shape, dtype):
             return keep.tile(shape, dtype, name=name, align_bytes=64)
 
         offsets = keep.tile([P, N // 16], U16, name="offsets")
-        nc.sync.dma_start(offsets[:], offs)
 
         wd_sc_raw = tile("wd_sc_raw", [P, V], U8)
         wv_sc_raw = tile("wv_sc_raw", [P, PASSES * D], U8)
-        nc.vector.memset(wd_sc_raw[:].bitcast(I32), 0)
-        nc.vector.memset(wv_sc_raw[:].bitcast(I32), 0)
+        nc.gpsimd.memset(wd_sc_raw[:].bitcast(I32), 0)
+        nc.gpsimd.memset(wv_sc_raw[:].bitcast(I32), 0)
+        for q in range(QUADS):
+            nc.scalar.dma_start(
+                wd_sc_raw[32 * q : 32 * q + 4, :].bitcast(I32), wd_scales[0, 4 * q : 4 * q + 4, :].bitcast(I32)
+            )
 
         x_rows = xT.rearrange("(p r) t -> p r t", r=LANES)
         x_planes = [tile(f"x{r}", [P, T], F32) for r in range(LANES)]
         for r in range(LANES):
             nc.sync.dma_start(x_planes[r][:], x_rows[:, r, :])
+            if r == 0:
+                nc.sync.dma_start(offsets[:], offs)
 
-        for q in range(QUADS):
-            nc.scalar.dma_start(
-                wd_sc_raw[32 * q : 32 * q + 4, :].bitcast(I32), wd_scales[0, 4 * q : 4 * q + 4, :].bitcast(I32)
-            )
-        wd_raw = tile("wd_raw", [P, V], I32)
-        nc.sync.dma_start(wd_raw[:], wd_words[0].rearrange("p n t -> p (n t)").bitcast(I32))
+        rw_cols = keep.tile([P, 2, 2], F32, name="rw_cols", tag="rw_then_codes", align_bytes=64)
+        nc.sync.dma_start(rw_cols[:], rw[0].rearrange("(h p j) -> p h j", h=2, j=2))
         cw_cols = tile("cw_cols", [P, PASSES, LANES], F32)
         nc.sync.dma_start(cw_cols[:], cw.rearrange("(o p r) one -> p o (r one)", p=P, r=LANES))
-
-        y_rows = y.rearrange("(o p r) i -> o p (r i)", p=P, r=LANES)
-        y_pairs = [[tile(f"y{o}{u}", [P, 2 * N], F32) for u in range(2)] for o in range(PASSES)]
-        rw_rows = tile("rw_rows", [P, N], F32)
-        wv_raw = [tile(f"wv_raw{o}", [P, D], I32) for o in range(PASSES)]
-        for u in range(2):
-            nc.sync.dma_start(y_pairs[0][u][:], y_rows[0, :, 2 * N * u : 2 * N * (u + 1)])
+        wd_all = wd_words[0].rearrange("p n t -> p (n t)").bitcast(I32)
+        wd_raw = [
+            keep.tile([P, 512], I32, name="wd_raw0", tag="wd_then_x", align_bytes=64),
+            tile("wd_raw1", [P, 512], I32),
+        ]
+        for o in range(PASSES):
+            nc.sync.dma_start(wd_raw[o][:], wd_all[:, 512 * o : 512 * (o + 1)])
         for q in range(QUADS):
-            nc.sync.dma_start(
+            nc.gpsimd.dma_start(
                 wv_sc_raw[32 * q : 32 * q + 4, :].bitcast(I32).rearrange("f (o w) -> f o w", o=PASSES),
                 wv_scales[:, 4 * q : 4 * q + 4, :].bitcast(I32).rearrange("o f w -> f o w"),
             )
-        nc.sync.dma_start(rw_rows[:], rw)
-        for u in range(2):
-            nc.sync.dma_start(y_pairs[1][u][:], y_rows[1, :, 2 * N * u : 2 * N * (u + 1)])
+        y_rows = y.rearrange("(o p r) i -> o p (r i)", p=P, r=LANES)
+        y_pairs = [[tile(f"y{o}{u}", [P, 2 * N], F32) for u in range(2)] for o in range(PASSES)]
         for o in range(PASSES):
-            nc.sync.dma_start(wv_raw[o][:], wv_words[o].rearrange("p n t -> p (n t)").bitcast(I32))
+            for u in range(2):
+                nc.sync.dma_start(y_pairs[o][u][:], y_rows[o, :, 2 * N * u : 2 * N * (u + 1)])
+        wv_raw = tile("wv_raw", [P, PASSES, D], I32)
+        nc.sync.dma_start(wv_raw[:], wv_words.rearrange("o p n t -> p o (n t)").bitcast(I32))
 
+        identity = tile("identity", [P, P], F32)
+        make_identity(nc, identity[:])
         windows = [tile(f"window{r}", [P, T], F32) for r in range(LANES)]
         for r in range(LANES):
-            nc.gpsimd.memset(windows[r][:], 0.0)
+            (nc.vector if r < 2 else nc.gpsimd).memset(windows[r][:], 0.0)
 
-        def deal(dst, src):
-            nc.vector.tensor_copy(
+        def deal(engine, dst, src):
+            engine.tensor_copy(
                 dst.rearrange("p (r c i) -> p c r i", r=LANES, i=2), src.rearrange("p (c i r) -> p c r i", r=LANES, i=2)
             )
 
-        def deal_bytes(dst, src):
-            nc.vector.tensor_copy(
+        def deal_bytes(engine, dst, src):
+            engine.tensor_copy(
                 dst.rearrange("p (o r s) -> p o r s", r=LANES, s=P), src.rearrange("p (o s r) -> p o r s", r=LANES, s=P)
             )
 
         wd_sc = tile("wd_sc", [P, V], U8)
-        wv_sc = tile("wv_sc", [P, PASSES * D], U8)
-        deal_bytes(wd_sc[:], wd_sc_raw[:])
+        deal_bytes(nc.vector, wd_sc[:], wd_sc_raw[:])
+
+        dx_banks = [psum_keep.tile([P, N], F32, name=f"dx_bank{b}") for b in range(4)]
+        a_banks = [psum_keep.tile([P, N], F32, name=f"a_bank{b}") for b in range(3)]
+        rw_bank = psum_keep.tile([P, 2, 2, P], F32, name="rw_bank")
+        for h in range(2):
+            for j in range(2):
+                nc.tensor.transpose(rw_bank[:, h, j, :], rw_cols[:, h, j : j + 1].to_broadcast([P, P]), identity[:])
 
         picked = [tile(f"picked{u}", [P, 2, N], BF16) for u in range(2)]
-        x_lanes = tile("x_lanes", [P, N, LANES], BF16)
+        x_lanes = keep.tile([P, N, LANES], BF16, name="x_lanes", tag="x_then_sc", align_bytes=64)
         for r in range(LANES):
             nc.vector.tensor_copy(picked[r // 2][:, r % 2, :], x_planes[r][:].indirect(offsets[:]))
         nc.scalar.activation(x_lanes[:, :, 0:2], picked[0][:].rearrange("p e i -> p i e"), COPY)
-        nc.vector.tensor_copy(x_lanes[:, :, 2:4], picked[1][:].rearrange("p e i -> p i e"))
+        nc.vector.tensor_copy(x_lanes[:, :X_SPLIT, 2:4], picked[1][:, :, :X_SPLIT].rearrange("p e i -> p i e"))
+        nc.scalar.copy(x_lanes[:, X_SPLIT:, 2:4], picked[1][:, :, X_SPLIT:].rearrange("p e i -> p i e"))
 
-        wd_codes = [tile(f"wd_codes{o}", [P, V // PASSES], I32) for o in range(PASSES)]
-        deal(wd_codes[0][:], wd_raw[:, 0:512])
-        x_codes = tile("x_codes", [P, N], U32)
+        wd_codes = [
+            keep.tile([P, V // PASSES], I32, name="wd_codes0", tag="rw_then_codes", align_bytes=64),
+            tile("wd_codes1", [P, V // PASSES], I32),
+        ]
+        deal(nc.vector, wd_codes[0][:], wd_raw[0][:])
+        x_codes = keep.tile([P, N], U32, name="x_codes", tag="wd_then_x", align_bytes=64)
         x_sc = tile("x_sc", [P, N], U8)
         nc.vector.quantize_mx(
             out=x_codes[:].bitcast(E4M3), scales=x_sc[:], in_=x_lanes[:].rearrange("p i r -> p (i r)")
         )
-        deal(wd_codes[1][:], wd_raw[:, 512:1024])
-        deal_bytes(wv_sc[:], wv_sc_raw[:])
 
         wv_codes = [tile(f"wv_codes{o}", [P, D], I32) for o in range(PASSES)]
-        g_codes = [tile(f"g_codes{o}", [P, N], U32) for o in range(PASSES)]
+        g_codes = [
+            None,
+            tile("g_codes1", [P, N], U32),
+        ]
         g_sc = [tile(f"g_sc{o}", [P, N], U8) for o in range(PASSES)]
-        dx_banks = [psum_dx.tile([P, N], F32, name=f"dx_bank{r}") for r in range(LANES)]
         g_lanes = [tile(f"g_lanes{o}", [P, N, LANES], BF16) for o in range(PASSES)]
-        resid = [tile(f"resid{o}", [P, LANES, N], F32) for o in range(PASSES)]
+        resid = [
+            tile("resid0", [P, LANES, N], F32),
+            keep.tile([P, LANES, N], F32, name="resid1", tag="g_then_out", align_bytes=64),
+        ]
 
         def residual(o, r):
-            a_bank = psum_a.tile([P, N], F32, name="a_bank")
+            a_bank = a_banks[(o * LANES + r) % 3]
             nc.tensor.matmul_mx(
                 out=a_bank[:],
                 lhsT=wd_codes[o][:, r * P : (r + 1) * P].bitcast(E4M3),
@@ -134,64 +155,97 @@ def tile_attend_gml_pl_sq_kernel(
             nc.scalar.activation(ycw[:], y_pairs[o][r // 2][:, (r % 2) * N : (r % 2 + 1) * N], COPY, scale=weight)
             nc.vector.scalar_tensor_tensor(resid[o][:, r, :], a_bank[:], weight, ycw[:], MULT, SUBTRACT)
 
-        def weigh(o):
-            nc.vector.tensor_tensor(
-                g_lanes[o][:].rearrange("p (c i) r -> p c r i", i=2),
-                resid[o][:].rearrange("p r (c i) -> p c r i", i=2),
-                rw_rows[:].rearrange("p (c i) -> p c i", i=2).unsqueeze(2).to_broadcast([P, N // 2, LANES, 2]),
+        def weigh(engine, o, a, b, rw_pairs):
+            engine.tensor_tensor(
+                g_lanes[o][:, a:b, :].rearrange("p (c i) r -> p c r i", i=2),
+                resid[o][:, :, a:b].rearrange("p r (c i) -> p c r i", i=2),
+                rw_pairs.unsqueeze(2).to_broadcast([P, (b - a) // 2, LANES, 2]),
                 MULT,
             )
+
+        def weigh_vector(o, a, b):
+            h = a // 256
+            weigh(nc.vector, o, a, b, rw_bank[:, h, :, (a - 256 * h) // 2 : (b - 256 * h) // 2].rearrange("p j c -> p c j"))
 
         def quantise_g(o):
             nc.vector.quantize_mx(
                 out=g_codes[o][:].bitcast(E5M2), scales=g_sc[o][:], in_=g_lanes[o][:].rearrange("p i r -> p (i r)")
             )
 
-        def back(o, r):
+        def back(o, r, start):
             nc.tensor.matmul_mx(
-                out=dx_banks[r][:],
+                out=dx_banks[r % 4][:],
                 lhsT=wv_codes[o][:, r * P : (r + 1) * P].bitcast(E4M3),
                 lhsT_scale=wv_sc[:, o * D + r * P : o * D + (r + 1) * P],
                 rhs=g_codes[o][:].bitcast(E5M2),
                 rhs_scale=g_sc[o][:],
-                start=(o == 0),
-                stop=(o == PASSES - 1),
+                start=start,
+                stop=not start,
             )
 
+        deal(nc.vector, wd_codes[1][:], wd_raw[1][:])
+        wv_sc = keep.tile([P, PASSES * D], U8, name="wv_sc", tag="x_then_sc", align_bytes=64)
+        deal_bytes(nc.gpsimd, wv_sc[:], wv_sc_raw[:])
+        rw_rows = tile("rw_rows", [P, N], F32)
+        nc.scalar.copy(rw_rows[:].rearrange("p (h c j) -> p h c j", h=2, j=2), rw_bank[:].rearrange("p h j c -> p h c j"))
+        g_planes = tile("g_planes", [P, LANES, N], BF16)
         for r in range(LANES):
             residual(0, r)
+            if r < 3:
+                nc.gpsimd.tensor_tensor(g_planes[:, r, :], resid[0][:, r, :], rw_rows[:], MULT)
         residual(1, 0)
-        weigh(0)
-        residual(1, 1)
+        for r in range(3, LANES):
+            nc.vector.tensor_tensor(
+                g_planes[:, r, :].rearrange("p (h c j) -> p h c j", h=2, j=2),
+                resid[0][:, r, :].rearrange("p (h c j) -> p h c j", h=2, j=2),
+                rw_bank[:].rearrange("p h j c -> p h c j"),
+                MULT,
+            )
+        for r in range(1, LANES):
+            residual(1, r)
+        nc.scalar.copy(
+            g_lanes[0][:].rearrange("p (c i) r -> p c r i", i=2), g_planes[:].rearrange("p r (c i) -> p c r i", i=2)
+        )
+        for o in range(PASSES):
+            deal(nc.gpsimd, wv_codes[o][:], wv_raw[:, o, :])
+        weigh_vector(1, 0, 256)
+        weigh_vector(1, 256, N)
+        g_codes[0] = keep.tile([P, N], U32, name="g_codes0", tag="g_then_out", align_bytes=64)
         quantise_g(0)
-        residual(1, 2)
-        residual(1, 3)
-        deal(wv_codes[0][:], wv_raw[0][:])
-        for r in range(LANES):
-            back(0, r)
-        weigh(1)
-        deal(wv_codes[1][:], wv_raw[1][:])
         quantise_g(1)
 
         out_rows = out_0.rearrange("(p r) t -> p r t", r=LANES)
-        out_lanes = tile("out_lanes", [P, T, LANES], BF16)
 
-        for r in range(LANES):
-            back(1, r)
         dx = [tile(f"dx{r}", [P, N], F32) for r in range(LANES)]
         for r in range(LANES):
-            nc.scalar.copy(dx[r][:], dx_banks[r][:])
+            order = (0, 1) if r == 0 else (1, 0)
+            back(order[0], r, True)
+            back(order[1], r, False)
+            if r == 0:
+                nc.scalar.copy(dx[0][:, :FIRST], dx_banks[0][:, :FIRST])
+                nc.scalar.copy(dx[0][:, FIRST:], dx_banks[0][:, FIRST:])
+            else:
+                nc.scalar.copy(dx[r][:], dx_banks[r % 4][:])
+        out_lanes = keep.tile([P, T, LANES], BF16, name="out_lanes", tag="g_then_out", align_bytes=64)
         for r in range(LANES):
-            nc.vector.tensor_copy(windows[r][:].indirect(offsets[:]), dx[r][:])
+            if r == 0:
+                nc.vector.tensor_copy(windows[r][:].indirect(offsets[:, : FIRST // 16]), dx[r][:, :FIRST])
+                nc.vector.tensor_copy(windows[r][:].indirect(offsets[:, FIRST // 16 :]), dx[r][:, FIRST:])
+            else:
+                nc.vector.tensor_copy(windows[r][:].indirect(offsets[:]), dx[r][:])
             nc.sync.dma_start(out_rows[:, r, :], windows[r][:])
             if r < LANES - 1:
                 first = SPLIT if r == 2 else 0
                 nc.scalar.copy(out_lanes[:, first:, r], windows[r][:, first:])
+        staged = tile("staged", [P, 2, SPLIT], BF16)
+        nc.scalar.copy(staged[:, 0, :], windows[2][:, :SPLIT])
 
         out_sc = tile("out_sc", [P, T], U8)
         out_words = out_1[0].rearrange("p n t -> p (n t)").bitcast(I32)
-        for r in (2, 3):
-            nc.vector.tensor_copy(out_lanes[:, :SPLIT, r], windows[r][:, :SPLIT])
+        for a, b in ((0, 256), (256, SPLIT)):
+            nc.vector.tensor_copy(staged[:, 1, a:b], windows[3][:, a:b])
+        for a, b in ((0, 256), (256, SPLIT)):
+            nc.vector.tensor_copy(out_lanes[:, a:b, 2:4], staged[:, :, a:b].rearrange("p e t -> p t e"))
         for a, b in ((SPLIT, 512), (512, 768), (768, T)):
             nc.scalar.copy(out_lanes[:, a:b, 3], windows[3][:, a:b])
         width = T // CHUNKS

@@ -23,10 +23,10 @@ LANES = 4
 PASSES = V // (P * LANES)
 QUADS = 4
 CHUNKS = 4
-SPLIT = 448
-GP_SLOTS = 512
-FIRST = 128
-X_SPLIT = 352
+SPLIT = 512
+BLOCKS = N // P
+HALF = N // 2
+LANE_ORDER = (2, 0, 1, 3)
 
 
 def tile_attend_gml_pl_sq_kernel(
@@ -46,47 +46,44 @@ def tile_attend_gml_pl_sq_kernel(
         wv_sc_raw = tile("wv_sc_raw", [P, PASSES * D], U8)
         nc.gpsimd.memset(wd_sc_raw[:].bitcast(I32), 0)
         nc.gpsimd.memset(wv_sc_raw[:].bitcast(I32), 0)
-        for q in range(QUADS):
-            nc.scalar.dma_start(
-                wd_sc_raw[32 * q : 32 * q + 4, :].bitcast(I32), wd_scales[0, 4 * q : 4 * q + 4, :].bitcast(I32)
-            )
+        identity = tile("identity", [P, P], F32)
+        make_identity(nc, identity[:])
 
         x_rows = xT.rearrange("(p r) t -> p r t", r=LANES)
         x_planes = [tile(f"x{r}", [P, T], F32) for r in range(LANES)]
-        for r in range(LANES):
-            nc.sync.dma_start(x_planes[r][:], x_rows[:, r, :])
-            if r == 0:
-                nc.sync.dma_start(offsets[:], offs)
-
-        rw_cols = keep.tile([P, 2, 2], F32, name="rw_cols", tag="rw_then_codes", align_bytes=64)
-        nc.sync.dma_start(rw_cols[:], rw[0].rearrange("(h p j) -> p h j", h=2, j=2))
+        wd_all = wd_words[0].rearrange("p n t -> p (n t)").bitcast(I32)
+        wd_raw = [tile(f"wd_raw{o}", [P, 512], I32) for o in range(PASSES)]
+        nc.sync.dma_start(x_planes[0][:], x_rows[:, 0, :])
+        for q in range(QUADS):
+            nc.sync.dma_start(
+                wd_sc_raw[32 * q : 32 * q + 4, :].bitcast(I32), wd_scales[0, 4 * q : 4 * q + 4, :].bitcast(I32)
+            )
+        nc.sync.dma_start(offsets[:], offs)
+        nc.sync.dma_start(x_planes[1][:], x_rows[:, 1, :])
+        nc.sync.dma_start(x_planes[2][:], x_rows[:, 2, :])
+        nc.sync.dma_start(x_planes[3][:], x_rows[:, 3, :])
+        nc.sync.dma_start(wd_raw[0][:], wd_all[:, :512])
+        rw_cols = tile("rw_cols", [P, BLOCKS], F32)
+        nc.sync.dma_start(rw_cols[:], rw[0].rearrange("(c p) -> p c", p=P))
         cw_cols = tile("cw_cols", [P, PASSES, LANES], F32)
         nc.sync.dma_start(cw_cols[:], cw.rearrange("(o p r) one -> p o (r one)", p=P, r=LANES))
-        wd_all = wd_words[0].rearrange("p n t -> p (n t)").bitcast(I32)
-        wd_raw = [
-            keep.tile([P, 512], I32, name="wd_raw0", tag="wd_then_x", align_bytes=64),
-            tile("wd_raw1", [P, 512], I32),
-        ]
-        for o in range(PASSES):
-            nc.sync.dma_start(wd_raw[o][:], wd_all[:, 512 * o : 512 * (o + 1)])
+        nc.sync.dma_start(wd_raw[1][:], wd_all[:, 512:])
         for q in range(QUADS):
             nc.gpsimd.dma_start(
                 wv_sc_raw[32 * q : 32 * q + 4, :].bitcast(I32).rearrange("f (o w) -> f o w", o=PASSES),
                 wv_scales[:, 4 * q : 4 * q + 4, :].bitcast(I32).rearrange("o f w -> f o w"),
             )
         y_rows = y.rearrange("(o p r) i -> o p (r i)", p=P, r=LANES)
-        y_pairs = [[tile(f"y{o}{u}", [P, 2 * N], F32) for u in range(2)] for o in range(PASSES)]
+        y_pairs = [
+            [keep.tile([P, 2 * N], F32, name=f"y{o}{u}", tag=f"y_then_window{2 * o + u}", align_bytes=64) for u in range(2)]
+            for o in range(PASSES)
+        ]
         for o in range(PASSES):
             for u in range(2):
                 nc.sync.dma_start(y_pairs[o][u][:], y_rows[o, :, 2 * N * u : 2 * N * (u + 1)])
         wv_raw = tile("wv_raw", [P, PASSES, D], I32)
         nc.sync.dma_start(wv_raw[:], wv_words.rearrange("o p n t -> p o (n t)").bitcast(I32))
 
-        identity = tile("identity", [P, P], F32)
-        make_identity(nc, identity[:])
-        windows = [tile(f"window{r}", [P, T], F32) for r in range(LANES)]
-        for r in range(LANES):
-            (nc.vector if r < 2 else nc.gpsimd).memset(windows[r][:], 0.0)
 
         def deal(engine, dst, src):
             engine.tensor_copy(
@@ -101,154 +98,183 @@ def tile_attend_gml_pl_sq_kernel(
         wd_sc = tile("wd_sc", [P, V], U8)
         deal_bytes(nc.vector, wd_sc[:], wd_sc_raw[:])
 
-        dx_banks = [psum_keep.tile([P, N], F32, name=f"dx_bank{b}") for b in range(4)]
-        a_banks = [psum_keep.tile([P, N], F32, name=f"a_bank{b}") for b in range(3)]
-        rw_bank = psum_keep.tile([P, 2, 2, P], F32, name="rw_bank")
-        for h in range(2):
-            for j in range(2):
-                nc.tensor.transpose(rw_bank[:, h, j, :], rw_cols[:, h, j : j + 1].to_broadcast([P, P]), identity[:])
+        banks = [psum_keep.tile([P, N], F32, name=f"bank{b}") for b in range(7)]
+        turn_banks = banks[1:5]
+        word_banks = [bank[:].rearrange("p (u i) -> p u i", u=2) for bank in banks[1:3]]
+        dx_banks = banks[3:7]
+        rw_bank = psum_keep.tile([P, N], F32, name="rw_bank")
+        for c in range(BLOCKS):
+            nc.tensor.transpose(rw_bank[:, c * P : (c + 1) * P], rw_cols[:, c : c + 1].to_broadcast([P, P]), identity[:])
 
         picked = [tile(f"picked{u}", [P, 2, N], BF16) for u in range(2)]
-        x_lanes = keep.tile([P, N, LANES], BF16, name="x_lanes", tag="x_then_sc", align_bytes=64)
-        for r in range(LANES):
+        x_lanes = tile("x_lanes", [P, N, LANES], BF16)
+        x_first = tile("x_first", [P, T], BF16)
+        nc.scalar.copy(x_first[:], x_planes[0][:])
+        nc.scalar.activation(picked[0][:, 0, :], x_first[:].indirect(offsets[:]), COPY)
+        for r in range(1, LANES - 1):
             nc.vector.tensor_copy(picked[r // 2][:, r % 2, :], x_planes[r][:].indirect(offsets[:]))
-        nc.scalar.activation(x_lanes[:, :, 0:2], picked[0][:].rearrange("p e i -> p i e"), COPY)
-        nc.vector.tensor_copy(x_lanes[:, :X_SPLIT, 2:4], picked[1][:, :, :X_SPLIT].rearrange("p e i -> p i e"))
-        nc.scalar.copy(x_lanes[:, X_SPLIT:, 2:4], picked[1][:, :, X_SPLIT:].rearrange("p e i -> p i e"))
+        for h in range(2):
+            nc.vector.tensor_copy(
+                picked[1][:, 1, h * HALF : (h + 1) * HALF],
+                x_planes[3][:].indirect(offsets[:, h * HALF // 16 : (h + 1) * HALF // 16]),
+            )
+        nc.scalar.copy(x_lanes[:, :, 0:2], picked[0][:].rearrange("p e i -> p i e"))
+        nc.scalar.copy(x_lanes[:, :HALF, 2:4], picked[1][:, :, :HALF].rearrange("p e i -> p i e"))
+        nc.vector.tensor_copy(x_lanes[:, HALF:, 2:4], picked[1][:, :, HALF:].rearrange("p e i -> p i e"))
 
-        wd_codes = [
-            keep.tile([P, V // PASSES], I32, name="wd_codes0", tag="rw_then_codes", align_bytes=64),
-            tile("wd_codes1", [P, V // PASSES], I32),
-        ]
-        deal(nc.vector, wd_codes[0][:], wd_raw[0][:])
-        x_codes = keep.tile([P, N], U32, name="x_codes", tag="wd_then_x", align_bytes=64)
+        wd_codes = [tile(f"wd_codes{o}", [P, V // PASSES], I32) for o in range(PASSES)]
+        wv_sc = tile("wv_sc", [P, PASSES * D], U8)
+        deal(nc.gpsimd, wd_codes[0][:], wd_raw[0][:])
+        deal(nc.gpsimd, wd_codes[1][:], wd_raw[1][:])
+        deal_bytes(nc.gpsimd, wv_sc[:], wv_sc_raw[:])
+        x_codes = tile("x_codes", [P, N], U32)
         x_sc = tile("x_sc", [P, N], U8)
-        nc.vector.quantize_mx(
-            out=x_codes[:].bitcast(E4M3), scales=x_sc[:], in_=x_lanes[:].rearrange("p i r -> p (i r)")
-        )
+        for h in range(2):
+            cols = slice(h * HALF, (h + 1) * HALF)
+            nc.vector.quantize_mx(
+                out=x_codes[:, cols].bitcast(E4M3), scales=x_sc[:, cols], in_=x_lanes[:, cols, :].rearrange("p i r -> p (i r)")
+            )
 
-        wv_codes = [tile(f"wv_codes{o}", [P, D], I32) for o in range(PASSES)]
-        g_codes = [
-            None,
-            tile("g_codes1", [P, N], U32),
-        ]
+        g_codes = [tile(f"g_codes{o}", [P, N], U32) for o in range(PASSES)]
         g_sc = [tile(f"g_sc{o}", [P, N], U8) for o in range(PASSES)]
+        for o in range(PASSES):
+            nc.gpsimd.memset(g_codes[o][:, HALF:], 0)
+            nc.gpsimd.memset(g_sc[o][:, HALF:].bitcast(U32), 0)
         g_lanes = [tile(f"g_lanes{o}", [P, N, LANES], BF16) for o in range(PASSES)]
-        resid = [
-            tile("resid0", [P, LANES, N], F32),
-            keep.tile([P, LANES, N], F32, name="resid1", tag="g_then_out", align_bytes=64),
-        ]
+        resid = [tile(f"resid{o}", [P, LANES, N], F32) for o in range(PASSES)]
 
-        def residual(o, r):
-            a_bank = a_banks[(o * LANES + r) % 3]
+        def scores(out, o, r, a, b):
             nc.tensor.matmul_mx(
-                out=a_bank[:],
+                out=out,
                 lhsT=wd_codes[o][:, r * P : (r + 1) * P].bitcast(E4M3),
                 lhsT_scale=wd_sc[:, (o * LANES + r) * P : (o * LANES + r + 1) * P],
-                rhs=x_codes[:].bitcast(E4M3),
-                rhs_scale=x_sc[:],
+                rhs=x_codes[:, a:b].bitcast(E4M3),
+                rhs_scale=x_sc[:, a:b],
                 start=True,
                 stop=True,
             )
-            ycw = tile(f"ycw{o}{r}", [P, N], F32)
-            weight = cw_cols[:, o, r : r + 1]
-            nc.scalar.activation(ycw[:], y_pairs[o][r // 2][:, (r % 2) * N : (r % 2 + 1) * N], COPY, scale=weight)
-            nc.vector.scalar_tensor_tensor(resid[o][:, r, :], a_bank[:], weight, ycw[:], MULT, SUBTRACT)
 
-        def weigh(engine, o, a, b, rw_pairs):
-            engine.tensor_tensor(
+        def y_plane(o, r):
+            return y_pairs[o][r // 2][:, (r % 2) * N : (r % 2 + 1) * N]
+
+        def quantise_g(o, h):
+            cols = slice(h * HALF, (h + 1) * HALF)
+            nc.vector.quantize_mx(
+                out=g_codes[o][:, cols].bitcast(E5M2),
+                scales=g_sc[o][:, cols],
+                in_=g_lanes[o][:, cols, :].rearrange("p i r -> p (i r)"),
+            )
+
+        def scale_y(o, r):
+            ycw = tile(f"ycw{o}{r}", [P, N], F32)
+            nc.scalar.activation(ycw[:], y_plane(o, r), COPY, scale=cw_cols[:, o, r : r + 1])
+            return ycw
+
+        def residual(sums, ycw, o, r, a, b):
+            nc.vector.scalar_tensor_tensor(
+                resid[o][:, r, a:b], sums, cw_cols[:, o, r : r + 1], ycw[:, a:b], MULT, SUBTRACT
+            )
+
+        def weigh(o, a, b):
+            pairs = rw_bank[:, a:b].rearrange("p (c i) -> p c i", i=2)
+            nc.vector.tensor_tensor(
                 g_lanes[o][:, a:b, :].rearrange("p (c i) r -> p c r i", i=2),
                 resid[o][:, :, a:b].rearrange("p r (c i) -> p c r i", i=2),
-                rw_pairs.unsqueeze(2).to_broadcast([P, (b - a) // 2, LANES, 2]),
+                pairs.unsqueeze(2).to_broadcast([P, (b - a) // 2, LANES, 2]),
                 MULT,
             )
 
-        def weigh_vector(o, a, b):
-            h = a // 256
-            weigh(nc.vector, o, a, b, rw_bank[:, h, :, (a - 256 * h) // 2 : (b - 256 * h) // 2].rearrange("p j c -> p c j"))
-
-        def quantise_g(o):
-            nc.vector.quantize_mx(
-                out=g_codes[o][:].bitcast(E5M2), scales=g_sc[o][:], in_=g_lanes[o][:].rearrange("p i r -> p (i r)")
+        early = [scale_y(0, r) for r in range(2)]
+        for h in range(2):
+            for r in range(2):
+                scores(banks[h][:, r * HALF : (r + 1) * HALF], 0, r, h * HALF, (h + 1) * HALF)
+            for r in range(2):
+                residual(banks[h][:, r * HALF : (r + 1) * HALF], early[r], 0, r, h * HALF, (h + 1) * HALF)
+        for plane in range(2, PASSES * LANES):
+            o, r = divmod(plane, LANES)
+            bank = banks[plane % len(banks)]
+            scores(bank[:], o, r, 0, N)
+            residual(bank[:], scale_y(o, r), o, r, 0, N)
+        for c in range(BLOCKS):
+            bank = turn_banks[c]
+            for r in range(LANES):
+                nc.tensor.transpose(bank[:, r * P : (r + 1) * P], resid[0][:, r, c * P : (c + 1) * P], identity[:])
+            turned = tile(f"turned{c}", [P, 2, P, 2], BF16)
+            nc.scalar.activation(
+                turned[:], bank[:].rearrange("i (u e p) -> i u p e", u=2, e=2), COPY, scale=rw_cols[:, c : c + 1]
             )
+            h, j = divmod(c, 2)
+            for u in range(2):
+                nc.tensor.transpose(
+                    word_banks[h][:, u, j * P : (j + 1) * P],
+                    turned[:, u, :, :].rearrange("i p e -> i (p e)").bitcast(F32),
+                    identity[:],
+                )
+            if j == 1:
+                nc.scalar.copy(
+                    g_lanes[0][:, h * HALF : (h + 1) * HALF, :].rearrange("p i r -> p (i r)").bitcast(F32).rearrange("p (i u) -> p i u", u=2),
+                    word_banks[h].rearrange("p u i -> p i u"),
+                )
+        wv_codes = tile("wv_codes", [P, PASSES, D], I32)
+        for o in (1, 0):
+            deal(nc.gpsimd, wv_codes[:, o, :], wv_raw[:, o, :])
+        windows = [None] * LANES
+        for k, r in enumerate(LANE_ORDER):
+            windows[r] = keep.tile([P, T], F32, name=f"window{r}", tag=f"y_then_window{k}", align_bytes=64)
+            nc.gpsimd.memset(windows[r][:], 0.0)
 
-        def back(o, r, start):
-            nc.tensor.matmul_mx(
-                out=dx_banks[r % 4][:],
-                lhsT=wv_codes[o][:, r * P : (r + 1) * P].bitcast(E4M3),
-                lhsT_scale=wv_sc[:, o * D + r * P : o * D + (r + 1) * P],
-                rhs=g_codes[o][:].bitcast(E5M2),
-                rhs_scale=g_sc[o][:],
-                start=start,
-                stop=not start,
-            )
+        def back(bank, r):
+            for o in (1, 0):
+                nc.tensor.matmul_mx(
+                    out=bank[:],
+                    lhsT=wv_codes[:, o, r * P : (r + 1) * P].bitcast(E4M3),
+                    lhsT_scale=wv_sc[:, o * D + r * P : o * D + (r + 1) * P],
+                    rhs=g_codes[o][:].bitcast(E5M2),
+                    rhs_scale=g_sc[o][:],
+                    start=o == 1,
+                    stop=o == 0,
+                )
 
-        deal(nc.vector, wd_codes[1][:], wd_raw[1][:])
-        wv_sc = keep.tile([P, PASSES * D], U8, name="wv_sc", tag="x_then_sc", align_bytes=64)
-        deal_bytes(nc.gpsimd, wv_sc[:], wv_sc_raw[:])
-        rw_rows = tile("rw_rows", [P, N], F32)
-        nc.scalar.copy(rw_rows[:].rearrange("p (h c j) -> p h c j", h=2, j=2), rw_bank[:].rearrange("p h j c -> p h c j"))
-        g_planes = tile("g_planes", [P, LANES, N], BF16)
-        for r in range(LANES):
-            residual(0, r)
-            if r < 3:
-                nc.gpsimd.tensor_tensor(g_planes[:, r, :], resid[0][:, r, :], rw_rows[:], MULT)
-        residual(1, 0)
-        for r in range(3, LANES):
-            nc.vector.tensor_tensor(
-                g_planes[:, r, :].rearrange("p (h c j) -> p h c j", h=2, j=2),
-                resid[0][:, r, :].rearrange("p (h c j) -> p h c j", h=2, j=2),
-                rw_bank[:].rearrange("p h j c -> p h c j"),
-                MULT,
-            )
-        for r in range(1, LANES):
-            residual(1, r)
-        nc.scalar.copy(
-            g_lanes[0][:].rearrange("p (c i) r -> p c r i", i=2), g_planes[:].rearrange("p r (c i) -> p c r i", i=2)
-        )
-        for o in range(PASSES):
-            deal(nc.gpsimd, wv_codes[o][:], wv_raw[:, o, :])
-        weigh_vector(1, 0, 256)
-        weigh_vector(1, 256, N)
-        g_codes[0] = keep.tile([P, N], U32, name="g_codes0", tag="g_then_out", align_bytes=64)
-        quantise_g(0)
-        quantise_g(1)
+        weigh(1, 0, HALF)
+        quantise_g(1, 0)
+        quantise_g(0, 0)
+        back(banks[0], LANE_ORDER[0])
+        weigh(1, HALF, N)
+        quantise_g(1, 1)
+        quantise_g(0, 1)
 
         out_rows = out_0.rearrange("(p r) t -> p r t", r=LANES)
+        out_lanes = tile("out_lanes", [P, T, LANES], BF16)
 
-        dx = [tile(f"dx{r}", [P, N], F32) for r in range(LANES)]
-        for r in range(LANES):
-            order = (0, 1) if r == 0 else (1, 0)
-            back(order[0], r, True)
-            back(order[1], r, False)
-            if r == 0:
-                nc.scalar.copy(dx[0][:, :FIRST], dx_banks[0][:, :FIRST])
-                nc.scalar.copy(dx[0][:, FIRST:], dx_banks[0][:, FIRST:])
+        def empty(k):
+            dx = keep.tile([P, N], F32, name=f"dx{k}", tag=f"dx{k % 3}", align_bytes=64)
+            if k == 0:
+                nc.scalar.copy(dx[:, :HALF], banks[0][:, :HALF])
+                nc.scalar.copy(dx[:, HALF:], dx_banks[0][:, HALF:])
             else:
-                nc.scalar.copy(dx[r][:], dx_banks[r % 4][:])
-        out_lanes = keep.tile([P, T, LANES], BF16, name="out_lanes", tag="g_then_out", align_bytes=64)
-        for r in range(LANES):
-            if r == 0:
-                nc.vector.tensor_copy(windows[r][:].indirect(offsets[:, : FIRST // 16]), dx[r][:, :FIRST])
-                nc.vector.tensor_copy(windows[r][:].indirect(offsets[:, FIRST // 16 :]), dx[r][:, FIRST:])
-            else:
-                nc.vector.tensor_copy(windows[r][:].indirect(offsets[:]), dx[r][:])
+                nc.scalar.copy(dx[:], dx_banks[k][:])
+            return dx
+
+        for k, r in enumerate(LANE_ORDER):
+            back(dx_banks[k], r)
+        dxs = [empty(k) for k in range(LANES - 1)]
+        for k, r in enumerate(LANE_ORDER):
+            for a, b in ((0, HALF), (HALF, N)) if k == 0 else ((0, N),):
+                nc.vector.tensor_copy(windows[r][:].indirect(offsets[:, a // 16 : b // 16]), dxs[k][:, a:b])
             nc.sync.dma_start(out_rows[:, r, :], windows[r][:])
-            if r < LANES - 1:
-                first = SPLIT if r == 2 else 0
-                nc.scalar.copy(out_lanes[:, first:, r], windows[r][:, first:])
-        staged = tile("staged", [P, 2, SPLIT], BF16)
-        nc.scalar.copy(staged[:, 0, :], windows[2][:, :SPLIT])
+            if k < LANES - 1:
+                nc.scalar.copy(out_lanes[:, :, r], windows[r][:])
+            if k == 0:
+                dxs.append(empty(LANES - 1))
 
+        last = LANE_ORDER[-1]
         out_sc = tile("out_sc", [P, T], U8)
         out_words = out_1[0].rearrange("p n t -> p (n t)").bitcast(I32)
-        for a, b in ((0, 256), (256, SPLIT)):
-            nc.vector.tensor_copy(staged[:, 1, a:b], windows[3][:, a:b])
-        for a, b in ((0, 256), (256, SPLIT)):
-            nc.vector.tensor_copy(out_lanes[:, a:b, 2:4], staged[:, :, a:b].rearrange("p e t -> p t e"))
-        for a, b in ((SPLIT, 512), (512, 768), (768, T)):
-            nc.scalar.copy(out_lanes[:, a:b, 3], windows[3][:, a:b])
         width = T // CHUNKS
+        for a in range(0, SPLIT, width):
+            nc.vector.tensor_copy(out_lanes[:, a : a + width, last], windows[last][:, a : a + width])
+        for a in range(SPLIT, T, width):
+            nc.scalar.copy(out_lanes[:, a : a + width, last], windows[last][:, a : a + width])
         for c in range(CHUNKS):
             cols = slice(c * width, (c + 1) * width)
             codes = tile(f"out_codes{c}", [P, width], I32)

@@ -23,7 +23,8 @@ LANES = 4
 PASSES = V // (P * LANES)
 QUADS = 4
 CHUNKS = 4
-SPLIT = 512
+SPLIT = 576
+LATE = 128
 BLOCKS = N // P
 HALF = N // 2
 LANE_ORDER = (2, 0, 1, 3)
@@ -68,22 +69,22 @@ def tile_attend_gml_pl_sq_kernel(
         cw_cols = tile("cw_cols", [P, PASSES, LANES], F32)
         nc.sync.dma_start(cw_cols[:], cw.rearrange("(o p r) one -> p o (r one)", p=P, r=LANES))
         nc.sync.dma_start(wd_raw[1][:], wd_all[:, 512:])
+        y_rows = y.rearrange("(o p r) i -> o p (r i)", p=P, r=LANES)
+        y_pairs = [[tile(f"y{o}{u}", [P, 2 * N], F32) for u in range(2)] for o in range(PASSES)]
+        for o, u in ((0, 0), (0, 1), (1, 0), (1, 1)):
+            nc.sync.dma_start(y_pairs[o][u][:], y_rows[o, :, 2 * N * u : 2 * N * (u + 1)])
         for q in range(QUADS):
-            nc.gpsimd.dma_start(
+            nc.sync.dma_start(
                 wv_sc_raw[32 * q : 32 * q + 4, :].bitcast(I32).rearrange("f (o w) -> f o w", o=PASSES),
                 wv_scales[:, 4 * q : 4 * q + 4, :].bitcast(I32).rearrange("o f w -> f o w"),
             )
-        y_rows = y.rearrange("(o p r) i -> o p (r i)", p=P, r=LANES)
-        y_pairs = [
-            [keep.tile([P, 2 * N], F32, name=f"y{o}{u}", tag=f"y_then_window{2 * o + u}", align_bytes=64) for u in range(2)]
-            for o in range(PASSES)
-        ]
-        for o in range(PASSES):
-            for u in range(2):
-                nc.sync.dma_start(y_pairs[o][u][:], y_rows[o, :, 2 * N * u : 2 * N * (u + 1)])
         wv_raw = tile("wv_raw", [P, PASSES, D], I32)
         nc.sync.dma_start(wv_raw[:], wv_words.rearrange("o p n t -> p o (n t)").bitcast(I32))
 
+
+        windows = [tile(f"window{r}", [P, T], F32) for r in range(LANES)]
+        for r in range(LANES):
+            nc.gpsimd.memset(windows[r][:], 0.0)
 
         def deal(engine, dst, src):
             engine.tensor_copy(
@@ -99,7 +100,7 @@ def tile_attend_gml_pl_sq_kernel(
         deal_bytes(nc.vector, wd_sc[:], wd_sc_raw[:])
 
         banks = [psum_keep.tile([P, N], F32, name=f"bank{b}") for b in range(7)]
-        turn_banks = banks[1:5]
+        turn_banks = [banks[b] for b in (1, 2, 3, 4)]
         word_banks = [bank[:].rearrange("p (u i) -> p u i", u=2) for bank in banks[1:3]]
         dx_banks = banks[3:7]
         rw_bank = psum_keep.tile([P, N], F32, name="rw_bank")
@@ -107,7 +108,7 @@ def tile_attend_gml_pl_sq_kernel(
             nc.tensor.transpose(rw_bank[:, c * P : (c + 1) * P], rw_cols[:, c : c + 1].to_broadcast([P, P]), identity[:])
 
         picked = [tile(f"picked{u}", [P, 2, N], BF16) for u in range(2)]
-        x_lanes = tile("x_lanes", [P, N, LANES], BF16)
+        x_lanes = keep.tile([P, N, LANES], BF16, name="x_lanes", tag="x_then_wd", align_bytes=64)
         x_first = tile("x_first", [P, T], BF16)
         nc.scalar.copy(x_first[:], x_planes[0][:])
         nc.scalar.activation(picked[0][:, 0, :], x_first[:].indirect(offsets[:]), COPY)
@@ -122,11 +123,8 @@ def tile_attend_gml_pl_sq_kernel(
         nc.scalar.copy(x_lanes[:, :HALF, 2:4], picked[1][:, :, :HALF].rearrange("p e i -> p i e"))
         nc.vector.tensor_copy(x_lanes[:, HALF:, 2:4], picked[1][:, :, HALF:].rearrange("p e i -> p i e"))
 
-        wd_codes = [tile(f"wd_codes{o}", [P, V // PASSES], I32) for o in range(PASSES)]
-        wv_sc = tile("wv_sc", [P, PASSES * D], U8)
+        wd_codes = [tile("wd_codes0", [P, V // PASSES], I32)]
         deal(nc.gpsimd, wd_codes[0][:], wd_raw[0][:])
-        deal(nc.gpsimd, wd_codes[1][:], wd_raw[1][:])
-        deal_bytes(nc.gpsimd, wv_sc[:], wv_sc_raw[:])
         x_codes = tile("x_codes", [P, N], U32)
         x_sc = tile("x_sc", [P, N], U8)
         for h in range(2):
@@ -134,6 +132,8 @@ def tile_attend_gml_pl_sq_kernel(
             nc.vector.quantize_mx(
                 out=x_codes[:, cols].bitcast(E4M3), scales=x_sc[:, cols], in_=x_lanes[:, cols, :].rearrange("p i r -> p (i r)")
             )
+        wd_codes.append(keep.tile([P, V // PASSES], I32, name="wd_codes1", tag="x_then_wd", align_bytes=64))
+        deal(nc.gpsimd, wd_codes[1][:], wd_raw[1][:])
 
         g_codes = [tile(f"g_codes{o}", [P, N], U32) for o in range(PASSES)]
         g_sc = [tile(f"g_sc{o}", [P, N], U8) for o in range(PASSES)]
@@ -215,13 +215,11 @@ def tile_attend_gml_pl_sq_kernel(
                     g_lanes[0][:, h * HALF : (h + 1) * HALF, :].rearrange("p i r -> p (i r)").bitcast(F32).rearrange("p (i u) -> p i u", u=2),
                     word_banks[h].rearrange("p u i -> p i u"),
                 )
+        wv_sc = tile("wv_sc", [P, PASSES * D], U8)
+        deal_bytes(nc.gpsimd, wv_sc[:], wv_sc_raw[:])
         wv_codes = tile("wv_codes", [P, PASSES, D], I32)
         for o in (1, 0):
             deal(nc.gpsimd, wv_codes[:, o, :], wv_raw[:, o, :])
-        windows = [None] * LANES
-        for k, r in enumerate(LANE_ORDER):
-            windows[r] = keep.tile([P, T], F32, name=f"window{r}", tag=f"y_then_window{k}", align_bytes=64)
-            nc.gpsimd.memset(windows[r][:], 0.0)
 
         def back(bank, r):
             for o in (1, 0):
@@ -246,42 +244,48 @@ def tile_attend_gml_pl_sq_kernel(
         out_rows = out_0.rearrange("(p r) t -> p r t", r=LANES)
         out_lanes = tile("out_lanes", [P, T, LANES], BF16)
 
-        def empty(k):
-            dx = keep.tile([P, N], F32, name=f"dx{k}", tag=f"dx{k % 3}", align_bytes=64)
-            if k == 0:
-                nc.scalar.copy(dx[:, :HALF], banks[0][:, :HALF])
-                nc.scalar.copy(dx[:, HALF:], dx_banks[0][:, HALF:])
-            else:
-                nc.scalar.copy(dx[:], dx_banks[k][:])
-            return dx
-
         for k, r in enumerate(LANE_ORDER):
             back(dx_banks[k], r)
-        dxs = [empty(k) for k in range(LANES - 1)]
+        pieces = [[(0, HALF), (HALF, N)], [(0, N)], [(0, N)], [(0, N - LATE), (N - LATE, N)]]
+        dx = {}
+
+        def empty(k, a, b, bank, tag):
+            dx[k, a] = keep.tile([P, b - a], F32, name=f"dx{k}_{a}", tag=tag, align_bytes=64)
+            nc.scalar.copy(dx[k, a][:], bank[:, a:b])
+
+        empty(0, 0, HALF, banks[0], "dx_first")
+        empty(0, HALF, N, dx_banks[0], "dx_ring")
+        for k in range(1, LANES):
+            a, b = pieces[k][0]
+            empty(k, a, b, dx_banks[k], f"dx{k}")
         for k, r in enumerate(LANE_ORDER):
-            for a, b in ((0, HALF), (HALF, N)) if k == 0 else ((0, N),):
-                nc.vector.tensor_copy(windows[r][:].indirect(offsets[:, a // 16 : b // 16]), dxs[k][:, a:b])
+            for a, b in pieces[k]:
+                nc.vector.tensor_copy(windows[r][:].indirect(offsets[:, a // 16 : b // 16]), dx[k, a][:])
             nc.sync.dma_start(out_rows[:, r, :], windows[r][:])
             if k < LANES - 1:
                 nc.scalar.copy(out_lanes[:, :, r], windows[r][:])
             if k == 0:
-                dxs.append(empty(LANES - 1))
+                empty(LANES - 1, N - LATE, N, dx_banks[LANES - 1], "dx_ring")
 
         last = LANE_ORDER[-1]
         out_sc = tile("out_sc", [P, T], U8)
         out_words = out_1[0].rearrange("p n t -> p (n t)").bitcast(I32)
         width = T // CHUNKS
-        for a in range(0, SPLIT, width):
-            nc.vector.tensor_copy(out_lanes[:, a : a + width, last], windows[last][:, a : a + width])
-        for a in range(SPLIT, T, width):
-            nc.scalar.copy(out_lanes[:, a : a + width, last], windows[last][:, a : a + width])
+        codes = tile("out_codes", [P, T], I32)
+        for a, b in ((0, width), (width, 2 * width), (2 * width, SPLIT)):
+            nc.vector.tensor_copy(out_lanes[:, a:b, last], windows[last][:, a:b])
+        for a, b in ((SPLIT, 3 * width), (3 * width, T)):
+            nc.scalar.copy(out_lanes[:, a:b, last], windows[last][:, a:b])
         for c in range(CHUNKS):
             cols = slice(c * width, (c + 1) * width)
-            codes = tile(f"out_codes{c}", [P, width], I32)
             nc.vector.quantize_mx(
-                out=codes[:].bitcast(E4M3), scales=out_sc[:, cols], in_=out_lanes[:, cols, :].rearrange("p t r -> p (t r)")
+                out=codes[:, cols].bitcast(E4M3),
+                scales=out_sc[:, cols],
+                in_=out_lanes[:, cols, :].rearrange("p t r -> p (t r)"),
             )
-            nc.sync.dma_start(out_words[:, cols], codes[:])
+            if c > 0:
+                stored = slice(0 if c == 1 else c * width, (c + 1) * width)
+                nc.sync.dma_start(out_words[:, stored], codes[:, stored])
         queues = (nc.scalar, nc.sync, nc.scalar, nc.sync)
         for q in range(QUADS):
             queues[q].dma_start(out_2[0, 4 * q : 4 * q + 4, :].bitcast(I32), out_sc[32 * q : 32 * q + 4, :].bitcast(I32))

@@ -53,7 +53,10 @@ def tile_attend_gml_pl_sq_kernel(
         x_rows = xT.rearrange("(p r) t -> p r t", r=LANES)
         x_planes = [tile(f"x{r}", [P, T], F32) for r in range(LANES)]
         wd_all = wd_words[0].rearrange("p n t -> p (n t)").bitcast(I32)
-        wd_raw = [tile(f"wd_raw{o}", [P, 512], I32) for o in range(PASSES)]
+        wd_raw = [
+            tile("wd_raw0", [P, 512], I32),
+            keep.tile([P, 512], I32, name="wd_raw1", tag="wd_then_wv_sc", align_bytes=64),
+        ]
         nc.sync.dma_start(x_planes[0][:], x_rows[:, 0, :])
         for q in range(QUADS):
             nc.sync.dma_start(
@@ -74,7 +77,7 @@ def tile_attend_gml_pl_sq_kernel(
         for o, u in ((0, 0), (0, 1), (1, 0), (1, 1)):
             nc.sync.dma_start(y_pairs[o][u][:], y_rows[o, :, 2 * N * u : 2 * N * (u + 1)])
         for q in range(QUADS):
-            nc.sync.dma_start(
+            nc.gpsimd.dma_start(
                 wv_sc_raw[32 * q : 32 * q + 4, :].bitcast(I32).rearrange("f (o w) -> f o w", o=PASSES),
                 wv_scales[:, 4 * q : 4 * q + 4, :].bitcast(I32).rearrange("o f w -> f o w"),
             )
@@ -84,12 +87,15 @@ def tile_attend_gml_pl_sq_kernel(
 
         windows = [tile(f"window{r}", [P, T], F32) for r in range(LANES)]
         for r in range(LANES):
-            nc.gpsimd.memset(windows[r][:], 0.0)
+            nc.vector.memset(windows[r][:], 0.0)
 
         def deal(engine, dst, src):
             engine.tensor_copy(
                 dst.rearrange("p (r c i) -> p c r i", r=LANES, i=2), src.rearrange("p (c i r) -> p c r i", r=LANES, i=2)
             )
+
+        def deal_rows(dst, src):
+            nc.gpsimd.tensor_copy(dst.rearrange("p (r s) -> p r s", r=LANES), src.rearrange("p (s r) -> p r s", r=LANES))
 
         def deal_bytes(engine, dst, src):
             engine.tensor_copy(
@@ -119,12 +125,12 @@ def tile_attend_gml_pl_sq_kernel(
                 picked[1][:, 1, h * HALF : (h + 1) * HALF],
                 x_planes[3][:].indirect(offsets[:, h * HALF // 16 : (h + 1) * HALF // 16]),
             )
+        wd_codes = [tile("wd_codes0", [P, V // PASSES], I32)]
+        deal(nc.vector, wd_codes[0][:], wd_raw[0][:])
         nc.scalar.copy(x_lanes[:, :, 0:2], picked[0][:].rearrange("p e i -> p i e"))
         nc.scalar.copy(x_lanes[:, :HALF, 2:4], picked[1][:, :, :HALF].rearrange("p e i -> p i e"))
         nc.vector.tensor_copy(x_lanes[:, HALF:, 2:4], picked[1][:, :, HALF:].rearrange("p e i -> p i e"))
 
-        wd_codes = [tile("wd_codes0", [P, V // PASSES], I32)]
-        deal(nc.gpsimd, wd_codes[0][:], wd_raw[0][:])
         x_codes = tile("x_codes", [P, N], U32)
         x_sc = tile("x_sc", [P, N], U8)
         for h in range(2):
@@ -133,7 +139,7 @@ def tile_attend_gml_pl_sq_kernel(
                 out=x_codes[:, cols].bitcast(E4M3), scales=x_sc[:, cols], in_=x_lanes[:, cols, :].rearrange("p i r -> p (i r)")
             )
         wd_codes.append(keep.tile([P, V // PASSES], I32, name="wd_codes1", tag="x_then_wd", align_bytes=64))
-        deal(nc.gpsimd, wd_codes[1][:], wd_raw[1][:])
+        deal_rows(wd_codes[1][:], wd_raw[1][:])
 
         g_codes = [tile(f"g_codes{o}", [P, N], U32) for o in range(PASSES)]
         g_sc = [tile(f"g_sc{o}", [P, N], U8) for o in range(PASSES)]
@@ -215,11 +221,11 @@ def tile_attend_gml_pl_sq_kernel(
                     g_lanes[0][:, h * HALF : (h + 1) * HALF, :].rearrange("p i r -> p (i r)").bitcast(F32).rearrange("p (i u) -> p i u", u=2),
                     word_banks[h].rearrange("p u i -> p i u"),
                 )
-        wv_sc = tile("wv_sc", [P, PASSES * D], U8)
+        wv_sc = keep.tile([P, PASSES * D], U8, name="wv_sc", tag="wd_then_wv_sc", align_bytes=64)
         deal_bytes(nc.gpsimd, wv_sc[:], wv_sc_raw[:])
         wv_codes = tile("wv_codes", [P, PASSES, D], I32)
         for o in (1, 0):
-            deal(nc.gpsimd, wv_codes[:, o, :], wv_raw[:, o, :])
+            deal_rows(wv_codes[:, o, :], wv_raw[:, o, :])
 
         def back(bank, r):
             for o in (1, 0):

@@ -57,25 +57,35 @@ def tile_attend_gml_pl_sq_kernel(
             tile("wd_raw0", [P, 512], I32),
             keep.tile([P, 512], I32, name="wd_raw1", tag="wd_then_wv_sc", align_bytes=64),
         ]
+        rw_cols = tile("rw_cols", [P, BLOCKS], F32)
+        cw_cols = [tile(f"cw_cols{o}", [P, LANES], F32) for o in range(PASSES)]
+        y_pairs = [
+            [keep.tile([P, 2, N], F32, name=f"y{o}{u}", tag=f"y{o}{u}_reused", align_bytes=64) for u in range(2)]
+            for o in range(PASSES)
+        ]
+        y_rows = [y[:512].rearrange("(r p) i -> p r i", p=P), y[512:].rearrange("(p r) i -> p r i", r=LANES)]
+
+        def load_y(o, u):
+            nc.sync.dma_start(y_pairs[o][u][:], y_rows[o][:, 2 * u : 2 * u + 2, :])
+
         nc.sync.dma_start(x_planes[0][:], x_rows[:, 0, :])
+        nc.sync.dma_start(offsets[:], offs)
+        for r in range(1, LANES - 1):
+            nc.sync.dma_start(x_planes[r][:], x_rows[:, r, :])
+        nc.sync.dma_start(rw_cols[:], rw[0].rearrange("(c p) -> p c", p=P))
+        nc.sync.dma_start(x_planes[LANES - 1][:], x_rows[:, LANES - 1, :])
+        nc.sync.dma_start(cw_cols[0][:], cw[:512].rearrange("(r p) one -> p (r one)", p=P))
+        nc.sync.dma_start(wd_raw[0][:], wd_all[:, :512])
         for q in range(QUADS):
             nc.sync.dma_start(
                 wd_sc_raw[32 * q : 32 * q + 4, :].bitcast(I32), wd_scales[0, 4 * q : 4 * q + 4, :].bitcast(I32)
             )
-        nc.sync.dma_start(offsets[:], offs)
-        nc.sync.dma_start(x_planes[1][:], x_rows[:, 1, :])
-        nc.sync.dma_start(x_planes[2][:], x_rows[:, 2, :])
-        nc.sync.dma_start(x_planes[3][:], x_rows[:, 3, :])
-        nc.sync.dma_start(wd_raw[0][:], wd_all[:, :512])
-        rw_cols = tile("rw_cols", [P, BLOCKS], F32)
-        nc.sync.dma_start(rw_cols[:], rw[0].rearrange("(c p) -> p c", p=P))
-        cw_cols = tile("cw_cols", [P, PASSES, LANES], F32)
-        nc.sync.dma_start(cw_cols[:], cw.rearrange("(o p r) one -> p o (r one)", p=P, r=LANES))
+        load_y(0, 0)
         nc.sync.dma_start(wd_raw[1][:], wd_all[:, 512:])
-        y_rows = y.rearrange("(o p r) i -> o p (r i)", p=P, r=LANES)
-        y_pairs = [[tile(f"y{o}{u}", [P, 2 * N], F32) for u in range(2)] for o in range(PASSES)]
-        for o, u in ((0, 0), (0, 1), (1, 0), (1, 1)):
-            nc.sync.dma_start(y_pairs[o][u][:], y_rows[o, :, 2 * N * u : 2 * N * (u + 1)])
+        load_y(0, 1)
+        nc.sync.dma_start(cw_cols[1][:], cw[512:].rearrange("(p r) one -> p (r one)", r=LANES))
+        load_y(1, 0)
+        load_y(1, 1)
         for q in range(QUADS):
             nc.gpsimd.dma_start(
                 wv_sc_raw[32 * q : 32 * q + 4, :].bitcast(I32).rearrange("f (o w) -> f o w", o=PASSES),
@@ -102,8 +112,6 @@ def tile_attend_gml_pl_sq_kernel(
                 dst.rearrange("p (o r s) -> p o r s", r=LANES, s=P), src.rearrange("p (o s r) -> p o r s", r=LANES, s=P)
             )
 
-        wd_sc = tile("wd_sc", [P, V], U8)
-        deal_bytes(nc.vector, wd_sc[:], wd_sc_raw[:])
 
         banks = [psum_keep.tile([P, N], F32, name=f"bank{b}") for b in range(7)]
         turn_banks = [banks[b] for b in (1, 2, 3, 4)]
@@ -114,7 +122,9 @@ def tile_attend_gml_pl_sq_kernel(
             nc.tensor.transpose(rw_bank[:, c * P : (c + 1) * P], rw_cols[:, c : c + 1].to_broadcast([P, P]), identity[:])
 
         picked = [tile(f"picked{u}", [P, 2, N], BF16) for u in range(2)]
-        x_lanes = keep.tile([P, N, LANES], BF16, name="x_lanes", tag="x_then_wd", align_bytes=64)
+        x_lanes = [
+            keep.tile([P, HALF, LANES], BF16, name=f"x_lanes{h}", tag=f"x_then_wd{h}", align_bytes=64) for h in range(2)
+        ]
         x_first = tile("x_first", [P, T], BF16)
         nc.scalar.copy(x_first[:], x_planes[0][:])
         nc.scalar.activation(picked[0][:, 0, :], x_first[:].indirect(offsets[:]), COPY)
@@ -125,35 +135,41 @@ def tile_attend_gml_pl_sq_kernel(
                 picked[1][:, 1, h * HALF : (h + 1) * HALF],
                 x_planes[3][:].indirect(offsets[:, h * HALF // 16 : (h + 1) * HALF // 16]),
             )
-        wd_codes = [tile("wd_codes0", [P, V // PASSES], I32)]
-        deal(nc.vector, wd_codes[0][:], wd_raw[0][:])
-        nc.scalar.copy(x_lanes[:, :, 0:2], picked[0][:].rearrange("p e i -> p i e"))
-        nc.scalar.copy(x_lanes[:, :HALF, 2:4], picked[1][:, :, :HALF].rearrange("p e i -> p i e"))
-        nc.vector.tensor_copy(x_lanes[:, HALF:, 2:4], picked[1][:, :, HALF:].rearrange("p e i -> p i e"))
+        for h in range(2):
+            nc.scalar.copy(x_lanes[h][:, :, 0:2], picked[0][:, :, h * HALF : (h + 1) * HALF].rearrange("p e i -> p i e"))
+        nc.scalar.copy(x_lanes[0][:, :, 2:4], picked[1][:, :, :HALF].rearrange("p e i -> p i e"))
+        nc.vector.tensor_copy(x_lanes[1][:, :, 2:4], picked[1][:, :, HALF:].rearrange("p e i -> p i e"))
 
         x_codes = tile("x_codes", [P, N], U32)
         x_sc = tile("x_sc", [P, N], U8)
         for h in range(2):
             cols = slice(h * HALF, (h + 1) * HALF)
             nc.vector.quantize_mx(
-                out=x_codes[:, cols].bitcast(E4M3), scales=x_sc[:, cols], in_=x_lanes[:, cols, :].rearrange("p i r -> p (i r)")
+                out=x_codes[:, cols].bitcast(E4M3), scales=x_sc[:, cols], in_=x_lanes[h][:].rearrange("p i r -> p (i r)")
             )
-        wd_codes.append(keep.tile([P, V // PASSES], I32, name="wd_codes1", tag="x_then_wd", align_bytes=64))
-        deal_rows(wd_codes[1][:], wd_raw[1][:])
+        wd_dealt = keep.tile([P, 512], I32, name="wd_dealt", tag="x_then_wd1", align_bytes=64)
+        deal(nc.vector, wd_dealt[:], wd_raw[1][:])
+        wd_sc_dealt = keep.tile([P, 512], U8, name="wd_sc_dealt", tag="x_then_wd0", align_bytes=64)
+        deal_bytes(nc.vector, wd_sc_dealt[:], wd_sc_raw[:, 512:])
+        wd_codes = [wd_raw[0], wd_dealt]
+        wd_sc = [wd_sc_raw, wd_sc_dealt]
 
         g_codes = [tile(f"g_codes{o}", [P, N], U32) for o in range(PASSES)]
         g_sc = [tile(f"g_sc{o}", [P, N], U8) for o in range(PASSES)]
         for o in range(PASSES):
             nc.gpsimd.memset(g_codes[o][:, HALF:], 0)
             nc.gpsimd.memset(g_sc[o][:, HALF:].bitcast(U32), 0)
-        g_lanes = [tile(f"g_lanes{o}", [P, N, LANES], BF16) for o in range(PASSES)]
+        g_lanes = {
+            (o, h): keep.tile([P, HALF, LANES], BF16, name=f"g_lanes{o}{h}", tag=f"g_lanes{o}{h}", align_bytes=64)
+            for o, h in ((0, 0), (0, 1), (1, 0))
+        }
         resid = [tile(f"resid{o}", [P, LANES, N], F32) for o in range(PASSES)]
 
         def scores(out, o, r, a, b):
             nc.tensor.matmul_mx(
                 out=out,
                 lhsT=wd_codes[o][:, r * P : (r + 1) * P].bitcast(E4M3),
-                lhsT_scale=wd_sc[:, (o * LANES + r) * P : (o * LANES + r + 1) * P],
+                lhsT_scale=wd_sc[o][:, r * P : (r + 1) * P],
                 rhs=x_codes[:, a:b].bitcast(E4M3),
                 rhs_scale=x_sc[:, a:b],
                 start=True,
@@ -161,30 +177,30 @@ def tile_attend_gml_pl_sq_kernel(
             )
 
         def y_plane(o, r):
-            return y_pairs[o][r // 2][:, (r % 2) * N : (r % 2 + 1) * N]
+            return y_pairs[o][r // 2][:, r % 2, :]
 
         def quantise_g(o, h):
             cols = slice(h * HALF, (h + 1) * HALF)
             nc.vector.quantize_mx(
                 out=g_codes[o][:, cols].bitcast(E5M2),
                 scales=g_sc[o][:, cols],
-                in_=g_lanes[o][:, cols, :].rearrange("p i r -> p (i r)"),
+                in_=g_lanes[o, h][:].rearrange("p i r -> p (i r)"),
             )
 
         def scale_y(o, r):
             ycw = tile(f"ycw{o}{r}", [P, N], F32)
-            nc.scalar.activation(ycw[:], y_plane(o, r), COPY, scale=cw_cols[:, o, r : r + 1])
+            nc.scalar.activation(ycw[:], y_plane(o, r), COPY, scale=cw_cols[o][:, r : r + 1])
             return ycw
 
         def residual(sums, ycw, o, r, a, b):
             nc.vector.scalar_tensor_tensor(
-                resid[o][:, r, a:b], sums, cw_cols[:, o, r : r + 1], ycw[:, a:b], MULT, SUBTRACT
+                resid[o][:, r, a:b], sums, cw_cols[o][:, r : r + 1], ycw[:, a:b], MULT, SUBTRACT
             )
 
         def weigh(o, a, b):
             pairs = rw_bank[:, a:b].rearrange("p (c i) -> p c i", i=2)
             nc.vector.tensor_tensor(
-                g_lanes[o][:, a:b, :].rearrange("p (c i) r -> p c r i", i=2),
+                g_lanes[o, a // HALF][:].rearrange("p (c i) r -> p c r i", i=2),
                 resid[o][:, :, a:b].rearrange("p r (c i) -> p c r i", i=2),
                 pairs.unsqueeze(2).to_broadcast([P, (b - a) // 2, LANES, 2]),
                 MULT,
@@ -205,9 +221,11 @@ def tile_attend_gml_pl_sq_kernel(
             bank = turn_banks[c]
             for r in range(LANES):
                 nc.tensor.transpose(bank[:, r * P : (r + 1) * P], resid[0][:, r, c * P : (c + 1) * P], identity[:])
-            turned = tile(f"turned{c}", [P, 2, P, 2], BF16)
+            turned = keep.tile(
+                [P, 2, P, 2], BF16, name=f"turned{c}", tag="y11_reused" if c == 0 else f"turned{c}", align_bytes=64
+            )
             nc.scalar.activation(
-                turned[:], bank[:].rearrange("i (u e p) -> i u p e", u=2, e=2), COPY, scale=rw_cols[:, c : c + 1]
+                turned[:], bank[:].rearrange("i (p u e) -> i u p e", u=2, e=2), COPY, scale=rw_cols[:, c : c + 1]
             )
             h, j = divmod(c, 2)
             for u in range(2):
@@ -218,7 +236,7 @@ def tile_attend_gml_pl_sq_kernel(
                 )
             if j == 1:
                 nc.scalar.copy(
-                    g_lanes[0][:, h * HALF : (h + 1) * HALF, :].rearrange("p i r -> p (i r)").bitcast(F32).rearrange("p (i u) -> p i u", u=2),
+                    g_lanes[0, h][:].rearrange("p i r -> p (i r)").bitcast(F32).rearrange("p (i u) -> p i u", u=2),
                     word_banks[h].rearrange("p u i -> p i u"),
                 )
         wv_sc = keep.tile([P, PASSES * D], U8, name="wv_sc", tag="wd_then_wv_sc", align_bytes=64)
@@ -243,6 +261,7 @@ def tile_attend_gml_pl_sq_kernel(
         quantise_g(1, 0)
         quantise_g(0, 0)
         back(banks[0], LANE_ORDER[0])
+        g_lanes[1, 1] = keep.tile([P, HALF, LANES], BF16, name="g_lanes11", tag="g_lanes00", align_bytes=64)
         weigh(1, HALF, N)
         quantise_g(1, 1)
         quantise_g(0, 1)

@@ -23,7 +23,7 @@ LANES = 4
 PASSES = V // (P * LANES)
 QUADS = 4
 CHUNKS = 4
-SPLIT = 576
+SPLIT = 512
 LATE = 128
 BLOCKS = N // P
 HALF = N // 2
@@ -69,17 +69,16 @@ def tile_attend_gml_pl_sq_kernel(
             nc.sync.dma_start(y_pairs[o][u][:], y_rows[o][:, 2 * u : 2 * u + 2, :])
 
         nc.sync.dma_start(x_planes[0][:], x_rows[:, 0, :])
-        nc.sync.dma_start(offsets[:], offs)
-        for r in range(1, LANES - 1):
-            nc.sync.dma_start(x_planes[r][:], x_rows[:, r, :])
-        nc.sync.dma_start(rw_cols[:], rw[0].rearrange("(c p) -> p c", p=P))
-        nc.sync.dma_start(x_planes[LANES - 1][:], x_rows[:, LANES - 1, :])
-        nc.sync.dma_start(cw_cols[0][:], cw[:512].rearrange("(r p) one -> p (r one)", p=P))
-        nc.sync.dma_start(wd_raw[0][:], wd_all[:, :512])
         for q in range(QUADS):
             nc.sync.dma_start(
                 wd_sc_raw[32 * q : 32 * q + 4, :].bitcast(I32), wd_scales[0, 4 * q : 4 * q + 4, :].bitcast(I32)
             )
+        nc.sync.dma_start(offsets[:], offs)
+        for r in range(1, LANES):
+            nc.sync.dma_start(x_planes[r][:], x_rows[:, r, :])
+        nc.sync.dma_start(wd_raw[0][:], wd_all[:, :512])
+        nc.sync.dma_start(rw_cols[:], rw[0].rearrange("(c p) -> p c", p=P))
+        nc.sync.dma_start(cw_cols[0][:], cw[:512].rearrange("(r p) one -> p (r one)", p=P))
         load_y(0, 0)
         nc.sync.dma_start(wd_raw[1][:], wd_all[:, 512:])
         load_y(0, 1)
@@ -114,9 +113,9 @@ def tile_attend_gml_pl_sq_kernel(
 
 
         banks = [psum_keep.tile([P, N], F32, name=f"bank{b}") for b in range(7)]
-        turn_banks = [banks[b] for b in (1, 2, 3, 4)]
-        word_banks = [bank[:].rearrange("p (u i) -> p u i", u=2) for bank in banks[1:3]]
-        dx_banks = banks[3:7]
+        turn_banks = [banks[b] for b in (3, 2, 4, 5)]
+        early_bank = banks[6]
+        dx_banks = [banks[b] for b in (4, 5, 0, 1)]
         rw_bank = psum_keep.tile([P, N], F32, name="rw_bank")
         for c in range(BLOCKS):
             nc.tensor.transpose(rw_bank[:, c * P : (c + 1) * P], rw_cols[:, c : c + 1].to_broadcast([P, P]), identity[:])
@@ -154,7 +153,10 @@ def tile_attend_gml_pl_sq_kernel(
         wd_codes = [wd_raw[0], wd_dealt]
         wd_sc = [wd_sc_raw, wd_sc_dealt]
 
-        g_codes = [tile(f"g_codes{o}", [P, N], U32) for o in range(PASSES)]
+        g_codes = [
+            tile("g_codes0", [P, N], U32),
+            keep.tile([P, N], U32, name="g_codes1", tag="g_then_out", align_bytes=64),
+        ]
         g_sc = [tile(f"g_sc{o}", [P, N], U8) for o in range(PASSES)]
         for o in range(PASSES):
             nc.gpsimd.memset(g_codes[o][:, HALF:], 0)
@@ -187,9 +189,9 @@ def tile_attend_gml_pl_sq_kernel(
                 in_=g_lanes[o, h][:].rearrange("p i r -> p (i r)"),
             )
 
-        def scale_y(o, r):
+        def scale_y(o, r, factor):
             ycw = tile(f"ycw{o}{r}", [P, N], F32)
-            nc.scalar.activation(ycw[:], y_plane(o, r), COPY, scale=cw_cols[o][:, r : r + 1])
+            nc.scalar.activation(ycw[:], y_plane(o, r), COPY, scale=factor)
             return ycw
 
         def residual(sums, ycw, o, r, a, b):
@@ -206,21 +208,33 @@ def tile_attend_gml_pl_sq_kernel(
                 MULT,
             )
 
-        early = [scale_y(0, r) for r in range(2)]
+        minus_cw = tile("minus_cw", [P, 1], F32)
+        nc.scalar.activation(minus_cw[:], cw_cols[0][:, 0:1], COPY, scale=-1.0)
+        early = scale_y(0, 1, cw_cols[0][:, 1:2])
         for h in range(2):
-            for r in range(2):
-                scores(banks[h][:, r * HALF : (r + 1) * HALF], 0, r, h * HALF, (h + 1) * HALF)
-            for r in range(2):
-                residual(banks[h][:, r * HALF : (r + 1) * HALF], early[r], 0, r, h * HALF, (h + 1) * HALF)
-        for plane in range(2, PASSES * LANES):
-            o, r = divmod(plane, LANES)
-            bank = banks[plane % len(banks)]
-            scores(bank[:], o, r, 0, N)
-            residual(bank[:], scale_y(o, r), o, r, 0, N)
+            scores(banks[h][:, :HALF], 0, 1, h * HALF, (h + 1) * HALF)
+            residual(banks[h][:, :HALF], early, 0, 1, h * HALF, (h + 1) * HALF)
+        minus_ycw = scale_y(0, 0, minus_cw[:])
+        for o, r, b in ((0, 2, 3), (0, 3, 4), (1, 0, 5), (1, 1, 6), (1, 2, 0), (1, 3, 1)):
+            scores(banks[b][:], o, r, 0, N)
+            residual(banks[b][:], scale_y(o, r, cw_cols[o][:, r : r + 1]), o, r, 0, N)
+            if (o, r) == (0, 2):
+                scores(banks[2][:], 0, 0, 0, N)
+            if (o, r) == (0, 3):
+                acw = keep.tile([P, N], F32, name="acw", tag="y01_reused", align_bytes=64)
+                nc.scalar.activation(acw[:], banks[2][:], COPY, scale=cw_cols[0][:, 0:1])
         for c in range(BLOCKS):
             bank = turn_banks[c]
-            for r in range(LANES):
-                nc.tensor.transpose(bank[:, r * P : (r + 1) * P], resid[0][:, r, c * P : (c + 1) * P], identity[:])
+            for r in (1, 2, 3, 0):
+                block = bank[:, r * P : (r + 1) * P]
+                if r == 0:
+                    nc.tensor.matmul(
+                        block, minus_ycw[:, c * P : (c + 1) * P], identity[:], start=True, stop=False, is_transpose=True
+                    )
+                plane = acw[:] if r == 0 else resid[0][:, r, :]
+                nc.tensor.matmul(
+                    block, plane[:, c * P : (c + 1) * P], identity[:], start=r > 0, stop=True, is_transpose=True
+                )
             turned = keep.tile(
                 [P, 2, P, 2], BF16, name=f"turned{c}", tag="y11_reused" if c == 0 else f"turned{c}", align_bytes=64
             )
@@ -230,47 +244,46 @@ def tile_attend_gml_pl_sq_kernel(
             h, j = divmod(c, 2)
             for u in range(2):
                 nc.tensor.transpose(
-                    word_banks[h][:, u, j * P : (j + 1) * P],
+                    bank[:, u * P : (u + 1) * P],
                     turned[:, u, :, :].rearrange("i p e -> i (p e)").bitcast(F32),
                     identity[:],
                 )
-            if j == 1:
-                nc.scalar.copy(
-                    g_lanes[0, h][:].rearrange("p i r -> p (i r)").bitcast(F32).rearrange("p (i u) -> p i u", u=2),
-                    word_banks[h].rearrange("p u i -> p i u"),
-                )
+            nc.scalar.copy(
+                g_lanes[0, h][:, j * P : (j + 1) * P, :].rearrange("p i r -> p (i r)").bitcast(F32).rearrange("p (i u) -> p i u", u=2),
+                bank[:, : 2 * P].rearrange("p (u i) -> p i u", u=2),
+            )
         wv_sc = keep.tile([P, PASSES * D], U8, name="wv_sc", tag="wd_then_wv_sc", align_bytes=64)
         deal_bytes(nc.gpsimd, wv_sc[:], wv_sc_raw[:])
         wv_codes = tile("wv_codes", [P, PASSES, D], I32)
         for o in (1, 0):
             deal_rows(wv_codes[:, o, :], wv_raw[:, o, :])
 
-        def back(bank, r):
-            for o in (1, 0):
+        def back(bank, r, order):
+            for o in order:
                 nc.tensor.matmul_mx(
                     out=bank[:],
                     lhsT=wv_codes[:, o, r * P : (r + 1) * P].bitcast(E4M3),
                     lhsT_scale=wv_sc[:, o * D + r * P : o * D + (r + 1) * P],
                     rhs=g_codes[o][:].bitcast(E5M2),
                     rhs_scale=g_sc[o][:],
-                    start=o == 1,
-                    stop=o == 0,
+                    start=o == order[0],
+                    stop=o == order[1],
                 )
 
         weigh(1, 0, HALF)
         quantise_g(1, 0)
         quantise_g(0, 0)
-        back(banks[0], LANE_ORDER[0])
+        back(early_bank, LANE_ORDER[0], (1, 0))
         g_lanes[1, 1] = keep.tile([P, HALF, LANES], BF16, name="g_lanes11", tag="g_lanes00", align_bytes=64)
         weigh(1, HALF, N)
         quantise_g(1, 1)
         quantise_g(0, 1)
 
         out_rows = out_0.rearrange("(p r) t -> p r t", r=LANES)
-        out_lanes = tile("out_lanes", [P, T, LANES], BF16)
+        out_lanes = keep.tile([P, T, LANES], BF16, name="out_lanes", tag="g_then_out", align_bytes=64)
 
         for k, r in enumerate(LANE_ORDER):
-            back(dx_banks[k], r)
+            back(dx_banks[k], r, (1, 0) if k == 0 else (0, 1))
         pieces = [[(0, HALF), (HALF, N)], [(0, N)], [(0, N)], [(0, N - LATE), (N - LATE, N)]]
         dx = {}
 
@@ -278,7 +291,7 @@ def tile_attend_gml_pl_sq_kernel(
             dx[k, a] = keep.tile([P, b - a], F32, name=f"dx{k}_{a}", tag=tag, align_bytes=64)
             nc.scalar.copy(dx[k, a][:], bank[:, a:b])
 
-        empty(0, 0, HALF, banks[0], "dx_first")
+        empty(0, 0, HALF, early_bank, "dx_first")
         empty(0, HALF, N, dx_banks[0], "dx_ring")
         for k in range(1, LANES):
             a, b = pieces[k][0]
@@ -297,7 +310,7 @@ def tile_attend_gml_pl_sq_kernel(
         out_words = out_1[0].rearrange("p n t -> p (n t)").bitcast(I32)
         width = T // CHUNKS
         codes = tile("out_codes", [P, T], I32)
-        for a, b in ((0, width), (width, 2 * width), (2 * width, SPLIT)):
+        for a, b in ((0, width), (width, SPLIT)):
             nc.vector.tensor_copy(out_lanes[:, a:b, last], windows[last][:, a:b])
         for a, b in ((SPLIT, 3 * width), (3 * width, T)):
             nc.scalar.copy(out_lanes[:, a:b, last], windows[last][:, a:b])

@@ -45,6 +45,8 @@ def tile_attend_gml_pl_sq_kernel(
 
         wd_sc_raw = tile("wd_sc_raw", [P, V], U8)
         wv_sc_raw = tile("wv_sc_raw", [P, PASSES * D], U8)
+        factor_rows = tile("factor_rows", [P, P], F32)
+        nc.gpsimd.memset(factor_rows[:], 0.0)
         nc.gpsimd.memset(wd_sc_raw[:].bitcast(I32), 0)
         nc.gpsimd.memset(wv_sc_raw[:].bitcast(I32), 0)
         identity = tile("identity", [P, P], F32)
@@ -57,8 +59,10 @@ def tile_attend_gml_pl_sq_kernel(
             tile("wd_raw0", [P, 512], I32),
             keep.tile([P, 512], I32, name="wd_raw1", tag="wd_then_wv_sc", align_bytes=64),
         ]
-        rw_cols = tile("rw_cols", [P, BLOCKS], F32)
-        cw_cols = [tile(f"cw_cols{o}", [P, LANES], F32) for o in range(PASSES)]
+        factor_cols = tile("factor_cols", [P, LANES + BLOCKS], F32)
+        rw_cols = factor_cols[:, LANES:]
+        cw_dealt = tile("cw_dealt", [P, LANES], F32)
+        cw_cols = [factor_cols[:, :LANES], cw_dealt[:]]
         y_pairs = [
             [keep.tile([P, 2, N], F32, name=f"y{o}{u}", tag=f"y{o}{u}_reused", align_bytes=64) for u in range(2)]
             for o in range(PASSES)
@@ -68,25 +72,30 @@ def tile_attend_gml_pl_sq_kernel(
         def load_y(o, u):
             nc.sync.dma_start(y_pairs[o][u][:], y_rows[o][:, 2 * u : 2 * u + 2, :])
 
-        nc.sync.dma_start(x_planes[0][:], x_rows[:, 0, :])
-        for q in range(QUADS):
+        def load_wd_scales(q):
             nc.sync.dma_start(
                 wd_sc_raw[32 * q : 32 * q + 4, :].bitcast(I32), wd_scales[0, 4 * q : 4 * q + 4, :].bitcast(I32)
             )
+
         nc.sync.dma_start(offsets[:], offs)
-        for r in range(1, LANES):
+        for r in range(LANES - 1):
             nc.sync.dma_start(x_planes[r][:], x_rows[:, r, :])
+        nc.sync.dma_start(factor_rows[:LANES, :], cw[:512].rearrange("(r p) one -> r (p one)", p=P))
+        nc.sync.dma_start(factor_rows[LANES : LANES + BLOCKS, :], rw[0].rearrange("(c p) -> c p", p=P))
+        load_wd_scales(0)
+        load_wd_scales(1)
+        nc.sync.dma_start(x_planes[LANES - 1][:], x_rows[:, LANES - 1, :])
+        load_wd_scales(2)
+        load_wd_scales(3)
         nc.sync.dma_start(wd_raw[0][:], wd_all[:, :512])
-        nc.sync.dma_start(rw_cols[:], rw[0].rearrange("(c p) -> p c", p=P))
-        nc.sync.dma_start(cw_cols[0][:], cw[:512].rearrange("(r p) one -> p (r one)", p=P))
         load_y(0, 0)
         nc.sync.dma_start(wd_raw[1][:], wd_all[:, 512:])
         load_y(0, 1)
-        nc.sync.dma_start(cw_cols[1][:], cw[512:].rearrange("(p r) one -> p (r one)", r=LANES))
+        nc.sync.dma_start(cw_dealt[:], cw[512:].rearrange("(p r) one -> p (r one)", r=LANES))
         load_y(1, 0)
         load_y(1, 1)
         for q in range(QUADS):
-            nc.gpsimd.dma_start(
+            nc.sync.dma_start(
                 wv_sc_raw[32 * q : 32 * q + 4, :].bitcast(I32).rearrange("f (o w) -> f o w", o=PASSES),
                 wv_scales[:, 4 * q : 4 * q + 4, :].bitcast(I32).rearrange("o f w -> f o w"),
             )
@@ -117,6 +126,8 @@ def tile_attend_gml_pl_sq_kernel(
         early_bank = banks[6]
         dx_banks = [banks[b] for b in (4, 5, 0, 1)]
         rw_bank = psum_keep.tile([P, N], F32, name="rw_bank")
+        nc.tensor.transpose(early_bank[:, :P], factor_rows[:], identity[:])
+        nc.scalar.copy(factor_cols[:], early_bank[:, : LANES + BLOCKS])
         for c in range(BLOCKS):
             nc.tensor.transpose(rw_bank[:, c * P : (c + 1) * P], rw_cols[:, c : c + 1].to_broadcast([P, P]), identity[:])
 
@@ -300,8 +311,11 @@ def tile_attend_gml_pl_sq_kernel(
             for a, b in pieces[k]:
                 nc.vector.tensor_copy(windows[r][:].indirect(offsets[:, a // 16 : b // 16]), dx[k, a][:])
             nc.sync.dma_start(out_rows[:, r, :], windows[r][:])
-            if k < LANES - 1:
+            if k == 0:
                 nc.scalar.copy(out_lanes[:, :, r], windows[r][:])
+            elif k < LANES - 1:
+                nc.scalar.copy(out_lanes[:, :SPLIT, r], windows[r][:, :SPLIT])
+                nc.gpsimd.tensor_copy(out_lanes[:, SPLIT:, r], windows[r][:, SPLIT:])
             if k == 0:
                 empty(LANES - 1, N - LATE, N, dx_banks[LANES - 1], "dx_ring")
 

@@ -57,7 +57,7 @@ def tile_attend_gml_pl_sq_kernel(
         wd_all = wd_words[0].rearrange("p n t -> p (n t)").bitcast(I32)
         wd_raw = [
             tile("wd_raw0", [P, 512], I32),
-            keep.tile([P, 512], I32, name="wd_raw1", tag="wd_then_wv_sc", align_bytes=64),
+            tile("wd_raw1", [P, 512], I32),
         ]
         factor_cols = tile("factor_cols", [P, LANES + BLOCKS], F32)
         rw_cols = factor_cols[:, LANES:]
@@ -101,7 +101,11 @@ def tile_attend_gml_pl_sq_kernel(
             )
         wv_raw = tile("wv_raw", [P, PASSES, D], I32)
         nc.sync.dma_start(wv_raw[:], wv_words.rearrange("o p n t -> p o (n t)").bitcast(I32))
-
+        rw_rows = [
+            keep.tile([P, HALF], F32, name=f"rw_rows{h}", tag=f"rw{h}_reused", align_bytes=64) for h in range(2)
+        ]
+        for h in range(2):
+            nc.sync.dma_start(rw_rows[h][:], rw[:, h * HALF : (h + 1) * HALF])
 
         windows = [tile(f"window{r}", [P, T], F32) for r in range(LANES)]
         for r in range(LANES):
@@ -112,24 +116,18 @@ def tile_attend_gml_pl_sq_kernel(
                 dst.rearrange("p (r c i) -> p c r i", r=LANES, i=2), src.rearrange("p (c i r) -> p c r i", r=LANES, i=2)
             )
 
-        def deal_rows(dst, src):
-            nc.gpsimd.tensor_copy(dst.rearrange("p (r s) -> p r s", r=LANES), src.rearrange("p (s r) -> p r s", r=LANES))
-
         def deal_bytes(engine, dst, src):
             engine.tensor_copy(
                 dst.rearrange("p (o r s) -> p o r s", r=LANES, s=P), src.rearrange("p (o s r) -> p o r s", r=LANES, s=P)
             )
 
 
-        banks = [psum_keep.tile([P, N], F32, name=f"bank{b}") for b in range(7)]
+        banks = [psum_keep.tile([P, N], F32, name=f"bank{b}") for b in range(8)]
         turn_banks = [banks[b] for b in (3, 2, 4, 5)]
-        early_bank = banks[6]
+        early_bank = banks[7]
         dx_banks = [banks[b] for b in (4, 5, 0, 1)]
-        rw_bank = psum_keep.tile([P, N], F32, name="rw_bank")
         nc.tensor.transpose(early_bank[:, :P], factor_rows[:], identity[:])
         nc.scalar.copy(factor_cols[:], early_bank[:, : LANES + BLOCKS])
-        for c in range(BLOCKS):
-            nc.tensor.transpose(rw_bank[:, c * P : (c + 1) * P], rw_cols[:, c : c + 1].to_broadcast([P, P]), identity[:])
 
         picked = [tile(f"picked{u}", [P, 2, N], BF16) for u in range(2)]
         x_lanes = [
@@ -147,8 +145,8 @@ def tile_attend_gml_pl_sq_kernel(
             )
         for h in range(2):
             nc.scalar.copy(x_lanes[h][:, :, 0:2], picked[0][:, :, h * HALF : (h + 1) * HALF].rearrange("p e i -> p i e"))
-        nc.scalar.copy(x_lanes[0][:, :, 2:4], picked[1][:, :, :HALF].rearrange("p e i -> p i e"))
-        nc.vector.tensor_copy(x_lanes[1][:, :, 2:4], picked[1][:, :, HALF:].rearrange("p e i -> p i e"))
+        nc.vector.tensor_copy(x_lanes[0][:, :, 2:4], picked[1][:, :, :HALF].rearrange("p e i -> p i e"))
+        nc.scalar.copy(x_lanes[1][:, :, 2:4], picked[1][:, :, HALF:].rearrange("p e i -> p i e"))
 
         x_codes = tile("x_codes", [P, N], U32)
         x_sc = tile("x_sc", [P, N], U8)
@@ -168,10 +166,10 @@ def tile_attend_gml_pl_sq_kernel(
             tile("g_codes0", [P, N], U32),
             keep.tile([P, N], U32, name="g_codes1", tag="g_then_out", align_bytes=64),
         ]
-        g_sc = [tile(f"g_sc{o}", [P, N], U8) for o in range(PASSES)]
+        g_sc = [None, tile("g_sc1", [P, N], U8)]
         for o in range(PASSES):
             nc.gpsimd.memset(g_codes[o][:, HALF:], 0)
-            nc.gpsimd.memset(g_sc[o][:, HALF:].bitcast(U32), 0)
+        nc.gpsimd.memset(g_sc[1][:, HALF:].bitcast(U32), 0)
         g_lanes = {
             (o, h): keep.tile([P, HALF, LANES], BF16, name=f"g_lanes{o}{h}", tag=f"g_lanes{o}{h}", align_bytes=64)
             for o, h in ((0, 0), (0, 1), (1, 0))
@@ -211,7 +209,7 @@ def tile_attend_gml_pl_sq_kernel(
             )
 
         def weigh(o, a, b):
-            pairs = rw_bank[:, a:b].rearrange("p (c i) -> p c i", i=2)
+            pairs = rw_rows[a // HALF][:].rearrange("p (c i) -> p c i", i=2)
             nc.vector.tensor_tensor(
                 g_lanes[o, a // HALF][:].rearrange("p (c i) r -> p c r i", i=2),
                 resid[o][:, :, a:b].rearrange("p r (c i) -> p c r i", i=2),
@@ -263,18 +261,22 @@ def tile_attend_gml_pl_sq_kernel(
                 g_lanes[0, h][:, j * P : (j + 1) * P, :].rearrange("p i r -> p (i r)").bitcast(F32).rearrange("p (i u) -> p i u", u=2),
                 bank[:, : 2 * P].rearrange("p (u i) -> p i u", u=2),
             )
-        wv_sc = keep.tile([P, PASSES * D], U8, name="wv_sc", tag="wd_then_wv_sc", align_bytes=64)
-        deal_bytes(nc.gpsimd, wv_sc[:], wv_sc_raw[:])
-        wv_codes = tile("wv_codes", [P, PASSES, D], I32)
-        for o in (1, 0):
-            deal_rows(wv_codes[:, o, :], wv_raw[:, o, :])
+        wv_words_by_lane = wv_raw[:].rearrange("p o (s v l) -> p l v o s", v=2, l=2)
+        wv_bytes_by_lane = wv_sc_raw[:].rearrange("p (o s v l) -> p l v o s", o=PASSES, v=2, l=2)
+        first, second = LANE_ORDER[:2]
+        even_sc = tile("even_sc", [P, 2, PASSES, P], U8)
+        nc.vector.tensor_copy(even_sc[:], wv_bytes_by_lane[:, 0, :, :, :])
+        first_codes = tile("first_codes", [P, PASSES, P], I32)
+        nc.vector.tensor_copy(first_codes[:], wv_words_by_lane[:, 0, first // 2, :, :])
+        wv_codes = {first: first_codes[:]}
+        wv_sc = {r: even_sc[:, r // 2, :, :] for r in (first, second)}
 
         def back(bank, r, order):
             for o in order:
                 nc.tensor.matmul_mx(
                     out=bank[:],
-                    lhsT=wv_codes[:, o, r * P : (r + 1) * P].bitcast(E4M3),
-                    lhsT_scale=wv_sc[:, o * D + r * P : o * D + (r + 1) * P],
+                    lhsT=wv_codes[r][:, o, :].bitcast(E4M3),
+                    lhsT_scale=wv_sc[r][:, o, :],
                     rhs=g_codes[o][:].bitcast(E5M2),
                     rhs_scale=g_sc[o][:],
                     start=o == order[0],
@@ -282,6 +284,8 @@ def tile_attend_gml_pl_sq_kernel(
                 )
 
         weigh(1, 0, HALF)
+        g_sc[0] = keep.tile([P, N], U8, name="g_sc0", tag="rw0_reused", align_bytes=64)
+        nc.vector.memset(g_sc[0][:, HALF:].bitcast(U32), 0)
         quantise_g(1, 0)
         quantise_g(0, 0)
         back(early_bank, LANE_ORDER[0], (1, 0))
@@ -291,10 +295,7 @@ def tile_attend_gml_pl_sq_kernel(
         quantise_g(0, 1)
 
         out_rows = out_0.rearrange("(p r) t -> p r t", r=LANES)
-        out_lanes = keep.tile([P, T, LANES], BF16, name="out_lanes", tag="g_then_out", align_bytes=64)
 
-        for k, r in enumerate(LANE_ORDER):
-            back(dx_banks[k], r, (1, 0) if k == 0 else (0, 1))
         pieces = [[(0, HALF), (HALF, N)], [(0, N)], [(0, N)], [(0, N - LATE), (N - LATE, N)]]
         dx = {}
 
@@ -302,14 +303,32 @@ def tile_attend_gml_pl_sq_kernel(
             dx[k, a] = keep.tile([P, b - a], F32, name=f"dx{k}_{a}", tag=tag, align_bytes=64)
             nc.scalar.copy(dx[k, a][:], bank[:, a:b])
 
+        def scatter(k, a, b):
+            nc.vector.tensor_copy(windows[LANE_ORDER[k]][:].indirect(offsets[:, a // 16 : b // 16]), dx[k, a][:])
+
         empty(0, 0, HALF, early_bank, "dx_first")
+        scatter(0, 0, HALF)
+        back(dx_banks[0], first, (1, 0))
+        later_codes = keep.tile([P, LANES - 1, PASSES, P], I32, name="later_codes", tag="g_lanes01", align_bytes=64)
+        for k in range(1, LANES):
+            r = LANE_ORDER[k]
+            nc.gpsimd.tensor_copy(later_codes[:, k - 1, :, :], wv_words_by_lane[:, r % 2, r // 2, :, :])
+            wv_codes[r] = later_codes[:, k - 1, :, :]
+        back(dx_banks[1], second, (0, 1))
+        odd_sc = keep.tile([P, 2, PASSES, P], U8, name="odd_sc", tag="dx_first", align_bytes=64)
+        nc.gpsimd.tensor_copy(odd_sc[:], wv_bytes_by_lane[:, 1, :, :, :])
+        for k in (2, 3):
+            r = LANE_ORDER[k]
+            wv_sc[r] = odd_sc[:, r // 2, :, :]
+            back(dx_banks[k], r, (0, 1))
+        out_lanes = keep.tile([P, T, LANES], BF16, name="out_lanes", tag="g_then_out", align_bytes=64)
         empty(0, HALF, N, dx_banks[0], "dx_ring")
         for k in range(1, LANES):
             a, b = pieces[k][0]
             empty(k, a, b, dx_banks[k], f"dx{k}")
         for k, r in enumerate(LANE_ORDER):
-            for a, b in pieces[k]:
-                nc.vector.tensor_copy(windows[r][:].indirect(offsets[:, a // 16 : b // 16]), dx[k, a][:])
+            for a, b in pieces[k][1 if k == 0 else 0 :]:
+                scatter(k, a, b)
             nc.sync.dma_start(out_rows[:, r, :], windows[r][:])
             if k == 0:
                 nc.scalar.copy(out_lanes[:, :, r], windows[r][:])

@@ -24,7 +24,6 @@ PASSES = V // (P * LANES)
 QUADS = 4
 CHUNKS = 4
 SPLIT = 512
-LATE = 128
 BLOCKS = N // P
 HALF = N // 2
 LANE_ORDER = (2, 0, 1, 3)
@@ -36,6 +35,7 @@ def tile_attend_gml_pl_sq_kernel(
     nc = tc.nc
     with ExitStack() as ctx:
         keep = ctx.enter_context(tc.tile_pool(name="keep", bufs=1))
+        placed = ctx.enter_context(tc.tile_pool(name="placed", bufs=1))
         psum_keep = ctx.enter_context(tc.psum_pool(name="psum_keep", bufs=1))
 
         def tile(name, shape, dtype):
@@ -44,7 +44,7 @@ def tile_attend_gml_pl_sq_kernel(
         offsets = keep.tile([P, N // 16], U16, name="offsets")
 
         wd_sc_raw = tile("wd_sc_raw", [P, V], U8)
-        wv_sc_raw = tile("wv_sc_raw", [P, PASSES * D], U8)
+        wv_sc_raw = keep.tile([P, PASSES * D], U8, name="wv_sc_raw", tag="wv_sc_reused", align_bytes=64)
         factor_rows = tile("factor_rows", [P, P], F32)
         nc.gpsimd.memset(factor_rows[:], 0.0)
         nc.gpsimd.memset(wd_sc_raw[:].bitcast(I32), 0)
@@ -77,8 +77,9 @@ def tile_attend_gml_pl_sq_kernel(
                 wd_sc_raw[32 * q : 32 * q + 4, :].bitcast(I32), wd_scales[0, 4 * q : 4 * q + 4, :].bitcast(I32)
             )
 
+        nc.sync.dma_start(x_planes[0][:], x_rows[:, 0, :])
         nc.sync.dma_start(offsets[:], offs)
-        for r in range(LANES - 1):
+        for r in range(1, LANES - 1):
             nc.sync.dma_start(x_planes[r][:], x_rows[:, r, :])
         nc.sync.dma_start(factor_rows[:LANES, :], cw[:512].rearrange("(r p) one -> r (p one)", p=P))
         nc.sync.dma_start(factor_rows[LANES : LANES + BLOCKS, :], rw[0].rearrange("(c p) -> c p", p=P))
@@ -99,16 +100,11 @@ def tile_attend_gml_pl_sq_kernel(
                 wv_sc_raw[32 * q : 32 * q + 4, :].bitcast(I32).rearrange("f (o w) -> f o w", o=PASSES),
                 wv_scales[:, 4 * q : 4 * q + 4, :].bitcast(I32).rearrange("o f w -> f o w"),
             )
-        wv_raw = tile("wv_raw", [P, PASSES, D], I32)
+        wv_raw = keep.tile([P, PASSES, D], I32, name="wv_raw", tag="wv_reused", align_bytes=64)
         nc.sync.dma_start(wv_raw[:], wv_words.rearrange("o p n t -> p o (n t)").bitcast(I32))
-        rw_rows = [
-            keep.tile([P, HALF], F32, name=f"rw_rows{h}", tag=f"rw{h}_reused", align_bytes=64) for h in range(2)
-        ]
-        for h in range(2):
-            nc.sync.dma_start(rw_rows[h][:], rw[:, h * HALF : (h + 1) * HALF])
 
-        windows = [tile(f"window{r}", [P, T], F32) for r in range(LANES)]
-        for r in range(LANES):
+        windows = {r: tile(f"window{r}", [P, T], F32) for r in LANE_ORDER[:2]}
+        for r in LANE_ORDER[:2]:
             nc.vector.memset(windows[r][:], 0.0)
 
         def deal(engine, dst, src):
@@ -122,12 +118,15 @@ def tile_attend_gml_pl_sq_kernel(
             )
 
 
-        banks = [psum_keep.tile([P, N], F32, name=f"bank{b}") for b in range(8)]
+        banks = [psum_keep.tile([P, N], F32, name=f"bank{b}") for b in range(7)]
         turn_banks = [banks[b] for b in (3, 2, 4, 5)]
-        early_bank = banks[7]
-        dx_banks = [banks[b] for b in (4, 5, 0, 1)]
-        nc.tensor.transpose(early_bank[:, :P], factor_rows[:], identity[:])
-        nc.scalar.copy(factor_cols[:], early_bank[:, : LANES + BLOCKS])
+        early_bank = banks[6]
+        dx_banks = [banks[b] for b in (0, 1, 3, 2)]
+        rw_bank = psum_keep.tile([P, N], F32, name="rw_bank")
+        nc.tensor.transpose(banks[6][:, :P], factor_rows[:], identity[:])
+        nc.scalar.copy(factor_cols[:], banks[6][:, : LANES + BLOCKS])
+        for c in range(BLOCKS):
+            nc.tensor.transpose(rw_bank[:, c * P : (c + 1) * P], rw_cols[:, c : c + 1].to_broadcast([P, P]), identity[:])
 
         picked = [tile(f"picked{u}", [P, 2, N], BF16) for u in range(2)]
         x_lanes = [
@@ -164,17 +163,18 @@ def tile_attend_gml_pl_sq_kernel(
 
         g_codes = [
             tile("g_codes0", [P, N], U32),
-            keep.tile([P, N], U32, name="g_codes1", tag="g_then_out", align_bytes=64),
+            tile("g_codes1", [P, N], U32),
         ]
-        g_sc = [None, tile("g_sc1", [P, N], U8)]
+        g_sc = [tile(f"g_sc{o}", [P, N], U8) for o in range(PASSES)]
         for o in range(PASSES):
             nc.gpsimd.memset(g_codes[o][:, HALF:], 0)
-        nc.gpsimd.memset(g_sc[1][:, HALF:].bitcast(U32), 0)
-        g_lanes = {
-            (o, h): keep.tile([P, HALF, LANES], BF16, name=f"g_lanes{o}{h}", tag=f"g_lanes{o}{h}", align_bytes=64)
-            for o, h in ((0, 0), (0, 1), (1, 0))
-        }
-        resid = [tile(f"resid{o}", [P, LANES, N], F32) for o in range(PASSES)]
+            nc.gpsimd.memset(g_sc[o][:, HALF:].bitcast(U32), 0)
+        g_lanes = {(1, 0): tile("g_lanes10", [P, HALF, LANES], BF16)}
+        g_lanes[0, 1] = tile("g_lanes01", [P, HALF, LANES], BF16)
+        g_lanes[0, 0] = placed.tile([P, HALF, LANES], BF16, name="g_lanes00", offset=12544, align_bytes=64)
+        resid = [
+            keep.tile([P, LANES, N], F32, name=f"resid{o}", tag=f"resid{o}_reused", align_bytes=64) for o in range(PASSES)
+        ]
 
         def scores(out, o, r, a, b):
             nc.tensor.matmul_mx(
@@ -199,7 +199,10 @@ def tile_attend_gml_pl_sq_kernel(
             )
 
         def scale_y(o, r, factor):
-            ycw = tile(f"ycw{o}{r}", [P, N], F32)
+            if (o, r) == (1, 3):
+                ycw = placed.tile([P, N], F32, name="ycw13", offset=0, align_bytes=64)
+            else:
+                ycw = tile(f"ycw{o}{r}", [P, N], F32)
             nc.scalar.activation(ycw[:], y_plane(o, r), COPY, scale=factor)
             return ycw
 
@@ -209,7 +212,7 @@ def tile_attend_gml_pl_sq_kernel(
             )
 
         def weigh(o, a, b):
-            pairs = rw_rows[a // HALF][:].rearrange("p (c i) -> p c i", i=2)
+            pairs = rw_bank[:, a:b].rearrange("p (c i) -> p c i", i=2)
             nc.vector.tensor_tensor(
                 g_lanes[o, a // HALF][:].rearrange("p (c i) r -> p c r i", i=2),
                 resid[o][:, :, a:b].rearrange("p r (c i) -> p c r i", i=2),
@@ -232,6 +235,7 @@ def tile_attend_gml_pl_sq_kernel(
             if (o, r) == (0, 3):
                 acw = keep.tile([P, N], F32, name="acw", tag="y01_reused", align_bytes=64)
                 nc.scalar.activation(acw[:], banks[2][:], COPY, scale=cw_cols[0][:, 0:1])
+        turned = {}
         for c in range(BLOCKS):
             bank = turn_banks[c]
             for r in (1, 2, 3, 0):
@@ -244,32 +248,34 @@ def tile_attend_gml_pl_sq_kernel(
                 nc.tensor.matmul(
                     block, plane[:, c * P : (c + 1) * P], identity[:], start=r > 0, stop=True, is_transpose=True
                 )
-            turned = keep.tile(
+            turned[c] = keep.tile(
                 [P, 2, P, 2], BF16, name=f"turned{c}", tag="y11_reused" if c == 0 else f"turned{c}", align_bytes=64
             )
             nc.scalar.activation(
-                turned[:], bank[:].rearrange("i (p u e) -> i u p e", u=2, e=2), COPY, scale=rw_cols[:, c : c + 1]
+                turned[c][:], bank[:].rearrange("i (p u e) -> i u p e", u=2, e=2), COPY, scale=rw_cols[:, c : c + 1]
             )
+            words = bank[:, :HALF]
             h, j = divmod(c, 2)
             for u in range(2):
                 nc.tensor.transpose(
-                    bank[:, u * P : (u + 1) * P],
-                    turned[:, u, :, :].rearrange("i p e -> i (p e)").bitcast(F32),
+                    words[:, u * P : (u + 1) * P],
+                    turned[c][:, u, :, :].rearrange("i p e -> i (p e)").bitcast(F32),
                     identity[:],
                 )
             nc.scalar.copy(
                 g_lanes[0, h][:, j * P : (j + 1) * P, :].rearrange("p i r -> p (i r)").bitcast(F32).rearrange("p (i u) -> p i u", u=2),
-                bank[:, : 2 * P].rearrange("p (u i) -> p i u", u=2),
+                words.rearrange("p (u i) -> p i u", u=2),
             )
-        wv_words_by_lane = wv_raw[:].rearrange("p o (s v l) -> p l v o s", v=2, l=2)
-        wv_bytes_by_lane = wv_sc_raw[:].rearrange("p (o s v l) -> p l v o s", o=PASSES, v=2, l=2)
-        first, second = LANE_ORDER[:2]
-        even_sc = tile("even_sc", [P, 2, PASSES, P], U8)
-        nc.vector.tensor_copy(even_sc[:], wv_bytes_by_lane[:, 0, :, :, :])
-        first_codes = tile("first_codes", [P, PASSES, P], I32)
-        nc.vector.tensor_copy(first_codes[:], wv_words_by_lane[:, 0, first // 2, :, :])
-        wv_codes = {first: first_codes[:]}
-        wv_sc = {r: even_sc[:, r // 2, :, :] for r in (first, second)}
+
+        wv_words_by_lane = wv_raw[:].rearrange("p o (s r) -> p r o s", r=LANES)
+        wv_bytes_by_lane = wv_sc_raw[:].rearrange("p (o s r) -> p r o s", o=PASSES, r=LANES)
+        wv_codes, wv_sc = {}, {}
+
+        def deal_lane(r, offset):
+            wv_codes[r] = placed.tile([P, PASSES, P], I32, name=f"wv_codes{r}", offset=offset, align_bytes=64)
+            nc.gpsimd.tensor_copy(wv_codes[r][:], wv_words_by_lane[:, r, :, :])
+            wv_sc[r] = placed.tile([P, PASSES, P], U8, name=f"wv_sc{r}", offset=offset + 1024, align_bytes=64)
+            nc.gpsimd.tensor_copy(wv_sc[r][:], wv_bytes_by_lane[:, r, :, :])
 
         def back(bank, r, order):
             for o in order:
@@ -283,20 +289,7 @@ def tile_attend_gml_pl_sq_kernel(
                     stop=o == order[1],
                 )
 
-        weigh(1, 0, HALF)
-        g_sc[0] = keep.tile([P, N], U8, name="g_sc0", tag="rw0_reused", align_bytes=64)
-        nc.vector.memset(g_sc[0][:, HALF:].bitcast(U32), 0)
-        quantise_g(1, 0)
-        quantise_g(0, 0)
-        back(early_bank, LANE_ORDER[0], (1, 0))
-        g_lanes[1, 1] = keep.tile([P, HALF, LANES], BF16, name="g_lanes11", tag="g_lanes00", align_bytes=64)
-        weigh(1, HALF, N)
-        quantise_g(1, 1)
-        quantise_g(0, 1)
-
         out_rows = out_0.rearrange("(p r) t -> p r t", r=LANES)
-
-        pieces = [[(0, HALF), (HALF, N)], [(0, N)], [(0, N)], [(0, N - LATE), (N - LATE, N)]]
         dx = {}
 
         def empty(k, a, b, bank, tag):
@@ -306,37 +299,48 @@ def tile_attend_gml_pl_sq_kernel(
         def scatter(k, a, b):
             nc.vector.tensor_copy(windows[LANE_ORDER[k]][:].indirect(offsets[:, a // 16 : b // 16]), dx[k, a][:])
 
+        deal_lane(LANE_ORDER[0], 0)
+        weigh(1, 0, HALF)
+        quantise_g(1, 0)
+        quantise_g(0, 0)
+        back(early_bank, LANE_ORDER[0], (1, 0))
+        g_lanes[1, 1] = placed.tile([P, HALF, LANES], BF16, name="g_lanes11", offset=12544, align_bytes=64)
+        weigh(1, HALF, N)
+        quantise_g(0, 1)
+        quantise_g(1, 1)
         empty(0, 0, HALF, early_bank, "dx_first")
         scatter(0, 0, HALF)
-        back(dx_banks[0], first, (1, 0))
-        later_codes = keep.tile([P, LANES - 1, PASSES, P], I32, name="later_codes", tag="g_lanes01", align_bytes=64)
-        for k in range(1, LANES):
-            r = LANE_ORDER[k]
-            nc.gpsimd.tensor_copy(later_codes[:, k - 1, :, :], wv_words_by_lane[:, r % 2, r // 2, :, :])
-            wv_codes[r] = later_codes[:, k - 1, :, :]
-        back(dx_banks[1], second, (0, 1))
+        back(dx_banks[0], LANE_ORDER[0], (0, 1))
+        deal_lane(LANE_ORDER[1], 12544 + 768)
+        back(dx_banks[1], LANE_ORDER[1], (0, 1))
         odd_sc = keep.tile([P, 2, PASSES, P], U8, name="odd_sc", tag="dx_first", align_bytes=64)
-        nc.gpsimd.tensor_copy(odd_sc[:], wv_bytes_by_lane[:, 1, :, :, :])
+        nc.gpsimd.tensor_copy(odd_sc[:], wv_bytes_by_lane[:, 1::2, :, :])
         for k in (2, 3):
             r = LANE_ORDER[k]
             wv_sc[r] = odd_sc[:, r // 2, :, :]
+            wv_codes[r] = placed.tile(
+                [P, PASSES, P], I32, name=f"wv_codes{r}", offset=12544 - 256 if k == 2 else 12544 + 768, align_bytes=64
+            )
+            nc.gpsimd.tensor_copy(wv_codes[r][:], wv_words_by_lane[:, r, :, :])
             back(dx_banks[k], r, (0, 1))
-        out_lanes = keep.tile([P, T, LANES], BF16, name="out_lanes", tag="g_then_out", align_bytes=64)
+        windows[LANE_ORDER[2]] = keep.tile([P, T], F32, name="window_third", tag="wv_reused", align_bytes=64)
+        nc.gpsimd.memset(windows[LANE_ORDER[2]][:], 0.0)
+        out_lanes = placed.tile([P, T, LANES], BF16, name="out_lanes", offset=12544 + 768 - 8192, align_bytes=64)
         empty(0, HALF, N, dx_banks[0], "dx_ring")
-        for k in range(1, LANES):
-            a, b = pieces[k][0]
-            empty(k, a, b, dx_banks[k], f"dx{k}")
+        empty(1, 0, N, dx_banks[1], "dx1")
+        empty(2, 0, N, dx_banks[2], "dx2")
         for k, r in enumerate(LANE_ORDER):
-            for a, b in pieces[k][1 if k == 0 else 0 :]:
-                scatter(k, a, b)
+            scatter(k, HALF if k == 0 else 0, N)
+            if k == 1:
+                windows[LANE_ORDER[3]] = keep.tile([P, T], F32, name="window_last", tag="dx1", align_bytes=64)
+                nc.gpsimd.memset(windows[LANE_ORDER[3]][:], 0.0)
             nc.sync.dma_start(out_rows[:, r, :], windows[r][:])
             if k == 0:
                 nc.scalar.copy(out_lanes[:, :, r], windows[r][:])
+                empty(LANES - 1, 0, N, dx_banks[LANES - 1], "dx_ring")
             elif k < LANES - 1:
                 nc.scalar.copy(out_lanes[:, :SPLIT, r], windows[r][:, :SPLIT])
                 nc.gpsimd.tensor_copy(out_lanes[:, SPLIT:, r], windows[r][:, SPLIT:])
-            if k == 0:
-                empty(LANES - 1, N - LATE, N, dx_banks[LANES - 1], "dx_ring")
 
         last = LANE_ORDER[-1]
         out_sc = tile("out_sc", [P, T], U8)

@@ -46,8 +46,8 @@ def tile_attend_gml_pl_sq_kernel(
         wd_sc_raw = tile("wd_sc_raw", [P, V], U8)
         wv_sc_raw = keep.tile([P, PASSES * D], U8, name="wv_sc_raw", tag="wv_sc_reused", align_bytes=64)
         factor_rows = tile("factor_rows", [P, P], F32)
-        nc.gpsimd.memset(factor_rows[:], 0.0)
         nc.gpsimd.memset(wd_sc_raw[:].bitcast(I32), 0)
+        nc.gpsimd.memset(factor_rows[:], 0.0)
         nc.gpsimd.memset(wv_sc_raw[:].bitcast(I32), 0)
         identity = tile("identity", [P, P], F32)
         make_identity(nc, identity[:])
@@ -81,20 +81,19 @@ def tile_attend_gml_pl_sq_kernel(
         nc.sync.dma_start(offsets[:], offs)
         for r in range(1, LANES - 1):
             nc.sync.dma_start(x_planes[r][:], x_rows[:, r, :])
+        for q in range(QUADS):
+            load_wd_scales(q)
+        nc.sync.dma_start(x_planes[LANES - 1][:], x_rows[:, LANES - 1, :])
         nc.sync.dma_start(factor_rows[:LANES, :], cw[:512].rearrange("(r p) one -> r (p one)", p=P))
         nc.sync.dma_start(factor_rows[LANES : LANES + BLOCKS, :], rw[0].rearrange("(c p) -> c p", p=P))
-        load_wd_scales(0)
-        load_wd_scales(1)
-        nc.sync.dma_start(x_planes[LANES - 1][:], x_rows[:, LANES - 1, :])
-        load_wd_scales(2)
-        load_wd_scales(3)
-        nc.sync.dma_start(wd_raw[0][:], wd_all[:, :512])
         load_y(0, 0)
-        nc.sync.dma_start(wd_raw[1][:], wd_all[:, 512:])
+        nc.sync.dma_start(wd_raw[0][:], wd_all[:, :512])
         load_y(0, 1)
+        nc.sync.dma_start(wd_raw[1][:], wd_all[:, 512:])
         nc.sync.dma_start(cw_dealt[:], cw[512:].rearrange("(p r) one -> p (r one)", r=LANES))
         load_y(1, 0)
-        load_y(1, 1)
+        for e in range(2):
+            nc.sync.dma_start(y_pairs[1][1][:, e, :], y_rows[1][:, 2 + e, :])
         for q in range(QUADS):
             nc.sync.dma_start(
                 wv_sc_raw[32 * q : 32 * q + 4, :].bitcast(I32).rearrange("f (o w) -> f o w", o=PASSES),
@@ -137,7 +136,7 @@ def tile_attend_gml_pl_sq_kernel(
         nc.scalar.activation(picked[0][:, 0, :], x_first[:].indirect(offsets[:]), COPY)
         for r in range(1, LANES - 1):
             nc.vector.tensor_copy(picked[r // 2][:, r % 2, :], x_planes[r][:].indirect(offsets[:]))
-        for h in range(2):
+        for h in (1, 0):
             nc.vector.tensor_copy(
                 picked[1][:, 1, h * HALF : (h + 1) * HALF],
                 x_planes[3][:].indirect(offsets[:, h * HALF // 16 : (h + 1) * HALF // 16]),
@@ -156,8 +155,8 @@ def tile_attend_gml_pl_sq_kernel(
             )
         wd_dealt = keep.tile([P, 512], I32, name="wd_dealt", tag="x_then_wd1", align_bytes=64)
         deal(nc.vector, wd_dealt[:], wd_raw[1][:])
-        wd_sc_dealt = keep.tile([P, 512], U8, name="wd_sc_dealt", tag="x_then_wd0", align_bytes=64)
-        deal_bytes(nc.vector, wd_sc_dealt[:], wd_sc_raw[:, 512:])
+        wd_sc_dealt = tile("wd_sc_dealt", [P, 512], U8)
+        deal_bytes(nc.gpsimd, wd_sc_dealt[:], wd_sc_raw[:, 512:])
         wd_codes = [wd_raw[0], wd_dealt]
         wd_sc = [wd_sc_raw, wd_sc_dealt]
 
@@ -220,13 +219,12 @@ def tile_attend_gml_pl_sq_kernel(
                 MULT,
             )
 
-        minus_cw = tile("minus_cw", [P, 1], F32)
-        nc.scalar.activation(minus_cw[:], cw_cols[0][:, 0:1], COPY, scale=-1.0)
+        minus_ycw = keep.tile([P, N], F32, name="minus_ycw", tag="x_then_wd0", align_bytes=64)
+        nc.vector.tensor_scalar(minus_ycw[:], y_plane(0, 0), cw_cols[0][:, 0:1], -1.0, MULT, MULT)
         early = scale_y(0, 1, cw_cols[0][:, 1:2])
         for h in range(2):
             scores(banks[h][:, :HALF], 0, 1, h * HALF, (h + 1) * HALF)
             residual(banks[h][:, :HALF], early, 0, 1, h * HALF, (h + 1) * HALF)
-        minus_ycw = scale_y(0, 0, minus_cw[:])
         for o, r, b in ((0, 2, 3), (0, 3, 4), (1, 0, 5), (1, 1, 6), (1, 2, 0), (1, 3, 1)):
             scores(banks[b][:], o, r, 0, N)
             residual(banks[b][:], scale_y(o, r, cw_cols[o][:, r : r + 1]), o, r, 0, N)

@@ -22,11 +22,9 @@ P = 128
 LANES = 4
 PASSES = V // (P * LANES)
 QUADS = 4
-CHUNKS = 4
-SPLIT = 512
-BLOCKS = N // P
 HALF = N // 2
-LANE_ORDER = (2, 0, 1, 3)
+CHUNKS = 4
+SPLIT = 640
 
 
 def tile_attend_gml_pl_sq_kernel(
@@ -36,329 +34,269 @@ def tile_attend_gml_pl_sq_kernel(
     with ExitStack() as ctx:
         keep = ctx.enter_context(tc.tile_pool(name="keep", bufs=1))
         placed = ctx.enter_context(tc.tile_pool(name="placed", bufs=1))
-        psum_keep = ctx.enter_context(tc.psum_pool(name="psum_keep", bufs=1))
+        psum = ctx.enter_context(tc.psum_pool(name="psum", bufs=1))
 
-        def tile(name, shape, dtype):
-            return keep.tile(shape, dtype, name=name, align_bytes=64)
+        def tile(name, shape, dtype, tag=None):
+            return keep.tile(shape, dtype, name=name, tag=tag or name, align_bytes=64)
 
         offsets = keep.tile([P, N // 16], U16, name="offsets")
 
+        def listed(window, h):
+            return window[:].indirect(offsets[:, h * HALF // 16 : (h + 1) * HALF // 16])
+
         wd_sc_raw = tile("wd_sc_raw", [P, V], U8)
-        wv_sc_raw = keep.tile([P, PASSES * D], U8, name="wv_sc_raw", tag="wv_sc_reused", align_bytes=64)
-        factor_rows = tile("factor_rows", [P, P], F32)
+        wv_sc_raw = tile("wv_sc_raw", [P, PASSES * D], U8)
         nc.gpsimd.memset(wd_sc_raw[:].bitcast(I32), 0)
-        nc.gpsimd.memset(factor_rows[:], 0.0)
-        nc.gpsimd.memset(wv_sc_raw[:].bitcast(I32), 0)
         identity = tile("identity", [P, P], F32)
         make_identity(nc, identity[:])
+        nc.gpsimd.memset(wv_sc_raw[:].bitcast(I32), 0)
+        windows = [tile(f"window{r}", [P, T], F32) for r in range(LANES)]
+        for r in range(LANES):
+            (nc.vector if r < 2 else nc.gpsimd).memset(windows[r][:], 0.0)
 
         x_rows = xT.rearrange("(p r) t -> p r t", r=LANES)
         x_planes = [tile(f"x{r}", [P, T], F32) for r in range(LANES)]
         wd_all = wd_words[0].rearrange("p n t -> p (n t)").bitcast(I32)
-        wd_raw = [
-            tile("wd_raw0", [P, 512], I32),
-            tile("wd_raw1", [P, 512], I32),
+        wd_raw = [tile(f"wd_raw{o}", [P, 512], I32) for o in range(PASSES)]
+        cw_cols = tile("cw_cols", [P, PASSES, LANES], F32)
+        rw_cols = tile("rw_cols", [P, LANES], F32)
+        y_rows = y.rearrange("(o p r) i -> o p r i", o=PASSES, r=LANES)
+        y_first = [[tile(f"y0{o}{u}", [P, 2, HALF], F32) for u in range(2)] for o in range(PASSES)]
+        y_second = [
+            tile("y10", [P, LANES, HALF], F32),
+            placed.tile([P, LANES, HALF], F32, name="y11", offset=0, align_bytes=64),
         ]
-        factor_cols = tile("factor_cols", [P, LANES + BLOCKS], F32)
-        rw_cols = factor_cols[:, LANES:]
-        cw_dealt = tile("cw_dealt", [P, LANES], F32)
-        cw_cols = [factor_cols[:, :LANES], cw_dealt[:]]
-        y_pairs = [
-            [keep.tile([P, 2, N], F32, name=f"y{o}{u}", tag=f"y{o}{u}_reused", align_bytes=64) for u in range(2)]
-            for o in range(PASSES)
-        ]
-        y_rows = [y[:512].rearrange("(r p) i -> p r i", p=P), y[512:].rearrange("(p r) i -> p r i", r=LANES)]
-
-        def load_y(o, u):
-            nc.sync.dma_start(y_pairs[o][u][:], y_rows[o][:, 2 * u : 2 * u + 2, :])
-
-        def load_wd_scales(q):
-            nc.sync.dma_start(
-                wd_sc_raw[32 * q : 32 * q + 4, :].bitcast(I32), wd_scales[0, 4 * q : 4 * q + 4, :].bitcast(I32)
-            )
+        wv_raw = tile("wv_raw", [P, PASSES, D], I32)
 
         nc.sync.dma_start(x_planes[0][:], x_rows[:, 0, :])
         nc.sync.dma_start(offsets[:], offs)
-        for r in range(1, LANES - 1):
+        for r in (1, 2):
             nc.sync.dma_start(x_planes[r][:], x_rows[:, r, :])
         for q in range(QUADS):
-            load_wd_scales(q)
-        nc.sync.dma_start(x_planes[LANES - 1][:], x_rows[:, LANES - 1, :])
-        nc.sync.dma_start(factor_rows[:LANES, :], cw[:512].rearrange("(r p) one -> r (p one)", p=P))
-        nc.sync.dma_start(factor_rows[LANES : LANES + BLOCKS, :], rw[0].rearrange("(c p) -> c p", p=P))
-        load_y(0, 0)
-        nc.sync.dma_start(wd_raw[0][:], wd_all[:, :512])
-        load_y(0, 1)
-        nc.sync.dma_start(wd_raw[1][:], wd_all[:, 512:])
-        nc.sync.dma_start(cw_dealt[:], cw[512:].rearrange("(p r) one -> p (r one)", r=LANES))
-        load_y(1, 0)
-        for e in range(2):
-            nc.sync.dma_start(y_pairs[1][1][:, e, :], y_rows[1][:, 2 + e, :])
+            nc.sync.dma_start(
+                wd_sc_raw[32 * q : 32 * q + 4, :].bitcast(I32), wd_scales[0, 4 * q : 4 * q + 4, :].bitcast(I32)
+            )
+        nc.sync.dma_start(x_planes[3][:], x_rows[:, 3, :])
+        nc.sync.dma_start(cw_cols[:], cw.rearrange("(o p r) one -> p o (r one)", o=PASSES, r=LANES))
+        nc.sync.dma_start(rw_cols[:], rw[0].rearrange("(p c) -> p c", c=LANES))
+        for o in range(PASSES):
+            nc.sync.dma_start(wd_raw[o][:], wd_all[:, o * 512 : (o + 1) * 512])
+            for u in range(2):
+                nc.sync.dma_start(y_first[o][u][:], y_rows[o, :, 2 * u : 2 * u + 2, :HALF])
         for q in range(QUADS):
             nc.sync.dma_start(
                 wv_sc_raw[32 * q : 32 * q + 4, :].bitcast(I32).rearrange("f (o w) -> f o w", o=PASSES),
                 wv_scales[:, 4 * q : 4 * q + 4, :].bitcast(I32).rearrange("o f w -> f o w"),
             )
-        wv_raw = keep.tile([P, PASSES, D], I32, name="wv_raw", tag="wv_reused", align_bytes=64)
         nc.sync.dma_start(wv_raw[:], wv_words.rearrange("o p n t -> p o (n t)").bitcast(I32))
+        for o in range(PASSES):
+            nc.sync.dma_start(y_second[o][:], y_rows[o, :, :, HALF:])
 
-        windows = {r: tile(f"window{r}", [P, T], F32) for r in LANE_ORDER[:2]}
-        for r in LANE_ORDER[:2]:
-            nc.vector.memset(windows[r][:], 0.0)
+        def y_plane(h, o, r):
+            return y_first[o][r // 2][:, r % 2, :] if h == 0 else y_second[o][:, r, :]
 
-        def deal(engine, dst, src):
-            engine.tensor_copy(
-                dst.rearrange("p (r c i) -> p c r i", r=LANES, i=2), src.rearrange("p (c i r) -> p c r i", r=LANES, i=2)
+        def dealt_views(dst, src):
+            return (
+                dst.rearrange("p (r c i) -> p c r i", r=LANES, i=4),
+                src.rearrange("p (c i r) -> p c r i", r=LANES, i=4),
             )
 
-        def deal_bytes(engine, dst, src):
-            engine.tensor_copy(
+        def deal_bytes(dst, src):
+            nc.gpsimd.tensor_copy(
                 dst.rearrange("p (o r s) -> p o r s", r=LANES, s=P), src.rearrange("p (o s r) -> p o r s", r=LANES, s=P)
             )
 
-
-        banks = [psum_keep.tile([P, N], F32, name=f"bank{b}") for b in range(7)]
-        turn_banks = [banks[b] for b in (3, 2, 4, 5)]
-        early_bank = banks[6]
-        dx_banks = [banks[b] for b in (0, 1, 3, 2)]
-        rw_bank = psum_keep.tile([P, N], F32, name="rw_bank")
-        nc.tensor.transpose(banks[6][:, :P], factor_rows[:], identity[:])
-        nc.scalar.copy(factor_cols[:], banks[6][:, : LANES + BLOCKS])
-        for c in range(BLOCKS):
+        banks = [psum.tile([P, N], F32, name=f"bank{b}") for b in range(7)]
+        rw_bank = psum.tile([P, N], F32, name="rw_bank")
+        for c in range(LANES):
             nc.tensor.transpose(rw_bank[:, c * P : (c + 1) * P], rw_cols[:, c : c + 1].to_broadcast([P, P]), identity[:])
 
-        picked = [tile(f"picked{u}", [P, 2, N], BF16) for u in range(2)]
-        x_lanes = [
-            keep.tile([P, HALF, LANES], BF16, name=f"x_lanes{h}", tag=f"x_then_wd{h}", align_bytes=64) for h in range(2)
-        ]
-        x_first = tile("x_first", [P, T], BF16)
-        nc.scalar.copy(x_first[:], x_planes[0][:])
-        nc.scalar.activation(picked[0][:, 0, :], x_first[:].indirect(offsets[:]), COPY)
-        for r in range(1, LANES - 1):
-            nc.vector.tensor_copy(picked[r // 2][:, r % 2, :], x_planes[r][:].indirect(offsets[:]))
-        for h in (1, 0):
-            nc.vector.tensor_copy(
-                picked[1][:, 1, h * HALF : (h + 1) * HALF],
-                x_planes[3][:].indirect(offsets[:, h * HALF // 16 : (h + 1) * HALF // 16]),
-            )
-        for h in range(2):
-            nc.scalar.copy(x_lanes[h][:, :, 0:2], picked[0][:, :, h * HALF : (h + 1) * HALF].rearrange("p e i -> p i e"))
-        nc.vector.tensor_copy(x_lanes[0][:, :, 2:4], picked[1][:, :, :HALF].rearrange("p e i -> p i e"))
-        nc.scalar.copy(x_lanes[1][:, :, 2:4], picked[1][:, :, HALF:].rearrange("p e i -> p i e"))
+        wd_sc = tile("wd_sc", [P, V], U8)
+        deal_bytes(wd_sc[:], wd_sc_raw[:])
 
-        x_codes = tile("x_codes", [P, N], U32)
-        x_sc = tile("x_sc", [P, N], U8)
-        for h in range(2):
-            cols = slice(h * HALF, (h + 1) * HALF)
+        x_lanes = [tile(f"x_lanes{h}", [P, HALF, LANES], BF16) for h in range(2)]
+        picked = tile("picked", [P, LANES, HALF], BF16)
+        for r in range(LANES):
+            nc.vector.tensor_copy(x_lanes[0][:, :, r], listed(x_planes[r], 0))
+            nc.scalar.activation(picked[:, r, :], listed(x_planes[r], 1), COPY)
+        nc.scalar.copy(
+            x_lanes[1][:].rearrange("p (c i) r -> p c r i", i=4), picked[:].rearrange("p r (c i) -> p c r i", i=4)
+        )
+        x_codes = [tile(f"x_codes{h}", [P, HALF], U32) for h in range(2)]
+        x_sc = [tile(f"x_sc{h}", [P, HALF], U8) for h in range(2)]
+
+        def quantise_x(h):
             nc.vector.quantize_mx(
-                out=x_codes[:, cols].bitcast(E4M3), scales=x_sc[:, cols], in_=x_lanes[h][:].rearrange("p i r -> p (i r)")
-            )
-        wd_dealt = keep.tile([P, 512], I32, name="wd_dealt", tag="x_then_wd1", align_bytes=64)
-        deal(nc.vector, wd_dealt[:], wd_raw[1][:])
-        wd_sc_dealt = tile("wd_sc_dealt", [P, 512], U8)
-        deal_bytes(nc.gpsimd, wd_sc_dealt[:], wd_sc_raw[:, 512:])
-        wd_codes = [wd_raw[0], wd_dealt]
-        wd_sc = [wd_sc_raw, wd_sc_dealt]
-
-        g_codes = [
-            tile("g_codes0", [P, N], U32),
-            tile("g_codes1", [P, N], U32),
-        ]
-        g_sc = [tile(f"g_sc{o}", [P, N], U8) for o in range(PASSES)]
-        for o in range(PASSES):
-            nc.gpsimd.memset(g_codes[o][:, HALF:], 0)
-            nc.gpsimd.memset(g_sc[o][:, HALF:].bitcast(U32), 0)
-        g_lanes = {(1, 0): tile("g_lanes10", [P, HALF, LANES], BF16)}
-        g_lanes[0, 1] = tile("g_lanes01", [P, HALF, LANES], BF16)
-        g_lanes[0, 0] = placed.tile([P, HALF, LANES], BF16, name="g_lanes00", offset=12544, align_bytes=64)
-        resid = [
-            keep.tile([P, LANES, N], F32, name=f"resid{o}", tag=f"resid{o}_reused", align_bytes=64) for o in range(PASSES)
-        ]
-
-        def scores(out, o, r, a, b):
-            nc.tensor.matmul_mx(
-                out=out,
-                lhsT=wd_codes[o][:, r * P : (r + 1) * P].bitcast(E4M3),
-                lhsT_scale=wd_sc[o][:, r * P : (r + 1) * P],
-                rhs=x_codes[:, a:b].bitcast(E4M3),
-                rhs_scale=x_sc[:, a:b],
-                start=True,
-                stop=True,
+                out=x_codes[h][:].bitcast(E4M3), scales=x_sc[h][:], in_=x_lanes[h][:].rearrange("p i r -> p (i r)")
             )
 
-        def y_plane(o, r):
-            return y_pairs[o][r // 2][:, r % 2, :]
+        wd_codes = [tile(f"wd_codes{o}", [P, 512], I32) for o in range(PASSES)]
+        score_banks = {
+            (0, 0): [banks[r][:, :HALF] for r in range(LANES)],
+            (0, 1): [banks[4 + r // 2][:, (r % 2) * HALF : (r % 2 + 1) * HALF] for r in range(LANES)],
+            (1, 0): [banks[(6, 0)[r // 2]][:, (r % 2) * HALF : (r % 2 + 1) * HALF] for r in range(LANES)],
+            (1, 1): [banks[1 + r // 2][:, (r % 2) * HALF : (r % 2 + 1) * HALF] for r in range(LANES)],
+        }
 
-        def quantise_g(o, h):
-            cols = slice(h * HALF, (h + 1) * HALF)
-            nc.vector.quantize_mx(
-                out=g_codes[o][:, cols].bitcast(E5M2),
-                scales=g_sc[o][:, cols],
-                in_=g_lanes[o, h][:].rearrange("p i r -> p (i r)"),
-            )
+        def scores(h, o):
+            for r in range(LANES):
+                nc.tensor.matmul_mx(
+                    out=score_banks[h, o][r],
+                    lhsT=wd_codes[o][:, r * P : (r + 1) * P].bitcast(E4M3),
+                    lhsT_scale=wd_sc[:, o * 512 + r * P : o * 512 + (r + 1) * P],
+                    rhs=x_codes[h][:].bitcast(E4M3),
+                    rhs_scale=x_sc[h][:],
+                    start=True,
+                    stop=True,
+                )
 
-        def scale_y(o, r, factor):
-            if (o, r) == (1, 3):
-                ycw = placed.tile([P, N], F32, name="ycw13", offset=0, align_bytes=64)
-            else:
-                ycw = tile(f"ycw{o}{r}", [P, N], F32)
-            nc.scalar.activation(ycw[:], y_plane(o, r), COPY, scale=factor)
-            return ycw
+        ycw, resid, g_lanes, g_codes, g_sc = {}, {}, {}, {}, {}
 
-        def residual(sums, ycw, o, r, a, b):
-            nc.vector.scalar_tensor_tensor(
-                resid[o][:, r, a:b], sums, cw_cols[o][:, r : r + 1], ycw[:, a:b], MULT, SUBTRACT
-            )
+        def scale_y(h, o):
+            ycw[h, o] = tile(f"ycw{h}{o}", [P, LANES, HALF], F32)
+            for r in range(LANES):
+                nc.scalar.activation(ycw[h, o][:, r, :], y_plane(h, o, r), COPY, scale=cw_cols[:, o, r : r + 1])
+            resid[h, o] = tile(f"resid{h}{o}", [P, LANES, HALF], F32)
 
-        def weigh(o, a, b):
-            pairs = rw_bank[:, a:b].rearrange("p (c i) -> p c i", i=2)
+        def residual(h, o, lanes):
+            for r in lanes:
+                nc.vector.scalar_tensor_tensor(
+                    resid[h, o][:, r, :], score_banks[h, o][r], cw_cols[:, o, r : r + 1], ycw[h, o][:, r, :], MULT, SUBTRACT
+                )
+
+        def weigh(h, o):
+            g_lanes[h, o] = tile(f"g_lanes{h}{o}", [P, HALF, LANES], BF16)
+            quads = HALF // 4
+            factors = rw_bank[:].rearrange("p (c q) -> p q c", c=4)[:, h * quads : (h + 1) * quads, :]
             nc.vector.tensor_tensor(
-                g_lanes[o, a // HALF][:].rearrange("p (c i) r -> p c r i", i=2),
-                resid[o][:, :, a:b].rearrange("p r (c i) -> p c r i", i=2),
-                pairs.unsqueeze(2).to_broadcast([P, (b - a) // 2, LANES, 2]),
+                g_lanes[h, o][:].rearrange("p (q c) r -> p q r c", c=4),
+                resid[h, o][:].rearrange("p r (q c) -> p q r c", c=4),
+                factors.unsqueeze(2).to_broadcast([P, quads, LANES, 4]),
                 MULT,
             )
 
-        minus_ycw = keep.tile([P, N], F32, name="minus_ycw", tag="x_then_wd0", align_bytes=64)
-        nc.vector.tensor_scalar(minus_ycw[:], y_plane(0, 0), cw_cols[0][:, 0:1], -1.0, MULT, MULT)
-        early = scale_y(0, 1, cw_cols[0][:, 1:2])
-        for h in range(2):
-            scores(banks[h][:, :HALF], 0, 1, h * HALF, (h + 1) * HALF)
-            residual(banks[h][:, :HALF], early, 0, 1, h * HALF, (h + 1) * HALF)
-        for o, r, b in ((0, 2, 3), (0, 3, 4), (1, 0, 5), (1, 1, 6), (1, 2, 0), (1, 3, 1)):
-            scores(banks[b][:], o, r, 0, N)
-            residual(banks[b][:], scale_y(o, r, cw_cols[o][:, r : r + 1]), o, r, 0, N)
-            if (o, r) == (0, 2):
-                scores(banks[2][:], 0, 0, 0, N)
-            if (o, r) == (0, 3):
-                acw = keep.tile([P, N], F32, name="acw", tag="y01_reused", align_bytes=64)
-                nc.scalar.activation(acw[:], banks[2][:], COPY, scale=cw_cols[0][:, 0:1])
-        turned = {}
-        for c in range(BLOCKS):
-            bank = turn_banks[c]
-            for r in (1, 2, 3, 0):
-                block = bank[:, r * P : (r + 1) * P]
-                if r == 0:
-                    nc.tensor.matmul(
-                        block, minus_ycw[:, c * P : (c + 1) * P], identity[:], start=True, stop=False, is_transpose=True
+        def quantise_g(h, o):
+            g_codes[h, o] = tile(f"g_codes{h}{o}", [P, HALF], U32)
+            g_sc[h, o] = tile(f"g_sc{h}{o}", [P, HALF], U8)
+            nc.vector.quantize_mx(
+                out=g_codes[h, o][:].bitcast(E5M2),
+                scales=g_sc[h, o][:],
+                in_=g_lanes[h, o][:].rearrange("p i r -> p (i r)"),
+            )
+
+        quantise_x(0)
+        nc.gpsimd.tensor_copy(*dealt_views(wd_codes[0][:], wd_raw[0][:]))
+        scores(0, 0)
+        scale_y(0, 0)
+        residual(0, 0, range(LANES))
+        quantise_x(1)
+        nc.scalar.copy(*dealt_views(wd_codes[1][:].bitcast(U32), wd_raw[1][:].bitcast(U32)))
+        scores(0, 1)
+        scale_y(0, 1)
+        weigh(0, 0)
+        residual(0, 1, range(LANES))
+        scores(1, 0)
+        scores(1, 1)
+        wv_sc = tile("wv_sc", [P, PASSES * D], U8)
+        deal_bytes(wv_sc[:], wv_sc_raw[:])
+        wv_codes = [tile(f"wv_codes{o}", [P, D], I32) for o in range(PASSES)]
+        for o in range(PASSES):
+            nc.scalar.copy(*dealt_views(wv_codes[o][:].bitcast(U32), wv_raw[:, o, :].bitcast(U32)))
+        quantise_g(0, 0)
+        weigh(0, 1)
+        scale_y(1, 0)
+        scale_y(1, 1)
+        residual(1, 0, (0,))
+        quantise_g(0, 1)
+
+        dx_banks = {
+            0: [banks[3][:, :HALF], banks[4][:, :HALF], banks[4][:, HALF:], banks[5][:, :HALF]],
+            1: [banks[(6, 0)[r // 2]][:, (r % 2) * HALF : (r % 2 + 1) * HALF] for r in range(LANES)],
+        }
+
+        def back(h, lanes):
+            for r in lanes:
+                for o in range(PASSES):
+                    nc.tensor.matmul_mx(
+                        out=dx_banks[h][r],
+                        lhsT=wv_codes[o][:, r * P : (r + 1) * P].bitcast(E4M3),
+                        lhsT_scale=wv_sc[:, o * D + r * P : o * D + (r + 1) * P],
+                        rhs=g_codes[h, o][:].bitcast(E5M2),
+                        rhs_scale=g_sc[h, o][:],
+                        start=o == 0,
+                        stop=o == PASSES - 1,
                     )
-                plane = acw[:] if r == 0 else resid[0][:, r, :]
-                nc.tensor.matmul(
-                    block, plane[:, c * P : (c + 1) * P], identity[:], start=r > 0, stop=True, is_transpose=True
-                )
-            turned[c] = keep.tile(
-                [P, 2, P, 2], BF16, name=f"turned{c}", tag="y11_reused" if c == 0 else f"turned{c}", align_bytes=64
-            )
-            nc.scalar.activation(
-                turned[c][:], bank[:].rearrange("i (p u e) -> i u p e", u=2, e=2), COPY, scale=rw_cols[:, c : c + 1]
-            )
-            words = bank[:, :HALF]
-            h, j = divmod(c, 2)
-            for u in range(2):
-                nc.tensor.transpose(
-                    words[:, u * P : (u + 1) * P],
-                    turned[c][:, u, :, :].rearrange("i p e -> i (p e)").bitcast(F32),
-                    identity[:],
-                )
-            nc.scalar.copy(
-                g_lanes[0, h][:, j * P : (j + 1) * P, :].rearrange("p i r -> p (i r)").bitcast(F32).rearrange("p (i u) -> p i u", u=2),
-                words.rearrange("p (u i) -> p i u", u=2),
-            )
 
-        wv_words_by_lane = wv_raw[:].rearrange("p o (s r) -> p r o s", r=LANES)
-        wv_bytes_by_lane = wv_sc_raw[:].rearrange("p (o s r) -> p r o s", o=PASSES, r=LANES)
-        wv_codes, wv_sc = {}, {}
+        back(0, range(LANES))
+        residual(1, 0, (1, 2, 3))
+        residual(1, 1, (0,))
+        weigh(1, 0)
+        residual(1, 1, (1, 2, 3))
+        quantise_g(1, 0)
+        weigh(1, 1)
 
-        def deal_lane(r, offset):
-            wv_codes[r] = placed.tile([P, PASSES, P], I32, name=f"wv_codes{r}", offset=offset, align_bytes=64)
-            nc.gpsimd.tensor_copy(wv_codes[r][:], wv_words_by_lane[:, r, :, :])
-            wv_sc[r] = placed.tile([P, PASSES, P], U8, name=f"wv_sc{r}", offset=offset + 1024, align_bytes=64)
-            nc.gpsimd.tensor_copy(wv_sc[r][:], wv_bytes_by_lane[:, r, :, :])
+        dx00 = placed.tile([P, HALF], F32, name="dx00", offset=0, align_bytes=64)
+        nc.scalar.copy(dx00[:], dx_banks[0][0])
+        dx012 = placed.tile([P, 2, HALF], F32, name="dx012", offset=1024, align_bytes=64)
+        nc.scalar.copy(dx012[:].rearrange("p r i -> p (r i)"), banks[4][:])
+        nc.scalar.activation(listed(windows[0], 0), dx00[:], COPY)
+        for r in (1, 2):
+            nc.scalar.activation(listed(windows[r], 0), dx012[:, r - 1, :], COPY)
 
-        def back(bank, r, order):
-            for o in order:
-                nc.tensor.matmul_mx(
-                    out=bank[:],
-                    lhsT=wv_codes[r][:, o, :].bitcast(E4M3),
-                    lhsT_scale=wv_sc[r][:, o, :],
-                    rhs=g_codes[o][:].bitcast(E5M2),
-                    rhs_scale=g_sc[o][:],
-                    start=o == order[0],
-                    stop=o == order[1],
-                )
+        dx03 = tile("dx03", [P, HALF], F32, tag="resid11")
+        nc.vector.tensor_copy(dx03[:], dx_banks[0][3])
+        quantise_g(1, 1)
+        back(1, range(LANES))
+        nc.vector.tensor_copy(listed(windows[3], 0), dx03[:])
+        dx101 = tile("dx101", [P, 2, HALF], F32)
+        nc.vector.tensor_copy(dx101[:].rearrange("p r i -> p (r i)"), banks[6][:])
+        dx123 = tile("dx123", [P, 2, HALF], F32)
+        nc.scalar.copy(dx123[:].rearrange("p r i -> p (r i)"), banks[0][:])
 
         out_rows = out_0.rearrange("(p r) t -> p r t", r=LANES)
-        dx = {}
-
-        def empty(k, a, b, bank, tag):
-            dx[k, a] = keep.tile([P, b - a], F32, name=f"dx{k}_{a}", tag=tag, align_bytes=64)
-            nc.scalar.copy(dx[k, a][:], bank[:, a:b])
-
-        def scatter(k, a, b):
-            nc.vector.tensor_copy(windows[LANE_ORDER[k]][:].indirect(offsets[:, a // 16 : b // 16]), dx[k, a][:])
-
-        deal_lane(LANE_ORDER[0], 0)
-        weigh(1, 0, HALF)
-        quantise_g(1, 0)
-        quantise_g(0, 0)
-        back(early_bank, LANE_ORDER[0], (1, 0))
-        g_lanes[1, 1] = placed.tile([P, HALF, LANES], BF16, name="g_lanes11", offset=12544, align_bytes=64)
-        weigh(1, HALF, N)
-        quantise_g(0, 1)
-        quantise_g(1, 1)
-        empty(0, 0, HALF, early_bank, "dx_first")
-        scatter(0, 0, HALF)
-        back(dx_banks[0], LANE_ORDER[0], (0, 1))
-        deal_lane(LANE_ORDER[1], 12544 + 768)
-        back(dx_banks[1], LANE_ORDER[1], (0, 1))
-        odd_sc = keep.tile([P, 2, PASSES, P], U8, name="odd_sc", tag="dx_first", align_bytes=64)
-        nc.gpsimd.tensor_copy(odd_sc[:], wv_bytes_by_lane[:, 1::2, :, :])
-        for k in (2, 3):
-            r = LANE_ORDER[k]
-            wv_sc[r] = odd_sc[:, r // 2, :, :]
-            wv_codes[r] = placed.tile(
-                [P, PASSES, P], I32, name=f"wv_codes{r}", offset=12544 - 256 if k == 2 else 12544 + 768, align_bytes=64
-            )
-            nc.gpsimd.tensor_copy(wv_codes[r][:], wv_words_by_lane[:, r, :, :])
-            back(dx_banks[k], r, (0, 1))
-        windows[LANE_ORDER[2]] = keep.tile([P, T], F32, name="window_third", tag="wv_reused", align_bytes=64)
-        nc.gpsimd.memset(windows[LANE_ORDER[2]][:], 0.0)
-        out_lanes = placed.tile([P, T, LANES], BF16, name="out_lanes", offset=12544 + 768 - 8192, align_bytes=64)
-        empty(0, HALF, N, dx_banks[0], "dx_ring")
-        empty(1, 0, N, dx_banks[1], "dx1")
-        empty(2, 0, N, dx_banks[2], "dx2")
-        for k, r in enumerate(LANE_ORDER):
-            scatter(k, HALF if k == 0 else 0, N)
-            if k == 1:
-                windows[LANE_ORDER[3]] = keep.tile([P, T], F32, name="window_last", tag="dx1", align_bytes=64)
-                nc.gpsimd.memset(windows[LANE_ORDER[3]][:], 0.0)
+        rounded = tile("rounded", [P, LANES, T], BF16)
+        for r in (0, 2, 1, 3):
+            if r < 2:
+                nc.vector.tensor_copy(listed(windows[r], 1), dx101[:, r, :])
+            else:
+                nc.scalar.activation(listed(windows[r], 1), dx123[:, r - 2, :], COPY)
             nc.sync.dma_start(out_rows[:, r, :], windows[r][:])
-            if k == 0:
-                nc.scalar.copy(out_lanes[:, :, r], windows[r][:])
-                empty(LANES - 1, 0, N, dx_banks[LANES - 1], "dx_ring")
-            elif k < LANES - 1:
-                nc.scalar.copy(out_lanes[:, :SPLIT, r], windows[r][:, :SPLIT])
-                nc.gpsimd.tensor_copy(out_lanes[:, SPLIT:, r], windows[r][:, SPLIT:])
+            if r % 2 == 0:
+                nc.gpsimd.tensor_copy(rounded[:, r, :], windows[r][:])
+        nc.vector.tensor_copy(rounded[:, 1, :], windows[1][:])
+        nc.vector.tensor_copy(rounded[:, 3, :SPLIT], windows[3][:, :SPLIT])
+        nc.scalar.copy(rounded[:, 3, SPLIT:], windows[3][:, SPLIT:])
 
-        last = LANE_ORDER[-1]
+        out_lanes = tile("out_lanes", [P, T, LANES], BF16)
+
+        def weave(a, b):
+            return (
+                out_lanes[:, a:b, :].rearrange("p (c i) r -> p c r i", i=4),
+                rounded[:, :, a:b].rearrange("p r (c i) -> p c r i", i=4),
+            )
+
         out_sc = tile("out_sc", [P, T], U8)
         out_words = out_1[0].rearrange("p n t -> p (n t)").bitcast(I32)
         width = T // CHUNKS
         codes = tile("out_codes", [P, T], I32)
-        for a, b in ((0, width), (width, SPLIT)):
-            nc.vector.tensor_copy(out_lanes[:, a:b, last], windows[last][:, a:b])
-        for a, b in ((SPLIT, 3 * width), (3 * width, T)):
-            nc.scalar.copy(out_lanes[:, a:b, last], windows[last][:, a:b])
-        for c in range(CHUNKS):
+
+        def quantise_out(c):
             cols = slice(c * width, (c + 1) * width)
             nc.vector.quantize_mx(
                 out=codes[:, cols].bitcast(E4M3),
                 scales=out_sc[:, cols],
                 in_=out_lanes[:, cols, :].rearrange("p t r -> p (t r)"),
             )
-            if c > 0:
-                stored = slice(0 if c == 1 else c * width, (c + 1) * width)
-                nc.sync.dma_start(out_words[:, stored], codes[:, stored])
+            nc.sync.dma_start(out_words[:, cols], codes[:, cols])
+
+        nc.scalar.copy(*weave(SPLIT, 3 * width))
+        nc.scalar.copy(*weave(3 * width, T))
+        nc.vector.tensor_copy(*weave(0, width))
+        nc.vector.tensor_copy(*weave(width, 2 * width))
+        quantise_out(0)
+        nc.vector.tensor_copy(*weave(2 * width, SPLIT))
+        for c in range(1, CHUNKS):
+            quantise_out(c)
         queues = (nc.scalar, nc.sync, nc.scalar, nc.sync)
         for q in range(QUADS):
             queues[q].dma_start(out_2[0, 4 * q : 4 * q + 4, :].bitcast(I32), out_sc[32 * q : 32 * q + 4, :].bitcast(I32))

@@ -25,6 +25,7 @@ QUADS = 4
 HALF = N // 2
 CHUNKS = 4
 SPLIT = 640
+ASIDE = 256
 
 
 def tile_attend_gml_pl_sq_kernel(
@@ -41,8 +42,8 @@ def tile_attend_gml_pl_sq_kernel(
 
         offsets = keep.tile([P, N // 16], U16, name="offsets")
 
-        def listed(window, h):
-            return window[:].indirect(offsets[:, h * HALF // 16 : (h + 1) * HALF // 16])
+        def listed(window, h, a=0, b=HALF):
+            return window[:].indirect(offsets[:, (h * HALF + a) // 16 : (h * HALF + b) // 16])
 
         wd_sc_raw = tile("wd_sc_raw", [P, V], U8)
         wv_sc_raw = tile("wv_sc_raw", [P, PASSES * D], U8)
@@ -77,12 +78,14 @@ def tile_attend_gml_pl_sq_kernel(
                 wd_sc_raw[32 * q : 32 * q + 4, :].bitcast(I32), wd_scales[0, 4 * q : 4 * q + 4, :].bitcast(I32)
             )
         nc.sync.dma_start(x_planes[3][:], x_rows[:, 3, :])
-        nc.sync.dma_start(cw_cols[:], cw.rearrange("(o p r) one -> p o (r one)", o=PASSES, r=LANES))
-        nc.sync.dma_start(rw_cols[:], rw[0].rearrange("(p c) -> p c", c=LANES))
         for o in range(PASSES):
             nc.sync.dma_start(wd_raw[o][:], wd_all[:, o * 512 : (o + 1) * 512])
+            if o == 0:
+                nc.sync.dma_start(cw_cols[:], cw.rearrange("(o p r) one -> p o (r one)", o=PASSES, r=LANES))
             for u in range(2):
                 nc.sync.dma_start(y_first[o][u][:], y_rows[o, :, 2 * u : 2 * u + 2, :HALF])
+            if o == 0:
+                nc.sync.dma_start(rw_cols[:], rw[0].rearrange("(p c) -> p c", c=LANES))
         for q in range(QUADS):
             nc.sync.dma_start(
                 wv_sc_raw[32 * q : 32 * q + 4, :].bitcast(I32).rearrange("f (o w) -> f o w", o=PASSES),
@@ -197,9 +200,9 @@ def tile_attend_gml_pl_sq_kernel(
         residual(0, 1, range(LANES))
         scores(1, 0)
         scores(1, 1)
-        wv_sc = tile("wv_sc", [P, PASSES * D], U8)
+        wv_sc = tile("wv_sc", [P, PASSES * D], U8, tag="x_lanes1")
         deal_bytes(wv_sc[:], wv_sc_raw[:])
-        wv_codes = [tile(f"wv_codes{o}", [P, D], I32) for o in range(PASSES)]
+        wv_codes = [tile(f"wv_codes{o}", [P, D], I32, tag=f"y01{1 - o}") for o in range(PASSES)]
         for o in range(PASSES):
             nc.scalar.copy(*dealt_views(wv_codes[o][:].bitcast(U32), wv_raw[:, o, :].bitcast(U32)))
         quantise_g(0, 0)
@@ -214,25 +217,29 @@ def tile_attend_gml_pl_sq_kernel(
             1: [banks[(6, 0)[r // 2]][:, (r % 2) * HALF : (r % 2 + 1) * HALF] for r in range(LANES)],
         }
 
-        def back(h, lanes):
-            for r in lanes:
-                for o in range(PASSES):
+        shares_bank = {0: ((0,), (1, 2), (3,)), 1: ((0, 1), (2, 3))}
+
+        def back(h, o):
+            for lanes in shares_bank[h]:
+                for r in lanes:
                     nc.tensor.matmul_mx(
                         out=dx_banks[h][r],
                         lhsT=wv_codes[o][:, r * P : (r + 1) * P].bitcast(E4M3),
                         lhsT_scale=wv_sc[:, o * D + r * P : o * D + (r + 1) * P],
                         rhs=g_codes[h, o][:].bitcast(E5M2),
                         rhs_scale=g_sc[h, o][:],
-                        start=o == 0,
-                        stop=o == PASSES - 1,
+                        start=o == 0 and r == lanes[0],
+                        stop=o == PASSES - 1 and r == lanes[-1],
                     )
 
-        back(0, range(LANES))
+        back(0, 0)
+        back(0, 1)
         residual(1, 0, (1, 2, 3))
         residual(1, 1, (0,))
         weigh(1, 0)
         residual(1, 1, (1, 2, 3))
         quantise_g(1, 0)
+        back(1, 0)
         weigh(1, 1)
 
         dx00 = placed.tile([P, HALF], F32, name="dx00", offset=0, align_bytes=64)
@@ -246,8 +253,9 @@ def tile_attend_gml_pl_sq_kernel(
         dx03 = tile("dx03", [P, HALF], F32, tag="resid11")
         nc.vector.tensor_copy(dx03[:], dx_banks[0][3])
         quantise_g(1, 1)
-        back(1, range(LANES))
-        nc.vector.tensor_copy(listed(windows[3], 0), dx03[:])
+        back(1, 1)
+        nc.vector.tensor_copy(listed(windows[3], 0, 0, HALF // 2), dx03[:, : HALF // 2])
+        nc.scalar.activation(listed(windows[3], 0, HALF // 2, HALF), dx03[:, HALF // 2 :], COPY)
         dx101 = tile("dx101", [P, 2, HALF], F32)
         nc.vector.tensor_copy(dx101[:].rearrange("p r i -> p (r i)"), banks[6][:])
         dx123 = tile("dx123", [P, 2, HALF], F32)
@@ -262,8 +270,10 @@ def tile_attend_gml_pl_sq_kernel(
                 nc.scalar.activation(listed(windows[r], 1), dx123[:, r - 2, :], COPY)
             nc.sync.dma_start(out_rows[:, r, :], windows[r][:])
             if r % 2 == 0:
-                nc.gpsimd.tensor_copy(rounded[:, r, :], windows[r][:])
+                end = T if r == 0 else ASIDE
+                nc.gpsimd.tensor_copy(rounded[:, r, :end], windows[r][:, :end])
         nc.vector.tensor_copy(rounded[:, 1, :], windows[1][:])
+        nc.vector.tensor_copy(rounded[:, 2, ASIDE:], windows[2][:, ASIDE:])
         nc.vector.tensor_copy(rounded[:, 3, :SPLIT], windows[3][:, :SPLIT])
         nc.scalar.copy(rounded[:, 3, SPLIT:], windows[3][:, SPLIT:])
 

@@ -25,7 +25,6 @@ QUADS = 4
 HALF = N // 2
 CHUNKS = 4
 SPLIT = 640
-ASIDE = 256
 
 
 def tile_attend_gml_pl_sq_kernel(
@@ -42,8 +41,8 @@ def tile_attend_gml_pl_sq_kernel(
 
         offsets = keep.tile([P, N // 16], U16, name="offsets")
 
-        def listed(window, h, a=0, b=HALF):
-            return window[:].indirect(offsets[:, (h * HALF + a) // 16 : (h * HALF + b) // 16])
+        def listed(window, h):
+            return window[:].indirect(offsets[:, h * HALF // 16 : (h + 1) * HALF // 16])
 
         wd_sc_raw = tile("wd_sc_raw", [P, V], U8)
         wv_sc_raw = tile("wv_sc_raw", [P, PASSES * D], U8)
@@ -63,10 +62,8 @@ def tile_attend_gml_pl_sq_kernel(
         rw_cols = tile("rw_cols", [P, LANES], F32)
         y_rows = y.rearrange("(o p r) i -> o p r i", o=PASSES, r=LANES)
         y_first = [[tile(f"y0{o}{u}", [P, 2, HALF], F32) for u in range(2)] for o in range(PASSES)]
-        y_second = [
-            tile("y10", [P, LANES, HALF], F32),
-            placed.tile([P, LANES, HALF], F32, name="y11", offset=0, align_bytes=64),
-        ]
+        y_second = tile("y10", [P, LANES, HALF], F32)
+        y_last = [placed.tile([P, 2, HALF], F32, name=f"y11{u}", offset=2048 * u, align_bytes=64) for u in range(2)]
         wv_raw = tile("wv_raw", [P, PASSES, D], I32)
 
         nc.sync.dma_start(x_planes[0][:], x_rows[:, 0, :])
@@ -92,11 +89,14 @@ def tile_attend_gml_pl_sq_kernel(
                 wv_scales[:, 4 * q : 4 * q + 4, :].bitcast(I32).rearrange("o f w -> f o w"),
             )
         nc.sync.dma_start(wv_raw[:], wv_words.rearrange("o p n t -> p o (n t)").bitcast(I32))
-        for o in range(PASSES):
-            nc.sync.dma_start(y_second[o][:], y_rows[o, :, :, HALF:])
+        nc.sync.dma_start(y_second[:], y_rows[0, :, :, HALF:])
+        for u in range(2):
+            nc.sync.dma_start(y_last[u][:], y_rows[1, :, 2 * u : 2 * u + 2, HALF:])
 
         def y_plane(h, o, r):
-            return y_first[o][r // 2][:, r % 2, :] if h == 0 else y_second[o][:, r, :]
+            if (h, o) == (1, 0):
+                return y_second[:, r, :]
+            return (y_first[o] if h == 0 else y_last)[r // 2][:, r % 2, :]
 
         def dealt_views(dst, src):
             return (
@@ -202,10 +202,10 @@ def tile_attend_gml_pl_sq_kernel(
         scores(1, 1)
         wv_sc = tile("wv_sc", [P, PASSES * D], U8, tag="x_lanes1")
         deal_bytes(wv_sc[:], wv_sc_raw[:])
-        wv_codes = [tile(f"wv_codes{o}", [P, D], I32, tag=f"y01{1 - o}") for o in range(PASSES)]
-        for o in range(PASSES):
-            nc.scalar.copy(*dealt_views(wv_codes[o][:].bitcast(U32), wv_raw[:, o, :].bitcast(U32)))
         quantise_g(0, 0)
+        wv_codes = tile("wv_codes", [P, PASSES, D], I32, tag="g_lanes00")
+        for o in range(PASSES):
+            nc.gpsimd.tensor_copy(*dealt_views(wv_codes[:, o, :], wv_raw[:, o, :]))
         weigh(0, 1)
         scale_y(1, 0)
         scale_y(1, 1)
@@ -217,14 +217,14 @@ def tile_attend_gml_pl_sq_kernel(
             1: [banks[(6, 0)[r // 2]][:, (r % 2) * HALF : (r % 2 + 1) * HALF] for r in range(LANES)],
         }
 
-        shares_bank = {0: ((0,), (1, 2), (3,)), 1: ((0, 1), (2, 3))}
+        shares_bank = {0: ((0,), (1, 2), (3,)), 1: ((2, 3), (0, 1))}
 
         def back(h, o):
             for lanes in shares_bank[h]:
                 for r in lanes:
                     nc.tensor.matmul_mx(
                         out=dx_banks[h][r],
-                        lhsT=wv_codes[o][:, r * P : (r + 1) * P].bitcast(E4M3),
+                        lhsT=wv_codes[:, o, r * P : (r + 1) * P].bitcast(E4M3),
                         lhsT_scale=wv_sc[:, o * D + r * P : o * D + (r + 1) * P],
                         rhs=g_codes[h, o][:].bitcast(E5M2),
                         rhs_scale=g_sc[h, o][:],
@@ -242,9 +242,9 @@ def tile_attend_gml_pl_sq_kernel(
         back(1, 0)
         weigh(1, 1)
 
-        dx00 = placed.tile([P, HALF], F32, name="dx00", offset=0, align_bytes=64)
+        dx00 = placed.tile([P, HALF], F32, name="dx00", offset=1536, align_bytes=64)
         nc.scalar.copy(dx00[:], dx_banks[0][0])
-        dx012 = placed.tile([P, 2, HALF], F32, name="dx012", offset=1024, align_bytes=64)
+        dx012 = placed.tile([P, 2, HALF], F32, name="dx012", offset=2560, align_bytes=64)
         nc.scalar.copy(dx012[:].rearrange("p r i -> p (r i)"), banks[4][:])
         nc.scalar.activation(listed(windows[0], 0), dx00[:], COPY)
         for r in (1, 2):
@@ -254,8 +254,7 @@ def tile_attend_gml_pl_sq_kernel(
         nc.vector.tensor_copy(dx03[:], dx_banks[0][3])
         quantise_g(1, 1)
         back(1, 1)
-        nc.vector.tensor_copy(listed(windows[3], 0, 0, HALF // 2), dx03[:, : HALF // 2])
-        nc.scalar.activation(listed(windows[3], 0, HALF // 2, HALF), dx03[:, HALF // 2 :], COPY)
+        nc.vector.tensor_copy(listed(windows[3], 0), dx03[:])
         dx101 = tile("dx101", [P, 2, HALF], F32)
         nc.vector.tensor_copy(dx101[:].rearrange("p r i -> p (r i)"), banks[6][:])
         dx123 = tile("dx123", [P, 2, HALF], F32)
@@ -263,19 +262,18 @@ def tile_attend_gml_pl_sq_kernel(
 
         out_rows = out_0.rearrange("(p r) t -> p r t", r=LANES)
         rounded = tile("rounded", [P, LANES, T], BF16)
-        for r in (0, 2, 1, 3):
+        for r in (2, 0, 3, 1):
             if r < 2:
                 nc.vector.tensor_copy(listed(windows[r], 1), dx101[:, r, :])
             else:
                 nc.scalar.activation(listed(windows[r], 1), dx123[:, r - 2, :], COPY)
             nc.sync.dma_start(out_rows[:, r, :], windows[r][:])
-            if r % 2 == 0:
-                end = T if r == 0 else ASIDE
-                nc.gpsimd.tensor_copy(rounded[:, r, :end], windows[r][:, :end])
-        nc.vector.tensor_copy(rounded[:, 1, :], windows[1][:])
-        nc.vector.tensor_copy(rounded[:, 2, ASIDE:], windows[2][:, ASIDE:])
-        nc.vector.tensor_copy(rounded[:, 3, :SPLIT], windows[3][:, :SPLIT])
-        nc.scalar.copy(rounded[:, 3, SPLIT:], windows[3][:, SPLIT:])
+        nc.gpsimd.tensor_copy(rounded[:, 2, :], windows[2][:])
+        nc.gpsimd.tensor_copy(rounded[:, 0, :SPLIT], windows[0][:, :SPLIT])
+        for r in (3, 1):
+            nc.vector.tensor_copy(rounded[:, r, :SPLIT], windows[r][:, :SPLIT])
+        for r in (3, 0, 1):
+            nc.scalar.copy(rounded[:, r, SPLIT:], windows[r][:, SPLIT:])
 
         out_lanes = tile("out_lanes", [P, T, LANES], BF16)
 
@@ -297,7 +295,9 @@ def tile_attend_gml_pl_sq_kernel(
                 scales=out_sc[:, cols],
                 in_=out_lanes[:, cols, :].rearrange("p t r -> p (t r)"),
             )
-            nc.sync.dma_start(out_words[:, cols], codes[:, cols])
+            if c > 0:
+                stored = slice(0 if c == 1 else c * width, (c + 1) * width)
+                nc.sync.dma_start(out_words[:, stored], codes[:, stored])
 
         nc.scalar.copy(*weave(SPLIT, 3 * width))
         nc.scalar.copy(*weave(3 * width, T))

@@ -270,9 +270,9 @@ def tile_attend_gml_pl_sq_kernel(
             nc.sync.dma_start(out_rows[:, r, :], windows[r][:])
         nc.gpsimd.tensor_copy(rounded[:, 2, :], windows[2][:])
         nc.gpsimd.tensor_copy(rounded[:, 0, :SPLIT], windows[0][:, :SPLIT])
-        for r in (3, 1):
-            nc.vector.tensor_copy(rounded[:, r, :SPLIT], windows[r][:, :SPLIT])
-        for r in (3, 0, 1):
+        nc.vector.tensor_copy(rounded[:, 1, :], windows[1][:])
+        nc.vector.tensor_copy(rounded[:, 3, :SPLIT], windows[3][:, :SPLIT])
+        for r in (3, 0):
             nc.scalar.copy(rounded[:, r, SPLIT:], windows[r][:, SPLIT:])
 
         out_lanes = tile("out_lanes", [P, T, LANES], BF16)

@@ -75,14 +75,12 @@ def tile_attend_gml_pl_sq_kernel(
                 wd_sc_raw[32 * q : 32 * q + 4, :].bitcast(I32), wd_scales[0, 4 * q : 4 * q + 4, :].bitcast(I32)
             )
         nc.sync.dma_start(x_planes[3][:], x_rows[:, 3, :])
+        nc.sync.dma_start(cw_cols[:], cw.rearrange("(o p r) one -> p o (r one)", o=PASSES, r=LANES))
+        nc.sync.dma_start(rw_cols[:], rw[0].rearrange("(p c) -> p c", c=LANES))
         for o in range(PASSES):
             nc.sync.dma_start(wd_raw[o][:], wd_all[:, o * 512 : (o + 1) * 512])
-            if o == 0:
-                nc.sync.dma_start(cw_cols[:], cw.rearrange("(o p r) one -> p o (r one)", o=PASSES, r=LANES))
             for u in range(2):
                 nc.sync.dma_start(y_first[o][u][:], y_rows[o, :, 2 * u : 2 * u + 2, :HALF])
-            if o == 0:
-                nc.sync.dma_start(rw_cols[:], rw[0].rearrange("(p c) -> p c", c=LANES))
         for q in range(QUADS):
             nc.sync.dma_start(
                 wv_sc_raw[32 * q : 32 * q + 4, :].bitcast(I32).rearrange("f (o w) -> f o w", o=PASSES),
@@ -200,12 +198,12 @@ def tile_attend_gml_pl_sq_kernel(
         residual(0, 1, range(LANES))
         scores(1, 0)
         scores(1, 1)
-        wv_sc = tile("wv_sc", [P, PASSES * D], U8, tag="x_lanes1")
+        wv_sc = tile("wv_sc", [P, PASSES * D], U8)
         deal_bytes(wv_sc[:], wv_sc_raw[:])
-        quantise_g(0, 0)
-        wv_codes = tile("wv_codes", [P, PASSES, D], I32, tag="g_lanes00")
+        wv_codes = [tile(f"wv_codes{o}", [P, D], I32, tag=f"y01{1 - o}") for o in range(PASSES)]
         for o in range(PASSES):
-            nc.gpsimd.tensor_copy(*dealt_views(wv_codes[:, o, :], wv_raw[:, o, :]))
+            nc.scalar.copy(*dealt_views(wv_codes[o][:].bitcast(U32), wv_raw[:, o, :].bitcast(U32)))
+        quantise_g(0, 0)
         weigh(0, 1)
         scale_y(1, 0)
         scale_y(1, 1)
@@ -224,7 +222,7 @@ def tile_attend_gml_pl_sq_kernel(
                 for r in lanes:
                     nc.tensor.matmul_mx(
                         out=dx_banks[h][r],
-                        lhsT=wv_codes[:, o, r * P : (r + 1) * P].bitcast(E4M3),
+                        lhsT=wv_codes[o][:, r * P : (r + 1) * P].bitcast(E4M3),
                         lhsT_scale=wv_sc[:, o * D + r * P : o * D + (r + 1) * P],
                         rhs=g_codes[h, o][:].bitcast(E5M2),
                         rhs_scale=g_sc[h, o][:],

@@ -75,12 +75,14 @@ def tile_attend_gml_pl_sq_kernel(
                 wd_sc_raw[32 * q : 32 * q + 4, :].bitcast(I32), wd_scales[0, 4 * q : 4 * q + 4, :].bitcast(I32)
             )
         nc.sync.dma_start(x_planes[3][:], x_rows[:, 3, :])
-        nc.sync.dma_start(cw_cols[:], cw.rearrange("(o p r) one -> p o (r one)", o=PASSES, r=LANES))
-        nc.sync.dma_start(rw_cols[:], rw[0].rearrange("(p c) -> p c", c=LANES))
         for o in range(PASSES):
             nc.sync.dma_start(wd_raw[o][:], wd_all[:, o * 512 : (o + 1) * 512])
+            if o == 0:
+                nc.sync.dma_start(cw_cols[:], cw.rearrange("(o p r) one -> p o (r one)", o=PASSES, r=LANES))
             for u in range(2):
                 nc.sync.dma_start(y_first[o][u][:], y_rows[o, :, 2 * u : 2 * u + 2, :HALF])
+                if (o, u) == (0, 0):
+                    nc.sync.dma_start(rw_cols[:], rw[0].rearrange("(p c) -> p c", c=LANES))
         for q in range(QUADS):
             nc.sync.dma_start(
                 wv_sc_raw[32 * q : 32 * q + 4, :].bitcast(I32).rearrange("f (o w) -> f o w", o=PASSES),
@@ -115,15 +117,12 @@ def tile_attend_gml_pl_sq_kernel(
         wd_sc = tile("wd_sc", [P, V], U8)
         deal_bytes(wd_sc[:], wd_sc_raw[:])
 
-        x_lanes = [tile(f"x_lanes{h}", [P, HALF, LANES], BF16) for h in range(2)]
+        x_lanes = [tile("x_lanes0", [P, HALF, LANES], BF16)]
         picked = tile("picked", [P, LANES, HALF], BF16)
         for r in range(LANES):
             nc.vector.tensor_copy(x_lanes[0][:, :, r], listed(x_planes[r], 0))
             nc.scalar.activation(picked[:, r, :], listed(x_planes[r], 1), COPY)
-        nc.scalar.copy(
-            x_lanes[1][:].rearrange("p (c i) r -> p c r i", i=4), picked[:].rearrange("p r (c i) -> p c r i", i=4)
-        )
-        x_codes = [tile(f"x_codes{h}", [P, HALF], U32) for h in range(2)]
+        x_codes = [tile("x_codes0", [P, HALF], U32)]
         x_sc = [tile(f"x_sc{h}", [P, HALF], U8) for h in range(2)]
 
         def quantise_x(h):
@@ -186,12 +185,17 @@ def tile_attend_gml_pl_sq_kernel(
             )
 
         quantise_x(0)
+        x_lanes.append(tile("x_lanes1", [P, HALF, LANES], BF16, tag="x_lanes0"))
+        nc.vector.tensor_copy(
+            x_lanes[1][:].rearrange("p (c i) r -> p c r i", i=4), picked[:].rearrange("p r (c i) -> p c r i", i=4)
+        )
         nc.gpsimd.tensor_copy(*dealt_views(wd_codes[0][:], wd_raw[0][:]))
         scores(0, 0)
         scale_y(0, 0)
         residual(0, 0, range(LANES))
-        quantise_x(1)
         nc.scalar.copy(*dealt_views(wd_codes[1][:].bitcast(U32), wd_raw[1][:].bitcast(U32)))
+        x_codes.append(tile("x_codes1", [P, HALF], U32))
+        quantise_x(1)
         scores(0, 1)
         scale_y(0, 1)
         weigh(0, 0)

from contextlib import ExitStack

import concourse.mybir as mybir
from concourse.masks import make_identity

N, T, D, V = 512, 1024, 512, 1024
FLOPS = 2 * 2 * N * D * V

F32 = mybir.dt.float32
BF16 = mybir.dt.bfloat16
I32 = mybir.dt.int32
U32 = mybir.dt.uint32
U16 = mybir.dt.uint16
U8 = mybir.dt.uint8
E4M3 = mybir.dt.float8_e4m3fn_x4
E5M2 = mybir.dt.float8_e5m2_x4
MULT = mybir.AluOpType.mult
SUBTRACT = mybir.AluOpType.subtract
COPY = mybir.ActivationFunctionType.Copy

P = 128
LANES = 4
PASSES = V // (P * LANES)
QUADS = 4
HALF = N // 2
CHUNKS = 4
SPLIT = 640


def tile_attend_gml_pl_sq_kernel(
    tc, xT, wd_words, wd_scales, wv_words, wv_scales, y, cw, rw, offs, out_0, out_1, out_2
):
    nc = tc.nc
    with ExitStack() as ctx:
        keep = ctx.enter_context(tc.tile_pool(name="keep", bufs=1))
        placed = ctx.enter_context(tc.tile_pool(name="placed", bufs=1))
        psum = ctx.enter_context(tc.psum_pool(name="psum", bufs=1))

        def tile(name, shape, dtype, tag=None):
            return keep.tile(shape, dtype, name=name, tag=tag or name, align_bytes=64)

        offsets = keep.tile([P, N // 16], U16, name="offsets")

        def listed(window, h):
            return window[:].indirect(offsets[:, h * HALF // 16 : (h + 1) * HALF // 16])

        wd_sc_raw = tile("wd_sc_raw", [P, V], U8)
        wv_sc_raw = tile("wv_sc_raw", [P, PASSES * D], U8)
        nc.gpsimd.memset(wd_sc_raw[:].bitcast(I32), 0)
        identity = tile("identity", [P, P], F32)
        make_identity(nc, identity[:])
        nc.gpsimd.memset(wv_sc_raw[:].bitcast(I32), 0)
        windows = [tile(f"window{r}", [P, T], F32) for r in range(LANES)]
        for r in range(LANES):
            (nc.vector if r < 2 else nc.gpsimd).memset(windows[r][:], 0.0)

        x_rows = xT.rearrange("(p r) t -> p r t", r=LANES)
        x_planes = [tile(f"x{r}", [P, T], F32) for r in range(LANES)]
        wd_all = wd_words[0].rearrange("p n t -> p (n t)").bitcast(I32)
        wd_raw = [tile(f"wd_raw{o}", [P, 512], I32) for o in range(PASSES)]
        cw_cols = tile("cw_cols", [P, PASSES, LANES], F32)
        rw_cols = tile("rw_cols", [P, LANES], F32)
        y_rows = y.rearrange("(o p r) i -> o p r i", o=PASSES, r=LANES)
        y_first = [[tile(f"y0{o}{u}", [P, 2, HALF], F32) for u in range(2)] for o in range(PASSES)]
        y_second = tile("y10", [P, LANES, HALF], F32)
        y_last = [placed.tile([P, 2, HALF], F32, name=f"y11{u}", offset=2048 * u, align_bytes=64) for u in range(2)]
        wv_raw = tile("wv_raw", [P, PASSES, D], I32)

        nc.sync.dma_start(x_planes[0][:], x_rows[:, 0, :])
        nc.sync.dma_start(offsets[:], offs)
        for r in (1, 2):
            nc.sync.dma_start(x_planes[r][:], x_rows[:, r, :])
        for q in range(QUADS):
            nc.sync.dma_start(
                wd_sc_raw[32 * q : 32 * q + 4, :].bitcast(I32), wd_scales[0, 4 * q : 4 * q + 4, :].bitcast(I32)
            )
        nc.sync.dma_start(x_planes[3][:], x_rows[:, 3, :])
        for o in range(PASSES):
            nc.sync.dma_start(wd_raw[o][:], wd_all[:, o * 512 : (o + 1) * 512])
            if o == 0:
                nc.sync.dma_start(cw_cols[:], cw.rearrange("(o p r) one -> p o (r one)", o=PASSES, r=LANES))
            for u in range(2):
                nc.sync.dma_start(y_first[o][u][:], y_rows[o, :, 2 * u : 2 * u + 2, :HALF])
                if (o, u) == (0, 0):
                    nc.sync.dma_start(rw_cols[:], rw[0].rearrange("(p c) -> p c", c=LANES))
        for q in range(QUADS):
            nc.sync.dma_start(
                wv_sc_raw[32 * q : 32 * q + 4, :].bitcast(I32).rearrange("f (o w) -> f o w", o=PASSES),
                wv_scales[:, 4 * q : 4 * q + 4, :].bitcast(I32).rearrange("o f w -> f o w"),
            )
        nc.sync.dma_start(wv_raw[:], wv_words.rearrange("o p n t -> p o (n t)").bitcast(I32))
        nc.sync.dma_start(y_second[:], y_rows[0, :, :, HALF:])
        for u in range(2):
            nc.sync.dma_start(y_last[u][:], y_rows[1, :, 2 * u : 2 * u + 2, HALF:])

        def y_plane(h, o, r):
            if (h, o) == (1, 0):
                return y_second[:, r, :]
            return (y_first[o] if h == 0 else y_last)[r // 2][:, r % 2, :]

        def dealt_views(dst, src):
            return (
                dst.rearrange("p (r c i) -> p c r i", r=LANES, i=4),
                src.rearrange("p (c i r) -> p c r i", r=LANES, i=4),
            )

        def deal_bytes(dst, src):
            nc.gpsimd.tensor_copy(
                dst.rearrange("p (o r s) -> p o r s", r=LANES, s=P), src.rearrange("p (o s r) -> p o r s", r=LANES, s=P)
            )

        banks = [psum.tile([P, N], F32, name=f"bank{b}") for b in range(7)]
        rw_bank = psum.tile([P, N], F32, name="rw_bank")
        for c in range(LANES):
            nc.tensor.transpose(rw_bank[:, c * P : (c + 1) * P], rw_cols[:, c : c + 1].to_broadcast([P, P]), identity[:])

        wd_sc = tile("wd_sc", [P, V], U8)
        deal_bytes(wd_sc[:], wd_sc_raw[:])

        x_lanes = [tile("x_lanes0", [P, HALF, LANES], BF16)]
        picked = tile("picked", [P, LANES, HALF], BF16)
        for r in range(LANES):
            nc.vector.tensor_copy(x_lanes[0][:, :, r], listed(x_planes[r], 0))
            nc.scalar.activation(picked[:, r, :], listed(x_planes[r], 1), COPY)
        x_codes = [tile("x_codes0", [P, HALF], U32)]
        x_sc = [tile(f"x_sc{h}", [P, HALF], U8) for h in range(2)]

        def quantise_x(h):
            nc.vector.quantize_mx(
                out=x_codes[h][:].bitcast(E4M3), scales=x_sc[h][:], in_=x_lanes[h][:].rearrange("p i r -> p (i r)")
            )

        wd_codes = [tile(f"wd_codes{o}", [P, 512], I32) for o in range(PASSES)]
        score_banks = {
            (0, 0): [banks[r][:, :HALF] for r in range(LANES)],
            (0, 1): [banks[4 + r // 2][:, (r % 2) * HALF : (r % 2 + 1) * HALF] for r in range(LANES)],
            (1, 0): [banks[(6, 0)[r // 2]][:, (r % 2) * HALF : (r % 2 + 1) * HALF] for r in range(LANES)],
            (1, 1): [banks[1 + r // 2][:, (r % 2) * HALF : (r % 2 + 1) * HALF] for r in range(LANES)],
        }

        def scores(h, o):
            for r in range(LANES):
                nc.tensor.matmul_mx(
                    out=score_banks[h, o][r],
                    lhsT=wd_codes[o][:, r * P : (r + 1) * P].bitcast(E4M3),
                    lhsT_scale=wd_sc[:, o * 512 + r * P : o * 512 + (r + 1) * P],
                    rhs=x_codes[h][:].bitcast(E4M3),
                    rhs_scale=x_sc[h][:],
                    start=True,
                    stop=True,
                )

        ycw, resid, g_lanes, g_codes, g_sc = {}, {}, {}, {}, {}

        def scale_y(h, o):
            ycw[h, o] = tile(f"ycw{h}{o}", [P, LANES, HALF], F32)
            for r in range(LANES):
                nc.scalar.activation(ycw[h, o][:, r, :], y_plane(h, o, r), COPY, scale=cw_cols[:, o, r : r + 1])
            resid[h, o] = tile(f"resid{h}{o}", [P, LANES, HALF], F32)

        def residual(h, o, lanes):
            for r in lanes:
                nc.vector.scalar_tensor_tensor(
                    resid[h, o][:, r, :], score_banks[h, o][r], cw_cols[:, o, r : r + 1], ycw[h, o][:, r, :], MULT, SUBTRACT
                )

        def weigh(h, o):
            g_lanes[h, o] = tile(f"g_lanes{h}{o}", [P, HALF, LANES], BF16)
            quads = HALF // 4
            factors = rw_bank[:].rearrange("p (c q) -> p q c", c=4)[:, h * quads : (h + 1) * quads, :]
            nc.vector.tensor_tensor(
                g_lanes[h, o][:].rearrange("p (q c) r -> p q r c", c=4),
                resid[h, o][:].rearrange("p r (q c) -> p q r c", c=4),
                factors.unsqueeze(2).to_broadcast([P, quads, LANES, 4]),
                MULT,
            )

        def quantise_g(h, o):
            g_codes[h, o] = tile(f"g_codes{h}{o}", [P, HALF], U32)
            g_sc[h, o] = tile(f"g_sc{h}{o}", [P, HALF], U8)
            nc.vector.quantize_mx(
                out=g_codes[h, o][:].bitcast(E5M2),
                scales=g_sc[h, o][:],
                in_=g_lanes[h, o][:].rearrange("p i r -> p (i r)"),
            )

        quantise_x(0)
        x_lanes.append(tile("x_lanes1", [P, HALF, LANES], BF16, tag="x_lanes0"))
        nc.vector.tensor_copy(
            x_lanes[1][:].rearrange("p (c i) r -> p c r i", i=4), picked[:].rearrange("p r (c i) -> p c r i", i=4)
        )
        nc.gpsimd.tensor_copy(*dealt_views(wd_codes[0][:], wd_raw[0][:]))
        scores(0, 0)
        scale_y(0, 0)
        residual(0, 0, range(LANES))
        nc.scalar.copy(*dealt_views(wd_codes[1][:].bitcast(U32), wd_raw[1][:].bitcast(U32)))
        x_codes.append(tile("x_codes1", [P, HALF], U32))
        quantise_x(1)
        scores(0, 1)
        scale_y(0, 1)
        weigh(0, 0)
        residual(0, 1, range(LANES))
        scores(1, 0)
        scores(1, 1)
        wv_sc = tile("wv_sc", [P, PASSES * D], U8)
        deal_bytes(wv_sc[:], wv_sc_raw[:])
        wv_codes = [tile(f"wv_codes{o}", [P, D], I32, tag=f"y01{1 - o}") for o in range(PASSES)]
        for o in range(PASSES):
            nc.scalar.copy(*dealt_views(wv_codes[o][:].bitcast(U32), wv_raw[:, o, :].bitcast(U32)))
        quantise_g(0, 0)
        weigh(0, 1)
        scale_y(1, 0)
        scale_y(1, 1)
        residual(1, 0, (0,))
        quantise_g(0, 1)

        dx_banks = {
            0: [banks[3][:, :HALF], banks[4][:, :HALF], banks[4][:, HALF:], banks[5][:, :HALF]],
            1: [banks[(6, 0)[r // 2]][:, (r % 2) * HALF : (r % 2 + 1) * HALF] for r in range(LANES)],
        }

        shares_bank = {0: ((0,), (1, 2), (3,)), 1: ((2, 3), (0, 1))}

        def back(h, o):
            for lanes in shares_bank[h]:
                for r in lanes:
                    nc.tensor.matmul_mx(
                        out=dx_banks[h][r],
                        lhsT=wv_codes[o][:, r * P : (r + 1) * P].bitcast(E4M3),
                        lhsT_scale=wv_sc[:, o * D + r * P : o * D + (r + 1) * P],
                        rhs=g_codes[h, o][:].bitcast(E5M2),
                        rhs_scale=g_sc[h, o][:],
                        start=o == 0 and r == lanes[0],
                        stop=o == PASSES - 1 and r == lanes[-1],
                    )

        back(0, 0)
        back(0, 1)
        residual(1, 0, (1, 2, 3))
        residual(1, 1, (0,))
        weigh(1, 0)
        residual(1, 1, (1, 2, 3))
        quantise_g(1, 0)
        back(1, 0)
        weigh(1, 1)

        dx00 = placed.tile([P, HALF], F32, name="dx00", offset=1536, align_bytes=64)
        nc.scalar.copy(dx00[:], dx_banks[0][0])
        dx012 = placed.tile([P, 2, HALF], F32, name="dx012", offset=2560, align_bytes=64)
        nc.scalar.copy(dx012[:].rearrange("p r i -> p (r i)"), banks[4][:])
        nc.scalar.activation(listed(windows[0], 0), dx00[:], COPY)
        for r in (1, 2):
            nc.scalar.activation(listed(windows[r], 0), dx012[:, r - 1, :], COPY)

        dx03 = tile("dx03", [P, HALF], F32, tag="resid11")
        nc.vector.tensor_copy(dx03[:], dx_banks[0][3])
        quantise_g(1, 1)
        back(1, 1)
        nc.vector.tensor_copy(listed(windows[3], 0), dx03[:])
        dx101 = tile("dx101", [P, 2, HALF], F32)
        nc.vector.tensor_copy(dx101[:].rearrange("p r i -> p (r i)"), banks[6][:])
        dx123 = tile("dx123", [P, 2, HALF], F32)
        nc.scalar.copy(dx123[:].rearrange("p r i -> p (r i)"), banks[0][:])

        out_rows = out_0.rearrange("(p r) t -> p r t", r=LANES)
        rounded = tile("rounded", [P, LANES, T], BF16)
        for r in (2, 0, 3, 1):
            if r < 2:
                nc.vector.tensor_copy(listed(windows[r], 1), dx101[:, r, :])
            else:
                nc.scalar.activation(listed(windows[r], 1), dx123[:, r - 2, :], COPY)
            nc.sync.dma_start(out_rows[:, r, :], windows[r][:])
        nc.gpsimd.tensor_copy(rounded[:, 2, :], windows[2][:])
        nc.gpsimd.tensor_copy(rounded[:, 0, :SPLIT], windows[0][:, :SPLIT])
        nc.vector.tensor_copy(rounded[:, 1, :], windows[1][:])
        nc.vector.tensor_copy(rounded[:, 3, :SPLIT], windows[3][:, :SPLIT])
        for r in (3, 0):
            nc.scalar.copy(rounded[:, r, SPLIT:], windows[r][:, SPLIT:])

        out_lanes = tile("out_lanes", [P, T, LANES], BF16)

        def weave(a, b):
            return (
                out_lanes[:, a:b, :].rearrange("p (c i) r -> p c r i", i=4),
                rounded[:, :, a:b].rearrange("p r (c i) -> p c r i", i=4),
            )

        out_sc = tile("out_sc", [P, T], U8)
        out_words = out_1[0].rearrange("p n t -> p (n t)").bitcast(I32)
        width = T // CHUNKS
        codes = tile("out_codes", [P, T], I32)

        def quantise_out(c):
            cols = slice(c * width, (c + 1) * width)
            nc.vector.quantize_mx(
                out=codes[:, cols].bitcast(E4M3),
                scales=out_sc[:, cols],
                in_=out_lanes[:, cols, :].rearrange("p t r -> p (t r)"),
            )
            if c > 0:
                stored = slice(0 if c == 1 else c * width, (c + 1) * width)
                nc.sync.dma_start(out_words[:, stored], codes[:, stored])

        nc.scalar.copy(*weave(SPLIT, 3 * width))
        nc.scalar.copy(*weave(3 * width, T))
        nc.vector.tensor_copy(*weave(0, width))
        nc.vector.tensor_copy(*weave(width, 2 * width))
        quantise_out(0)
        nc.vector.tensor_copy(*weave(2 * width, SPLIT))
        for c in range(1, CHUNKS):
            quantise_out(c)
        queues = (nc.scalar, nc.sync, nc.scalar, nc.sync)
        for q in range(QUADS):
            queues[q].dma_start(out_2[0, 4 * q : 4 * q + 4, :].bitcast(I32), out_sc[32 * q : 32 * q + 4, :].bitcast(I32))
